import numpy as np, ml_dtypes
CORES = [3,11,19,27,35,43,51,59]
N = 8
BF = ml_dtypes.bfloat16
M, D, LV, CAP = 1024, 3, 5, 192
P, H = N * M, 2 ** LV - 1
def ancestors(t):
    p, s = t >> 1, t & 1
    L = np.full((8, P + 1), P, np.int64); R = L.copy()
    for k in range(LV):
        a = np.where(s == 1, p, np.take_along_axis(L, p, 1)); b = np.where(s == 0, p, np.take_along_axis(R, p, 1))
        L[:, :P] = a; R[:, :P] = b
    return L[:, :P], R[:, :P]
def wants(t):
    L, R = ancestors(t); w = np.zeros((8, N, P + 1), bool); g = np.arange(8)[:, None]; r = (np.arange(P) // M)[None]
    w[g, r, L] = True; w[g, r, R] = True
    return w[:, :, :P].reshape(8, N, N, M)
def fit(rng, t):
    w = wants(t); L, R = ancestors(t)
    for g, r, q in np.argwhere(np.count_nonzero(w, axis=3) > CAP):
        if r != q:
            c = rng.permutation(np.flatnonzero(w[g, r, q]))[CAP:] + q * M; a = r * M
            x = t[g, a:a + M]; x[np.isin(L[g, a:a + M], c) | np.isin(R[g, a:a + M], c)] = 2 * P
def grid(rng):
    lev = np.array([c.bit_length() - 1 for c in range(1, H + 1)]); k = rng.random((H,) * D); s = np.zeros((H,) * D, np.int64)
    for d in range(D):
        e = lev.reshape([H if i == d else 1 for i in range(D)]); s = s + e; k = k + (0.75 + 0.5 * rng.random()) * e
    for d in range(D):
        u = np.moveaxis(k, d, 0)
        for c in range(2, H + 1): u[c - 1] = np.maximum(u[c - 1], u[c // 2 - 1])
    o = np.lexsort((s.reshape(-1), k.reshape(-1)))[:P]; o = o[rng.permutation(P)]
    num = np.full(H ** D, P); num[o] = np.arange(P); c = np.stack(np.unravel_index(o, (H,) * D)) + 1
    t = np.full((D, P), 2 * P)
    for d in range(D):
        b = c.copy(); b[d] = np.maximum(b[d] // 2, 1)
        t[d] = np.where(c[d] > 1, 2 * num[np.ravel_multi_index(tuple(b - 1), (H,) * D)] + c[d] % 2, 2 * P)
    return t
def vals(rng):
    return (rng.standard_normal((N, 128, M), dtype=np.float32) * np.exp2(rng.integers(-2, 3, (N, 128, 1)))).astype(np.float32)
def made(rng, v, t):
    for d in range(D): fit(rng, t[:, d])
    return {"v": v, "tree": np.repeat(t.reshape(1, 8, D * P).astype(np.int32), N, axis=0)}
def heaps(o):
    b = o[:len(o) // H * H].reshape(-1, H); c = np.arange(2, H + 1)
    return b[:, 1:], 2 * b[:, c // 2 - 1] + c % 2
def setup_inputs(rng):
    return made(rng, vals(rng), np.stack([grid(rng) for g in range(8)]))
def setup_inputs_full(rng):
    t = np.full((8, D, P), 2 * P); n3 = min(CAP, M - 2 * CAP); n4 = max(0, min(CAP, M - 3 * CAP))
    for g, d in np.ndindex(8, D):
        o = np.stack([q * M + rng.permutation(M) for q in range(N)]); a = np.roll(o, -(1 + (g + d) % (N - 1)), axis=0)
        s = rng.integers(0, 2, (3, N, CAP)); x = t[g, d]
        x[o[:, CAP:2 * CAP]] = 2 * a[:, :CAP] + s[0]
        x[o[:, 2 * CAP:2 * CAP + n3]] = 2 * o[:, CAP:CAP + n3] + s[1][:, :n3]
        x[o[:, 3 * CAP:3 * CAP + n4]] = 2 * o[:, 2 * CAP:2 * CAP + n4] + s[2][:, :n4]
    return made(rng, vals(rng), t)
def setup_inputs_chains(rng):
    t = np.full((8, D, P), 2 * P); k = P // LV
    for g, d in np.ndindex(8, D):
        o = np.concatenate([[0, P - 1], 1 + rng.permutation(P - 2)])[:k * LV].reshape(k, LV)
        s = rng.integers(0, 2, (k, LV)); s[0] = 1; s[0, 1] = 0; s[1] = 0; s[1, 1] = 1
        x = t[g, d]; x[o[:, 1:]] = 2 * o[:, :-1] + s[:, 1:]
    return made(rng, vals(rng), t)
def setup_inputs_near(rng):
    t = np.full((8, D, P), 2 * P)
    for g, d in np.ndindex(8, D):
        x = t[g, d]
        if (g + d) % 3 == 1:
            for q in range(N):
                i, e = heaps(q * M + rng.permutation(M)); x[i] = e
        if (g + d) % 3 == 2:
            i, e = heaps(rng.permutation(P)); x[i] = e
    return made(rng, vals(rng), t)
def setup_inputs_spread(rng):
    d = setup_inputs(rng); k = (N, 1, M)
    d["v"] = (d["v"] * np.exp2(rng.integers(-6, 7, k)) * (rng.random(k) > 0.0625)).astype(np.float32); return d
def check_inputs(d):
    bad = []; a = np.abs(d["v"].astype(np.float64)); tr = d["tree"].astype(np.int64)
    if not ((a == 0) | ((a >= 2.0 ** -60) & (a <= 2.0 ** 60))).all(): bad.append("sizes")
    if (tr != tr[:1]).any(): bad.append("alike")
    if tr.min() < 0 or tr.max() > 2 * P: return bad + ["codes"]
    other = ~np.eye(N, dtype=bool)
    for k in range(D):
        t = tr[0][:, k * P:(k + 1) * P]
        for g in range(8):
            c = t[g][t[g] < 2 * P]; up = np.append(t[g] >> 1, P); x = np.arange(P)
            if len(np.unique(c)) < len(c): bad.append("sides")
            for i in range(LV): x = up[x]
            if (x != P).any(): bad.append("levels")
        if (np.count_nonzero(wants(t), axis=3)[:, other] > CAP).any(): bad.append("wanted")
    return sorted(set(bad))
def reference(v, tree):
    u = np.zeros((8, 16, P + 1), np.float32)
    u[:, :, :P] = v.reshape(N, 8, 16, M).transpose(1, 2, 0, 3).reshape(8, 16, P)
    for d in range(D):
        L, R = ancestors(tree[0][:, d * P:(d + 1) * P].astype(np.int64))
        for g in range(8):
            s = u[g][:, L[g]] + u[g][:, R[g]]
            u[g, :, :P] = u[g, :, :P] - np.float32(0.5) * s
    y = u[:, :, :P].reshape(8, 16, N, M).transpose(2, 0, 1, 3).reshape(N, 128, M)
    return {"y": np.ascontiguousarray(y)}

@@ -1,0 +1,405 @@
+from concourse.bass import DstId, RemoteDMATransfer
+from concourse.mybir import AluOpType as A, ActivationFunctionType as F
+
+P, M, NG = 8192, 1024, 8
+WW = P + 8
+PE_SLOTS = (1, 2, 3)
+DMA_SLOTS = (4, 5, 6, 7)
+
+SCRATCH = {}
+for _dt, _bufs in (
+        ("float32", dict(w0=WW, w1=WW, w2=WW, gb=M, ss=M, hh=M, res=M, cf=32, iy=144, pr=256, zr=256, sl=64, pp=320,
+                         ff=256, ee=192, ne=128, tt=192, rep=M, fh=256)),
+        ("bfloat16", dict(tab=P + 16, xb=512, lt=2048, cand=3072, p1=128, zs=3 * 144, zc=6 * 144)),
+        ("int32", dict(xi=512, xt=512, pcol=4, ci=4, ri=128, zi=128)),
+        ("uint16", dict(off=768, offm=384, offs=64))):
+    for _n, _w in _bufs.items():
+        SCRATCH[_n] = ("sbuf", [128, _w], _dt)
+SCRATCH["stg"] = ("dram", [16, 128, 64], "float32")
+SCRATCH["piece"] = ("dram", [2, 128, 64], "float32")
+SCRATCH["fs"] = ("dram", [16, 128, 32], "float32")
+SCRATCH["land"] = ("dram", [32, 128, 32], "float32")
+for _b in range(8):
+    SCRATCH["ps%d" % _b] = ("psum", [128, 512], "float32")
+
+SEMAPHORES = (["sv", "sa", "sp", "sg", "ls", "tree_in", "st0", "st1", "w0in", "w0own", "rot0", "rot1", "fq", "fst0", "fst1",
+               "yo", "ya", "pa0", "pa1", "pb0", "pb1"] + ["fa%d" % i for i in range(4)])
+
+
+def _bits(es):
+    m = 0
+    for e in es:
+        m |= 1 << e
+    return m
+
+
+def _dst(topo, c):
+    rid, pid, _ = topo.addr(c)
+    return DstId(rid=rid, pnc=pid)
+
+
+def _others(r):
+    return [q for q in range(NG) if q != r]
+
+
+def _helper_of(T, topo, grp, q):
+    rc = T.cores[grp]
+    return [c for c in topo.cores_of(rc) if c != rc][_others(grp).index(q)]
+
+
+def _far_senders(T, topo, grp):
+    rc = T.cores[grp]
+    far = [c for c in topo.cores_of(rc) if topo.die(c) != topo.die(rc) and all(topo.may_write(c, r) for r in T.cores)]
+    return far[0], far[1]
+
+
+def _half_engines(topo, src, dst):
+    es = topo.engines(src, dst)
+    return es[:len(es) // 2]
+
+
+def _send_back(g, T, topo, src, grp, quarter, base):
+    tr = []
+    for n, q in enumerate(_others(grp)):
+        c = T.cores[q]
+        tr.append(RemoteDMATransfer(dst_ids=[_dst(topo, c)], dma_engine_mask=1 << topo.engines(src, c)[n],
+                                    remote_sem=T.sem["fa%d" % quarter], src=T.fs[base + q], dst=T.land[quarter * NG + grp]))
+    g.remote_dma_fused(tr, local_sem=T.sem.ls)
+    return len(tr)
+
+
+def helper_program(g, core, T, topo):
+    grp = [r for r in range(NG) if topo.chip(T.cores[r]) == topo.chip(core)]
+    if not grp:
+        return
+    grp = grp[0]
+    rc = T.cores[grp]
+    rid, pid, _ = topo.addr(rc)
+    q = [r for r in _others(grp) if _helper_of(T, topo, grp, r) == core][0]
+    sent = 0
+    for h in range(2):
+        for qu in (g.sync, g.scalar):
+            qu.wait_ge(T.sem["pa%d" % h], 1)
+        for j in range(NG):
+            qu = g.sync if j % 2 == 0 else g.scalar
+            qu.dma_start(T.rep[16 * j:16 * j + 16, h * 512:h * 512 + 512], T.piece[h]).then_inc(T.sem["pb%d" % h], 16)
+    for h in range(2):
+        g.wait_ge(T.sem["pb%d" % h], 16 * NG)
+        g.remote_dma(T.w0[:, q * M + h * 512:q * M + h * 512 + 512], T.rep[:, h * 512:h * 512 + 512],
+                     T.sem.w0in, T.sem.ls, pid, rid, topo.mask(core, rc))
+        sent += len(topo.engines(core, rc))
+    far = _far_senders(T, topo, grp)
+    if core in far:
+        g.sync.wait_ge(T.sem.fq, len(_half_engines(topo, rc, core)))
+        g.sync.dma_start(T.fs[0:NG], T.fh[:, :]).then_inc(T.sem.fst0, 16)
+        g.wait_ge(T.sem.fst0, 16)
+        sent += _send_back(g, T, topo, core, grp, far.index(core), 0)
+    g.wait_ge(T.sem.ls, sent)
+
+
+def rank_program(g, core, T, topo):
+    rank = T.rank_of(core)
+    if rank is None:
+        return helper_program(g, core, T, topo)
+    Q = {"v": g.vector, "a": g.scalar, "p": g.tensor, "g": g, "s": g.sync}
+    SEM = {"v": "sv", "a": "sa", "p": "sp", "g": "sg"}
+    cnt = {"v": 0, "a": 0, "p": 0, "g": 0}
+    seen = {k: {} for k in Q}
+    V, S, PE = g.vector, g.scalar, g.tensor
+    ps = [T["ps%d" % b] for b in range(8)]
+    W = [T.w0, T.w1, T.w2]
+    cf = T.cf
+
+    def need(q, *toks):
+        for sem, n in toks:
+            if seen[q].get(sem, 0) < n:
+                Q[q].wait_ge(T.sem[sem], n)
+                seen[q][sem] = n
+
+    def done(q, inst):
+        inst.then_inc(T.sem[SEM[q]], 1)
+        cnt[q] += 1
+        return (SEM[q], cnt[q])
+
+    def last(q):
+        return (SEM[q], cnt[q])
+
+    def ts(out, in0, s1, s2, op0, op1=None):
+        if op1 is None:
+            return done("v", V.tensor_scalar(out, in0, s1, None, op0))
+        return done("v", V.tensor_scalar(out, in0, s1, s2, op0, op1))
+
+    def tt(out, in0, in1, op):
+        return done("v", V.tensor_tensor(out, in0, in1, op))
+
+    def cp(q, out, in_, scale=1.0):
+        if q == "v":
+            return done("v", V.tensor_copy(out, in_))
+        return done("a", S.activation(out, in_, F.Copy, scale=scale))
+
+    def chain():
+        need("v", last("v"))
+
+    def iota(out, pat, cm):
+        return done("g", g.iota(out, pat, 0, cm, allow_small_or_imprecise_dtypes=True))
+
+    S.dma_start(T.xi[0:48, :], T.tree[rank]).then_inc(T.sem.tree_in, 16)
+    S.dma_start(T.xi[64:112, :], T.tree[rank]).then_inc(T.sem.tree_in, 16)
+    S.dma_start(T.xi[48:64, :], T.tree[rank, 0:P]).then_inc(T.sem.tree_in, 16)
+    for h in range(2):
+        g.sync.dma_start(T.stg[h * NG:(h + 1) * NG], T.v[:, h * 512:h * 512 + 512]).then_inc(T.sem["st%d" % h], 16)
+    for j in range(NG):
+        g.sync.dma_start(T.w0[16 * j:16 * j + 16, rank * M:(rank + 1) * M],
+                         T.v[16 * rank:16 * rank + 16, :]).then_inc(T.sem.w0own, 16)
+
+    i_pc = done("g", g.iota(T.pcol[:, 0:1], [[0, 1]], 0, 1))
+    i_p1 = iota(T.p1[:, :], [[0, 8], [16, 16]], -1)
+    i_iy = iota(T.iy[:, :], [[1, 144]], 0)
+    sent = 0
+    for h in range(2):
+        tr = []
+        for n, grp in enumerate(_others(rank)):
+            hc = _helper_of(T, topo, grp, rank)
+            tr.append(RemoteDMATransfer(dst_ids=[_dst(topo, hc)], dma_engine_mask=1 << topo.engines(core, hc)[n],
+                                        remote_sem=T.sem["pa%d" % h], src=T.stg[h * NG + grp], dst=T.piece[h]))
+        sent += len(tr)
+        need("g", ("st%d" % h, 16))
+        g.remote_dma_fused(tr, local_sem=T.sem.ls)
+    i_pr = iota(T.pr[:, :], [[0, 2], [1, 128]], -1)
+    i_sl = iota(T.sl[:, :], [[16, 64]], 1)
+
+    need("v", i_pc)
+    ts(T.ci[:, 0:1], T.pcol[:, 0:1], 15, None, A.bitwise_and)
+    ts(T.ci[:, 1:2], T.pcol[:, 0:1], 4, None, A.arith_shift_right)
+    ts(T.ci[:, 2:3], T.pcol[:, 0:1], 1, None, A.bitwise_and)
+    t_ci = ts(T.ci[:, 3:4], T.pcol[:, 0:1], 14, None, A.bitwise_and)
+    need("v", i_p1)
+    t_lt = {}
+
+    def spreading(a, b):
+        for k in range(a, b):
+            t_lt[k] = ts(T.lt[:, k * 128:k * 128 + 128], T.p1[:, :], float(-k), None, A.is_equal)
+
+    spreading(0, 4)
+    need("v", t_ci)
+    t_cf = cp("v", cf[:, 0:4], T.ci[:, 0:4])
+    spreading(4, 8)
+    need("v", t_cf, i_iy)
+    ts(cf[:, 4:5], cf[:, 3:4], 8.0, 16.0, A.mult, A.add)
+    ts(cf[:, 5:6], cf[:, 2:3], -1.0, 1.0, A.mult, A.add)
+    ts(cf[:, 6:7], cf[:, 1:2], 16.0, 16.0, A.mult, A.add)
+    ts(cf[:, 8:11], T.iy[:, 0:3], cf[:, 1:2], 64.0, A.is_equal, A.mult)
+    ts(cf[:, 11:14], T.iy[:, 4:7], cf[:, 1:2], 0.5, A.is_equal, A.mult)
+    ts(cf[:, 14:17], T.iy[:, 0:3], cf[:, 0:1], 64.0, A.is_equal, A.mult)
+    ts(cf[:, 17:20], T.iy[:, 4:7], cf[:, 0:1], 0.5, A.is_equal, A.mult)
+    chain()
+    tt(cf[:, 20:23], cf[:, 8:11], cf[:, 11:14], A.add)
+    tt(cf[:, 23:26], cf[:, 14:17], cf[:, 17:20], A.add)
+    ts(T.tab[:, P:P + 1], cf[:, 0:1], 3.0, 128.0, A.is_lt, A.mult)
+    need("v", ("tree_in", 48))
+    ts(T.xt[0:64, :], T.xi[0:64, :], 7, None, A.arith_shift_right)
+    ts(T.xt[64:112, :], T.xi[64:112, :], 127, None, A.bitwise_and)
+    chain()
+    t_xb = cp("v", T.xb[0:112, :], T.xt[0:112, :])
+    ts(cf[:, 26:29], cf[:, 20:23], cf[:, 5:6], None, A.mult)
+    t_w = ts(cf[:, 29:32], cf[:, 20:23], cf[:, 2:3], None, A.mult)
+    spreading(8, 16)
+    for d in range(3):
+        ts(T.zs[:, d * 144:d * 144 + 144], T.iy[:, :], cf[:, 6:7], cf[:, 23 + d:24 + d], A.is_equal, A.mult)
+    need("v", t_w)
+    t_zc = {}
+    for d in range(3):
+        for h in range(2):
+            n = 2 * d + h
+            t_zc[d] = ts(T.zc[:, n * 144:n * 144 + 144], T.iy[:, :], cf[:, 4:5], cf[:, 26 + 3 * h + d:27 + 3 * h + d],
+                         A.is_equal, A.mult)
+
+    t_ev, t_sel, t_off = {}, {}, {}
+    on_v = (5, 7, 9, 11, 13, 15)
+
+    def spread(k):
+        b = ps[3 + k % 5]
+        need("p", t_xb, t_lt[k])
+        if k >= 5:
+            need("p", t_ev[k - 5])
+        t = done("p", PE.matmul(b[:, :], T.lt[0:112, k * 128:k * 128 + 128], T.xb[0:112, :], True, True))
+        q = "v" if k in on_v else "a"
+        need(q, t)
+        t_ev[k] = cp(q, T.tab[:, k * 512:k * 512 + 512], b[:, :])
+
+    def own_codes(d):
+        need("p", t_zc[d])
+        for h in range(2):
+            z = (2 * d + h) * 144
+            for i in range(16):
+                mm = PE.matmul(ps[d][:, 32 * h:32 * h + 32], T.zc[0:112, z + 16 - i:z + 144 - i], T.xb[0:112, i::16],
+                               i == 0, i == 15)
+            t_sel[d, 1] = done("p", mm)
+
+    for k in range(16):
+        spread(k)
+        if k in (6, 10, 14):
+            own_codes((k - 6) // 4)
+    t_tab = (t_ev[14], t_ev[15])
+
+    def offc(d, k):
+        return (4 * d + k - 1) * 64
+
+    def offsets(d, k):
+        need("v", t_sel[d, k])
+        c = offc(d, k)
+        t_off[d, k] = ts(T.off[:, c:c + 64], ps[d][:, 64 * (k - 1):64 * k], -0.25, None, A.add)
+
+    def climb(q, d, k, a, b):
+        need(q, t_off[d, k - 1], *t_tab)
+        c = offc(d, k - 1)
+        return cp(q, T.cand[:, d * M + 16 * a:d * M + 16 * b], T.tab[:, 0:P + 1].indirect(T.off[:, c + a:c + b]))
+
+    def pick(d, k, *toks):
+        need("p", *toks)
+        for i in range(16):
+            mm = PE.matmul(ps[d][:, 64 * (k - 1):64 * k], T.zs[:, d * 144 + 16 - i:d * 144 + 144 - i],
+                           T.cand[:, d * M + i:(d + 1) * M:16], i == 0, i == 15)
+        t_sel[d, k] = done("p", mm)
+
+    for k in (2, 3, 4):
+        offsets(0, k - 1)
+        ta = climb("v", 0, k, 0, 32)
+        tb = climb("a", 0, k, 32, 64)
+        pick(0, k, ta, tb)
+        offsets(1, k - 1)
+        offsets(2, k - 1)
+        pick(1, k, climb("a", 1, k, 0, 64))
+        pick(2, k, climb("a" if k == 4 else "v", 2, k, 0, 64))
+
+    need("v", i_pr, i_sl)
+    ts(T.zr[:, :], T.pr[:, :], 0.0, None, A.is_equal)
+    ts(cf[:, 7:8], cf[:, 1:2], float(M - 16), None, A.mult)
+    ts(cf[:, 4:5], cf[:, 1:2], float(-M), float(2 * P), A.mult, A.add)
+    for w in W:
+        done("v", V.memset(w[:, P:WW], 0.0))
+    chain()
+    ts(T.offs[:, :], T.sl[:, :], cf[:, 7:8], None, A.add)
+
+    def lists(d):
+        offsets(d, 4)
+        pp, ff, ee, ne, tq = T.pp, T.ff, T.ee, T.ne, T.tt
+        c = offc(d, 1)
+        chain()
+        ts(pp[:, 64:320], T.off[:, c:c + 256], float(-P), None, A.add)
+        chain()
+        tt(ff[:, :], ps[d][:, 0:256], pp[:, 64:320], A.subtract)
+        chain()
+        for k in range(3):
+            tt(ee[:, 64 * k:64 * k + 64], ff[:, 64 * k + 64:64 * k + 128], ff[:, 0:64], A.not_equal)
+        chain()
+        tt(tq[:, :], pp[:, 128:320], ee[:, :], A.mult)
+        ts(ne[:, :], ee[:, 0:128], -1.0, 1.0, A.mult, A.add)
+        for x, op in ((ne[:, 64:128], A.mult), (tq[:, 64:128], A.add), (ne[:, 0:64], A.mult), (tq[:, 0:64], A.add)):
+            chain()
+            tt(pp[:, 0:64], tq[:, 128:192] if x is None or op == A.mult and not lists_started[d] else pp[:, 0:64], x, op)
+            lists_started[d] = True
+        chain()
+        o = T.offm[:, 128 * d:128 * d + 128]
+        if d == 0:
+            return ts(o, pp[:, 0:128], float(P), None, A.add)
+        ts(T.ri[:, :], pp[:, 0:128], cf[:, 4:5], None, A.add)
+        ts(T.zi[:, :], pp[:, 0:128], 0.0, float(P), A.is_ge, A.mult)
+        chain()
+        ts(T.ri[:, :], T.ri[:, :], P - 1, None, A.bitwise_and)
+        chain()
+        tt(T.ri[:, :], T.ri[:, :], T.zi[:, :], A.max)
+        chain()
+        return cp("v", o, T.ri[:, :])
+
+    lists_started = [False, False, False]
+    ready = [lists(0), ("w0in", 2 * sum(len(topo.engines(_helper_of(T, topo, rank, q), core)) for q in _others(rank))),
+             ("w0own", 16 * NG)]
+    far = _far_senders(T, topo, rank)
+
+    for d in range(3):
+        w = W[d]
+        out = W[d + 1] if d < 2 else T.res
+        win = w[:, 0:P + 1]
+        need("v", *ready)
+        need("a", *ready)
+        tg, tsum, th, tn, t_rot = {}, {}, {}, {}, {}
+        banks = ((5, 6, 7), (0, 3, 4))
+
+        def ck(buf, c):
+            return buf[:, 256 * c:256 * c + 256]
+
+        def ga(c):
+            tg[c] = cp("a", ck(T.gb, c), win.indirect(T.offm[:, 128 * d + 16 * c:128 * d + 16 * c + 16]))
+
+        def su(c):
+            need("v", tg[c])
+            o = 128 * d + 64 + 16 * c
+            tsum[c] = tt(ck(T.ss, c), win.indirect(T.offm[:, o:o + 16]), ck(T.gb, c), A.add)
+
+        def hv(c):
+            return ck(T.hh, c) if d == 0 else ps[3 + c % 2][:, 0:256]
+
+        def ha(c):
+            need("a", tsum[c])
+            if c >= 2:
+                need("a", tn[c - 2])
+            th[c] = cp("a", hv(c), ck(T.ss, c), -0.5)
+
+        def turn(h):
+            cols = slice(512 * h, 512 * h + 512)
+            need("s", tn[2 * h + 1])
+            for t in DMA_SLOTS:
+                oc = slice(t * M + 512 * h, t * M + 512 * h + 512)
+                g.sync.dma_start(out[0:128 - 16 * t, oc], out[16 * t:128, cols]).then_inc(T.sem["rot%d" % d], 16)
+                g.sync.dma_start(out[128 - 16 * t:128, oc], out[0:16 * t, cols]).then_inc(T.sem["rot%d" % d], 16)
+            need("p", tn[2 * h + 1])
+            for n, t in enumerate(PE_SLOTS):
+                t_rot[h, n] = done("p", PE.matmul(ps[banks[h][n]][:, :], T.zr[:, 16 * t:16 * t + 128], out[:, cols], True, True))
+
+        def evac(q, h, n):
+            need(q, t_rot[h, n])
+            t = PE_SLOTS[n]
+            return cp(q, out[:, t * M + 512 * h:t * M + 512 * h + 512], ps[banks[h][n]][:, :])
+
+        def nw(c):
+            need("v", th[c])
+            own = win.indirect(T.offs[:, 16 * c:16 * c + 16]) if d == 0 else ck(w, c)
+            tn[c] = tt(ck(out, c), own, hv(c), A.add)
+            if d < 2 and c % 2 == 1:
+                turn(c // 2)
+            if d == 2 and c < 2:
+                need("g", tn[c])
+                rid, pid, _ = topo.addr(far[c])
+                g.remote_dma(T.fh[:, :], ck(T.res, c), T.sem.fq, T.sem.ls, pid, rid, _bits(_half_engines(topo, core, far[c])))
+            if d == 2 and c >= 2:
+                need("s", tn[c])
+                b = (c - 2) * NG
+                g.sync.dma_start(T.fs[b:b + NG], ck(T.res, c)).then_inc(T.sem["fst%d" % (c - 2)], 16)
+
+        ga(0); su(0); ga(1); ha(0); su(1); ga(2); nw(0); ha(1); su(2); ga(3); nw(1); ha(2); su(3); nw(2); ha(3); nw(3)
+        if d < 2:
+            evac("a", 0, 0)
+            evac("v", 0, 1)
+            evac("a", 0, 2)
+            lists(d + 1)
+            evac("a", 1, 0)
+            evac("a", 1, 1)
+            evac("v", 1, 2)
+            ready = [last("v"), last("a"), ("rot%d" % d, 16 * 4 * len(DMA_SLOTS))]
+
+    sent += sum(len(_half_engines(topo, core, f)) for f in far)
+    for c in (2, 3):
+        need("g", ("fst%d" % (c - 2), 16))
+        sent += _send_back(g, T, topo, core, rank, c, (c - 2) * NG)
+    g.sync.dma_start(T.y[16 * rank:16 * rank + 16, :], T.res[16 * rank:16 * rank + 16, :]).then_inc(T.sem.yo, 16)
+    n_y = {"yo": 16, "ya": 0}
+    for c in range(4):
+        q, sem = ("a", "ya") if c < 2 else ("s", "yo")
+        need(q, ("fa%d" % c, NG - 1))
+        cols = slice(256 * c, 256 * c + 256)
+        for a, b in ((0, rank), (rank + 1, NG)):
+            if b > a:
+                Q[q].dma_start(T.y[16 * a:16 * b, cols], T.land[c * NG + a:c * NG + b]).then_inc(T.sem[sem], 16)
+                n_y[sem] += 16
+    need("g", ("ls", sent), last("v"), last("a"), last("p"), last("g"), ("yo", n_y["yo"]), ("ya", n_y["ya"]))

@@ -3,13 +3,15 @@ from concourse.mybir import AluOpType as A, ActivationFunctionType as F
 
 P, M, NG = 8192, 1024, 8
 WW = P + 8
-PE_SLOTS = (1, 2, 3)
-DMA_SLOTS = (4, 5, 6, 7)
+NPE = 3
+LATE = True
+PE_SLOTS = tuple(range(1, NPE + 1))
+DMA_SLOTS = tuple(range(NPE + 1, NG))
 
 SCRATCH = {}
 for _dt, _bufs in (
-        ("float32", dict(w0=WW, w1=WW, w2=WW, gb=M, ss=M, hh=M, res=M, cf=32, iy=144, pr=256, zr=256, sl=64, pp=320,
-                         ff=256, ee=192, ne=128, tt=192, rep=M, fh=256)),
+        ("float32", dict(w0=WW, w1=WW, w2=WW, gb=M, ss=M, hh=M, res=M, cf=32, iy=144, pr=256, zr=256, sl=64, pp=256,
+                         ff=256, ee=192, ne=192, tt=192, so=192, rep=M, fh=256)),
         ("bfloat16", dict(tab=P + 16, xb=512, lt=2048, cand=3072, p1=128, zs=3 * 144, zc=6 * 144)),
         ("int32", dict(xi=512, xt=512, pcol=4, ci=4, ri=128, zi=128)),
         ("uint16", dict(off=768, offm=384, offs=64))):
@@ -238,8 +240,10 @@ def rank_program(g, core, T, topo):
 
     for k in range(16):
         spread(k)
-        if k in (6, 10, 14):
-            own_codes((k - 6) // 4)
+        if k == 6:
+            own_codes(0)
+    own_codes(1)
+    own_codes(2)
     t_tab = (t_ev[14], t_ev[15])
 
     def offc(d, k):
@@ -250,7 +254,7 @@ def rank_program(g, core, T, topo):
         c = offc(d, k)
         t_off[d, k] = ts(T.off[:, c:c + 64], ps[d][:, 64 * (k - 1):64 * k], -0.25, None, A.add)
 
-    def climb(q, d, k, a, b):
+    def climb(q, d, k, a=0, b=64):
         need(q, t_off[d, k - 1], *t_tab)
         c = offc(d, k - 1)
         return cp(q, T.cand[:, d * M + 16 * a:d * M + 16 * b], T.tab[:, 0:P + 1].indirect(T.off[:, c + a:c + b]))
@@ -262,15 +266,24 @@ def rank_program(g, core, T, topo):
                            T.cand[:, d * M + i:(d + 1) * M:16], i == 0, i == 15)
         t_sel[d, k] = done("p", mm)
 
+    def step(d, k):
+        offsets(d, k - 1)
+        pick(d, k, climb("v", d, k, 0, 32), climb("a", d, k, 32, 64))
+
     for k in (2, 3, 4):
-        offsets(0, k - 1)
-        ta = climb("v", 0, k, 0, 32)
-        tb = climb("a", 0, k, 32, 64)
-        pick(0, k, ta, tb)
-        offsets(1, k - 1)
-        offsets(2, k - 1)
-        pick(1, k, climb("a", 1, k, 0, 64))
-        pick(2, k, climb("a" if k == 4 else "v", 2, k, 0, 64))
+        step(0, k)
+        if not LATE:
+            offsets(1, k - 1)
+            offsets(2, k - 1)
+            pick(1, k, climb("a", 1, k))
+            pick(2, k, climb("a" if k == 4 else "v", 2, k))
+        elif k < 4:
+            step(1, k)
+        else:
+            offsets(1, 3)
+            offsets(2, 1)
+            pick(1, 4, climb("a", 1, 4))
+            pick(2, 2, climb("a", 2, 2))
 
     need("v", i_pr, i_sl)
     ts(T.zr[:, :], T.pr[:, :], 0.0, None, A.is_equal)
@@ -278,33 +291,38 @@ def rank_program(g, core, T, topo):
     ts(cf[:, 4:5], cf[:, 1:2], float(-M), float(2 * P), A.mult, A.add)
     for w in W:
         done("v", V.memset(w[:, P:WW], 0.0))
+    done("v", V.memset(T.ne[:, 0::3], 0.0))
     chain()
     ts(T.offs[:, :], T.sl[:, :], cf[:, 7:8], None, A.add)
 
     def lists(d):
         offsets(d, 4)
-        pp, ff, ee, ne, tq = T.pp, T.ff, T.ee, T.ne, T.tt
+        pp, ff, ee, ne, tq, so = T.pp, T.ff, T.ee, T.ne, T.tt, T.so
         c = offc(d, 1)
         chain()
-        ts(pp[:, 64:320], T.off[:, c:c + 256], float(-P), None, A.add)
+        ts(pp[:, :], T.off[:, c:c + 256], float(-P), None, A.add)
         chain()
-        tt(ff[:, :], ps[d][:, 0:256], pp[:, 64:320], A.subtract)
+        tt(ff[:, :], ps[d][:, 0:256], pp[:, :], A.subtract)
         chain()
         for k in range(3):
             tt(ee[:, 64 * k:64 * k + 64], ff[:, 64 * k + 64:64 * k + 128], ff[:, 0:64], A.not_equal)
         chain()
-        tt(tq[:, :], pp[:, 128:320], ee[:, :], A.mult)
-        ts(ne[:, :], ee[:, 0:128], -1.0, 1.0, A.mult, A.add)
-        for x, op in ((ne[:, 64:128], A.mult), (tq[:, 64:128], A.add), (ne[:, 0:64], A.mult), (tq[:, 0:64], A.add)):
-            chain()
-            tt(pp[:, 0:64], tq[:, 128:192] if x is None or op == A.mult and not lists_started[d] else pp[:, 0:64], x, op)
-            lists_started[d] = True
+        for k in range(3):
+            tt(tq[:, 2 - k::3], pp[:, 64 * k + 64:64 * k + 128], ee[:, 64 * k:64 * k + 64], A.mult)
+        for k in range(2):
+            ts(ne[:, 2 - k::3], ee[:, 64 * k:64 * k + 64], -1.0, 1.0, A.mult, A.add)
         chain()
+        done("v", V.tensor_tensor_scan(so[:, :], ne[:, :], tq[:, :], 0.0, A.mult, A.add))
         o = T.offm[:, 128 * d:128 * d + 128]
         if d == 0:
-            return ts(o, pp[:, 0:128], float(P), None, A.add)
-        ts(T.ri[:, :], pp[:, 0:128], cf[:, 4:5], None, A.add)
-        ts(T.zi[:, :], pp[:, 0:128], 0.0, float(P), A.is_ge, A.mult)
+            ts(T.offm[:, 64:128], pp[:, 0:64], float(P), None, A.add)
+            chain()
+            return ts(T.offm[:, 0:64], so[:, 2::3], float(P), None, A.add)
+        ts(T.ri[:, 64:128], pp[:, 0:64], cf[:, 4:5], None, A.add)
+        ts(T.zi[:, 64:128], pp[:, 0:64], 0.0, float(P), A.is_ge, A.mult)
+        chain()
+        ts(T.ri[:, 0:64], so[:, 2::3], cf[:, 4:5], None, A.add)
+        ts(T.zi[:, 0:64], so[:, 2::3], 0.0, float(P), A.is_ge, A.mult)
         chain()
         ts(T.ri[:, :], T.ri[:, :], P - 1, None, A.bitwise_and)
         chain()
@@ -312,7 +330,6 @@ def rank_program(g, core, T, topo):
         chain()
         return cp("v", o, T.ri[:, :])
 
-    lists_started = [False, False, False]
     ready = [lists(0), ("w0in", 2 * sum(len(topo.engines(_helper_of(T, topo, rank, q), core)) for q in _others(rank))),
              ("w0own", 16 * NG)]
     far = _far_senders(T, topo, rank)
@@ -323,8 +340,10 @@ def rank_program(g, core, T, topo):
         win = w[:, 0:P + 1]
         need("v", *ready)
         need("a", *ready)
-        tg, tsum, th, tn, t_rot = {}, {}, {}, {}, {}
-        banks = ((5, 6, 7), (0, 3, 4))
+        tg, tsum, th, tn, t_rot, t_e = {}, {}, {}, {}, {}, {}
+        free0 = [5, 6, 7, 0][:NPE]
+        free1 = [3, 4] + [b for b in (5, 6, 7, 0) if b not in free0]
+        banks = (free0, (free1 + free0)[:NPE])
 
         def ck(buf, c):
             return buf[:, 256 * c:256 * c + 256]
@@ -353,14 +372,19 @@ def rank_program(g, core, T, topo):
                 oc = slice(t * M + 512 * h, t * M + 512 * h + 512)
                 g.sync.dma_start(out[0:128 - 16 * t, oc], out[16 * t:128, cols]).then_inc(T.sem["rot%d" % d], 16)
                 g.sync.dma_start(out[128 - 16 * t:128, oc], out[0:16 * t, cols]).then_inc(T.sem["rot%d" % d], 16)
+
+        def pe_turn(h, n):
             need("p", tn[2 * h + 1])
-            for n, t in enumerate(PE_SLOTS):
-                t_rot[h, n] = done("p", PE.matmul(ps[banks[h][n]][:, :], T.zr[:, 16 * t:16 * t + 128], out[:, cols], True, True))
+            if h == 1 and n >= len(free1):
+                need("p", t_e[0, n - len(free1)])
+            t = PE_SLOTS[n]
+            t_rot[h, n] = done("p", PE.matmul(ps[banks[h][n]][:, :], T.zr[:, 16 * t:16 * t + 128],
+                                              out[:, 512 * h:512 * h + 512], True, True))
 
         def evac(q, h, n):
             need(q, t_rot[h, n])
             t = PE_SLOTS[n]
-            return cp(q, out[:, t * M + 512 * h:t * M + 512 * h + 512], ps[banks[h][n]][:, :])
+            t_e[h, n] = cp(q, out[:, t * M + 512 * h:t * M + 512 * h + 512], ps[banks[h][n]][:, :])
 
         def nw(c):
             need("v", th[c])
@@ -368,6 +392,11 @@ def rank_program(g, core, T, topo):
             tn[c] = tt(ck(out, c), own, hv(c), A.add)
             if d < 2 and c % 2 == 1:
                 turn(c // 2)
+            if d < 2 and c == 1:
+                for n in range(NPE):
+                    pe_turn(0, n)
+            if LATE and d == 1 and c == 0:
+                offsets(2, 3)
             if d == 2 and c < 2:
                 need("g", tn[c])
                 rid, pid, _ = topo.addr(far[c])
@@ -379,13 +408,25 @@ def rank_program(g, core, T, topo):
 
         ga(0); su(0); ga(1); ha(0); su(1); ga(2); nw(0); ha(1); su(2); ga(3); nw(1); ha(2); su(3); nw(2); ha(3); nw(3)
         if d < 2:
-            evac("a", 0, 0)
-            evac("v", 0, 1)
-            evac("a", 0, 2)
+            up = None
+            if LATE and d == 0:
+                offsets(2, 2)
+            if LATE and d == 1:
+                up = climb("a", 2, 4)
+            first = "v" if up else "a"
+            for n in range(NPE):
+                evac(first if n % 2 == 0 else "va".replace(first, ""), 0, n)
+            if LATE and d == 0:
+                up = climb("a", 2, 3)
+            for n in range(NPE):
+                pe_turn(1, n)
+                if LATE and d == 1 and n == 0:
+                    pick(2, 4, up)
+            if LATE and d == 0:
+                pick(2, 3, up)
             lists(d + 1)
-            evac("a", 1, 0)
-            evac("a", 1, 1)
-            evac("v", 1, 2)
+            for n in range(NPE):
+                evac("a", 1, n)
             ready = [last("v"), last("a"), ("rot%d" % d, 16 * 4 * len(DMA_SLOTS))]
 
     sent += sum(len(_half_engines(topo, core, f)) for f in far)

@@ -4,28 +4,31 @@ from concourse.mybir import AluOpType as A, ActivationFunctionType as F
 P, M, NG = 8192, 1024, 8
 WW = P + 8
 NPE = 3
-LATE = True
+NIN = 2
 PE_SLOTS = tuple(range(1, NPE + 1))
 DMA_SLOTS = tuple(range(NPE + 1, NG))
+TURN_PIECES = ((0, 1), (1, 4))
+CIN = M // NIN
 
 SCRATCH = {}
 for _dt, _bufs in (
-        ("float32", dict(w0=WW, w1=WW, w2=WW, gb=M, ss=M, hh=M, res=M, cf=32, iy=144, pr=256, zr=256, sl=64, pp=256,
-                         ff=256, ee=192, ne=192, tt=192, so=192, rep=M, fh=256)),
-        ("bfloat16", dict(tab=P + 16, xb=512, lt=2048, cand=3072, p1=128, zs=3 * 144, zc=6 * 144)),
-        ("int32", dict(xi=512, xt=512, pcol=4, ci=4, ri=128, zi=128)),
-        ("uint16", dict(off=768, offm=384, offs=64))):
+        ("float32", dict(w0=WW, w1=WW, w2=WW, gb=M, ss=M, hh=M, res=M, cf=16, iy=160, ib=72, ck=32, pr=256, zr=256,
+                         sl=64, z0=144, z1=144, ff=576, ee=576, tg=192, d0=768, d1=768, so=256, rep=M, fh=256)),
+        ("bfloat16", dict(tab=P + 16, xb=512, l16=128, l0=128, lt=2048, cand=9 * M, sb=72, zs=3 * 144, zc=6 * 144)),
+        ("int32", dict(xi=512, xt=512, pcol=4, ci=8, pi=576, z4=64, ri=128, zi=128)),
+        ("uint16", dict(off=576, offm=384, offs=64))):
     for _n, _w in _bufs.items():
         SCRATCH[_n] = ("sbuf", [128, _w], _dt)
-SCRATCH["stg"] = ("dram", [16, 128, 64], "float32")
-SCRATCH["piece"] = ("dram", [2, 128, 64], "float32")
+SCRATCH["stg"] = ("dram", [NIN * NG, 128, CIN // 8], "float32")
+SCRATCH["piece"] = ("dram", [NIN, 128, CIN // 8], "float32")
 SCRATCH["fs"] = ("dram", [16, 128, 32], "float32")
 SCRATCH["land"] = ("dram", [32, 128, 32], "float32")
 for _b in range(8):
     SCRATCH["ps%d" % _b] = ("psum", [128, 512], "float32")
 
-SEMAPHORES = (["sv", "sa", "sp", "sg", "ls", "tree_in", "st0", "st1", "w0in", "w0own", "rot0", "rot1", "fq", "fst0", "fst1",
-               "yo", "ya", "pa0", "pa1", "pb0", "pb1"] + ["fa%d" % i for i in range(4)])
+SEMAPHORES = (["sv", "sa", "sp", "sg", "ls", "hi_in", "lo_in", "w0in", "w0own", "rot0", "rot1", "fq", "fst0", "fst1",
+               "yo", "ya"] + ["fa%d" % i for i in range(4)]
+              + [n + str(i) for n in ("st", "pa", "pb") for i in range(NIN)])
 
 
 def _bits(es):
@@ -79,15 +82,15 @@ def helper_program(g, core, T, topo):
     rid, pid, _ = topo.addr(rc)
     q = [r for r in _others(grp) if _helper_of(T, topo, grp, r) == core][0]
     sent = 0
-    for h in range(2):
+    for h in range(NIN):
         for qu in (g.sync, g.scalar):
             qu.wait_ge(T.sem["pa%d" % h], 1)
         for j in range(NG):
             qu = g.sync if j % 2 == 0 else g.scalar
-            qu.dma_start(T.rep[16 * j:16 * j + 16, h * 512:h * 512 + 512], T.piece[h]).then_inc(T.sem["pb%d" % h], 16)
-    for h in range(2):
+            qu.dma_start(T.rep[16 * j:16 * j + 16, h * CIN:(h + 1) * CIN], T.piece[h]).then_inc(T.sem["pb%d" % h], 16)
+    for h in range(NIN):
         g.wait_ge(T.sem["pb%d" % h], 16 * NG)
-        g.remote_dma(T.w0[:, q * M + h * 512:q * M + h * 512 + 512], T.rep[:, h * 512:h * 512 + 512],
+        g.remote_dma(T.w0[:, q * M + h * CIN:q * M + (h + 1) * CIN], T.rep[:, h * CIN:(h + 1) * CIN],
                      T.sem.w0in, T.sem.ls, pid, rid, topo.mask(core, rc))
         sent += len(topo.engines(core, rc))
     far = _far_senders(T, topo, grp)
@@ -107,6 +110,7 @@ def rank_program(g, core, T, topo):
     SEM = {"v": "sv", "a": "sa", "p": "sp", "g": "sg"}
     cnt = {"v": 0, "a": 0, "p": 0, "g": 0}
     seen = {k: {} for k in Q}
+    wrote, read = {}, {}
     V, S, PE = g.vector, g.scalar, g.tensor
     ps = [T["ps%d" % b] for b in range(8)]
     W = [T.w0, T.w1, T.w2]
@@ -118,47 +122,81 @@ def rank_program(g, core, T, topo):
                 Q[q].wait_ge(T.sem[sem], n)
                 seen[q][sem] = n
 
-    def done(q, inst):
-        inst.then_inc(T.sem[SEM[q]], 1)
-        cnt[q] += 1
-        return (SEM[q], cnt[q])
-
     def last(q):
         return (SEM[q], cnt[q])
 
-    def ts(out, in0, s1, s2, op0, op1=None):
+    def after(q, r, w):
+        for k in r:
+            if k in wrote:
+                need(q, wrote[k])
+            if isinstance(k, int):
+                need(q, *[t for t in read.get(k, {}).values() if t[0] != SEM.get(q)])
+        for k in w:
+            old = list(read.get(k, {}).values()) + ([wrote[k]] if k in wrote else [])
+            need(q, *[t for t in old if t[0] != SEM.get(q) or q != "p"])
+
+    def call(q, r, w, make):
+        after(q, r, w)
+        make().then_inc(T.sem[SEM[q]], 1)
+        cnt[q] += 1
+        for k in r:
+            read.setdefault(k, {})[q] = last(q)
+        for k in w:
+            wrote[k] = last(q)
+            read[k] = {}
+        return last(q)
+
+    def ts(r, w, out, in0, s1, s2, op0, op1=None):
         if op1 is None:
-            return done("v", V.tensor_scalar(out, in0, s1, None, op0))
-        return done("v", V.tensor_scalar(out, in0, s1, s2, op0, op1))
+            return call("v", r, w, lambda: V.tensor_scalar(out, in0, s1, None, op0))
+        return call("v", r, w, lambda: V.tensor_scalar(out, in0, s1, s2, op0, op1))
 
-    def tt(out, in0, in1, op):
-        return done("v", V.tensor_tensor(out, in0, in1, op))
+    def tt(r, w, out, in0, in1, op):
+        return call("v", r, w, lambda: V.tensor_tensor(out, in0, in1, op))
 
-    def cp(q, out, in_, scale=1.0):
-        if q == "v":
-            return done("v", V.tensor_copy(out, in_))
-        return done("a", S.activation(out, in_, F.Copy, scale=scale))
+    def cp(q, r, w, out, in_, scale=None):
+        if q == "a":
+            return call(q, r, w, lambda: S.activation(out, in_, F.Copy, scale=1.0 if scale is None else scale))
+        if scale is None:
+            return call(q, r, w, lambda: V.tensor_copy(out, in_))
+        return ts(r, w, out, in_, scale, None, A.mult)
 
-    def chain():
-        need("v", last("v"))
+    def iota(w, out, pat, cm, base=0):
+        return call("g", [], w, lambda: g.iota(out, pat, base, cm, allow_small_or_imprecise_dtypes=True))
 
-    def iota(out, pat, cm):
-        return done("g", g.iota(out, pat, 0, cm, allow_small_or_imprecise_dtypes=True))
+    def mms(r, w, calls):
+        def make():
+            for c in calls[:-1]:
+                PE.matmul(*c)
+            return PE.matmul(*calls[-1])
+        return call("p", r, w, make)
 
-    S.dma_start(T.xi[0:48, :], T.tree[rank]).then_inc(T.sem.tree_in, 16)
-    S.dma_start(T.xi[64:112, :], T.tree[rank]).then_inc(T.sem.tree_in, 16)
-    S.dma_start(T.xi[48:64, :], T.tree[rank, 0:P]).then_inc(T.sem.tree_in, 16)
-    for h in range(2):
-        g.sync.dma_start(T.stg[h * NG:(h + 1) * NG], T.v[:, h * 512:h * 512 + 512]).then_inc(T.sem["st%d" % h], 16)
+    def weave(*chains):
+        chains = list(chains)
+        while chains:
+            chains = [c for c in chains if next(c, False)]
+
+    def links(*calls):
+        for c in calls:
+            c[0](*c[1:])
+            yield True
+
+    S.dma_start(T.xi[0:48, :], T.tree[rank]).then_inc(T.sem.hi_in, 16)
+    S.dma_start(T.xi[48:64, :], T.tree[rank, 0:P]).then_inc(T.sem.hi_in, 16)
+    g.sync.dma_start(T.xi[64:112, :], T.tree[rank]).then_inc(T.sem.lo_in, 16)
+    for h in range(NIN):
+        g.sync.dma_start(T.stg[h * NG:(h + 1) * NG], T.v[:, h * CIN:(h + 1) * CIN]).then_inc(T.sem["st%d" % h], 16)
     for j in range(NG):
         g.sync.dma_start(T.w0[16 * j:16 * j + 16, rank * M:(rank + 1) * M],
                          T.v[16 * rank:16 * rank + 16, :]).then_inc(T.sem.w0own, 16)
 
-    i_pc = done("g", g.iota(T.pcol[:, 0:1], [[0, 1]], 0, 1))
-    i_p1 = iota(T.p1[:, :], [[0, 8], [16, 16]], -1)
-    i_iy = iota(T.iy[:, :], [[1, 144]], 0)
+    call("g", [], ["pcol"], lambda: g.iota(T.pcol[:, 0:1], [[0, 1]], 0, 1))
+    iota(["l16"], T.l16[:, :], [[0, 8], [16, 16]], 0)
+    iota(["iy"], T.iy[:, :], [[1, 160]], 0, -16)
+    iota(["ib"], T.ib[:, 0:48], [[16, 3], [1, 2], [2, 8]], 0)
+    iota(["ic"], T.ib[:, 48:72], [[1, 3], [16, 8]], 0)
     sent = 0
-    for h in range(2):
+    for h in range(NIN):
         tr = []
         for n, grp in enumerate(_others(rank)):
             hc = _helper_of(T, topo, grp, rank)
@@ -167,170 +205,178 @@ def rank_program(g, core, T, topo):
         sent += len(tr)
         need("g", ("st%d" % h, 16))
         g.remote_dma_fused(tr, local_sem=T.sem.ls)
-    i_pr = iota(T.pr[:, :], [[0, 2], [1, 128]], -1)
-    i_sl = iota(T.sl[:, :], [[16, 64]], 1)
+    iota(["pr"], T.pr[:, :], [[0, 2], [1, 128]], -1)
+    iota(["sl"], T.sl[:, :], [[16, 64]], 1)
 
-    need("v", i_pc)
-    ts(T.ci[:, 0:1], T.pcol[:, 0:1], 15, None, A.bitwise_and)
-    ts(T.ci[:, 1:2], T.pcol[:, 0:1], 4, None, A.arith_shift_right)
-    ts(T.ci[:, 2:3], T.pcol[:, 0:1], 1, None, A.bitwise_and)
-    t_ci = ts(T.ci[:, 3:4], T.pcol[:, 0:1], 14, None, A.bitwise_and)
-    need("v", i_p1)
-    t_lt = {}
-
-    def spreading(a, b):
-        for k in range(a, b):
-            t_lt[k] = ts(T.lt[:, k * 128:k * 128 + 128], T.p1[:, :], float(-k), None, A.is_equal)
-
-    spreading(0, 4)
-    need("v", t_ci)
-    t_cf = cp("v", cf[:, 0:4], T.ci[:, 0:4])
-    spreading(4, 8)
-    need("v", t_cf, i_iy)
-    ts(cf[:, 4:5], cf[:, 3:4], 8.0, 16.0, A.mult, A.add)
-    ts(cf[:, 5:6], cf[:, 2:3], -1.0, 1.0, A.mult, A.add)
-    ts(cf[:, 6:7], cf[:, 1:2], 16.0, 16.0, A.mult, A.add)
-    ts(cf[:, 8:11], T.iy[:, 0:3], cf[:, 1:2], 64.0, A.is_equal, A.mult)
-    ts(cf[:, 11:14], T.iy[:, 4:7], cf[:, 1:2], 0.5, A.is_equal, A.mult)
-    ts(cf[:, 14:17], T.iy[:, 0:3], cf[:, 0:1], 64.0, A.is_equal, A.mult)
-    ts(cf[:, 17:20], T.iy[:, 4:7], cf[:, 0:1], 0.5, A.is_equal, A.mult)
-    chain()
-    tt(cf[:, 20:23], cf[:, 8:11], cf[:, 11:14], A.add)
-    tt(cf[:, 23:26], cf[:, 14:17], cf[:, 17:20], A.add)
-    ts(T.tab[:, P:P + 1], cf[:, 0:1], 3.0, 128.0, A.is_lt, A.mult)
-    need("v", ("tree_in", 48))
-    ts(T.xt[0:64, :], T.xi[0:64, :], 7, None, A.arith_shift_right)
-    ts(T.xt[64:112, :], T.xi[64:112, :], 127, None, A.bitwise_and)
-    chain()
-    t_xb = cp("v", T.xb[0:112, :], T.xt[0:112, :])
-    ts(cf[:, 26:29], cf[:, 20:23], cf[:, 5:6], None, A.mult)
-    t_w = ts(cf[:, 29:32], cf[:, 20:23], cf[:, 2:3], None, A.mult)
-    spreading(8, 16)
+    MASKS = (112, 15, 14, 49, 3, 63, 115)
+    call("v", [], ["wt"], lambda: V.memset(cf[0:64, 7:8], 64.0))
+    call("v", [], ["wt2"], lambda: V.memset(cf[64:128, 7:8], 0.5))
+    call("v", [], [("d0", d, 0) for d in range(3)], lambda: V.memset(T.d0[:, 0::4], 0.0))
+    for n, x in enumerate(MASKS):
+        ts(["pcol"], [("ci", n)], T.ci[:, n:n + 1], T.pcol[:, 0:1], x, None, A.bitwise_and)
+    call("v", [], [("d1", d, 0) for d in range(3)], lambda: V.memset(T.d1[:, 1::4], 0.0))
+    cp("v", [("ci", 6)], ["cf"], cf[:, 0:7], T.ci[:, 0:7])
     for d in range(3):
-        ts(T.zs[:, d * 144:d * 144 + 144], T.iy[:, :], cf[:, 6:7], cf[:, 23 + d:24 + d], A.is_equal, A.mult)
-    need("v", t_w)
-    t_zc = {}
-    for d in range(3):
-        for h in range(2):
-            n = 2 * d + h
-            t_zc[d] = ts(T.zc[:, n * 144:n * 144 + 144], T.iy[:, :], cf[:, 4:5], cf[:, 26 + 3 * h + d:27 + 3 * h + d],
-                         A.is_equal, A.mult)
+        call("v", [], [("zero", d)], lambda: V.memset(W[d][:, P:WW], 0.0))
+    ts(["cf", "l16"], ["l0"], T.l0[:, :], T.l16[:, :], cf[:, 0:1], None, A.is_equal)
+    ts(["iy"], ["ck"], T.ck[:, 0:16], T.iy[:, 16:32], cf[:, 1:2], None, A.is_equal)
 
-    t_ev, t_sel, t_off = {}, {}, {}
-    on_v = (5, 7, 9, 11, 13, 15)
+    def spreading(q, k):
+        cp(q, ["l0", "ck"], [("lt", k)], T.lt[:, k * 128:k * 128 + 128], T.l0[:, :], T.ck[:, k:k + 1])
 
-    def spread(k):
-        b = ps[3 + k % 5]
-        need("p", t_xb, t_lt[k])
-        if k >= 5:
-            need("p", t_ev[k - 5])
-        t = done("p", PE.matmul(b[:, :], T.lt[0:112, k * 128:k * 128 + 128], T.xb[0:112, :], True, True))
-        q = "v" if k in on_v else "a"
-        need(q, t)
-        t_ev[k] = cp(q, T.tab[:, k * 512:k * 512 + 512], b[:, :])
+    for k in range(8):
+        spreading("a", k)
+    ts(["ib"], ["cz"], T.ck[:, 16:22], T.ib[:, 0:48:8], cf[:, 3:4], None, A.is_equal)
+    ts([], ["z0"], T.z0[:, :], T.iy[:, 0:144], 0.125, cf[:, 2:3], A.mult, A.is_equal)
 
-    def own_codes(d):
-        need("p", t_zc[d])
-        for h in range(2):
-            z = (2 * d + h) * 144
-            for i in range(16):
-                mm = PE.matmul(ps[d][:, 32 * h:32 * h + 32], T.zc[0:112, z + 16 - i:z + 144 - i], T.xb[0:112, i::16],
-                               i == 0, i == 15)
-            t_sel[d, 1] = done("p", mm)
+    need("v", ("lo_in", 16))
+    ts([], ["xl"], T.xt[64:112, :], T.xi[64:112, :], 127, None, A.bitwise_and)
+    need("v", ("hi_in", 32))
+    ts([], ["xt"], T.xt[0:64, :], T.xi[0:64, :], 7, None, A.arith_shift_right)
+    ts([], ["cs"], T.ck[:, 22:25], T.iy[:, 16:19], cf[:, 4:5], None, A.is_equal)
+    ts([], ["z1"], T.z1[:, :], T.iy[:, 0:144], cf[:, 0:1], None, A.is_equal)
+    cp("v", ["xt", "xl"], ["xb"], T.xb[0:112, :], T.xt[0:112, :], cf[0:112, 7:8])
+    ts([], ["sb"], T.sb[:, 0:48], T.ib[:, 0:48], cf[:, 5:6], None, A.is_equal)
+    for k in range(8, 16):
+        spreading("v", k)
+    ts(["ic"], ["sn"], T.sb[:, 48:72], T.ib[:, 48:72], cf[:, 6:7], None, A.is_equal)
+    ts([], [("tab", 16)], T.tab[:, P:P + 1], cf[:, 1:2], 3.0, float(P), A.is_lt, A.mult)
+    for n in range(6):
+        cp("a", ["z0", "cz"], [("zc", n)], T.zc[:, n * 144:n * 144 + 144], T.z0[:, :], T.ck[:, 16 + n:17 + n])
+
+    def shifted(d):
+        cp("a", ["z1", "cs"], [("zs", d)], T.zs[:, d * 144:d * 144 + 144], T.z1[:, :], T.ck[:, 22 + d:23 + d])
+
+    def cross(b):
+        return 2 * (b % 4) + b // 4
 
     for k in range(16):
-        spread(k)
+        b = (4, 5, 0, 1, 2, 6, 7)[k % 7]
+        mms(["xb", ("lt", k)], [b], [(ps[b][:, :], T.lt[0:112, k * 128:k * 128 + 128], T.xb[0:112, :], True, True)])
+        cp("va"[k % 2], [b], [("tab", k)], T.tab[:, k * 512:k * 512 + 512], ps[b][:, :])
         if k == 6:
-            own_codes(0)
-    own_codes(1)
-    own_codes(2)
-    t_tab = (t_ev[14], t_ev[15])
+            mms(["xb", "sb"], [3], [(ps[3][:, 64 * d + 16 * b:64 * d + 16 * b + 16], T.xb[0:112, 128 * b:128 * b + 128],
+                                     T.sb[0:112, 16 * d:16 * d + 16], True, True) for d in range(3) for b in range(4)])
+        if k == 10:
+            ts([3], [("off", d, 1) for d in range(3)], T.off[:, 0:192], ps[3][:, 0:192], -0.25, None, A.add)
+    TAB = [("tab", k) for k in range(17)]
 
-    def offc(d, k):
-        return (4 * d + k - 1) * 64
+    def own_codes(d, h):
+        z = (2 * d + h) * 144
+        mms(["xb", ("zc", 2 * d + h)], [d], [(ps[d][:, 32 * h:32 * h + 32], T.zc[0:112, z + 16 - i:z + 144 - i],
+                                              T.xb[0:112, i::16], i == 0, i == 15) for i in range(16)])
+
+    def bank4(d):
+        return d or 3
+
+    def cand(d, k):
+        return (3 * d + k - 2) * M
+
+    def climb(q, d, k, a, b):
+        c, o = cand(d, k), 192 * (k - 2) + 64 * d
+        cp(q, [("off", d, k - 1)] + TAB, [("cand", d, k, q, a)], T.cand[:, c + 16 * a:c + 16 * b],
+           T.tab[:, 0:P + 1].indirect(T.off[:, o + a:o + b]))
+
+    def both(d, k, nv):
+        climb("v", d, k, 0, nv)
+        climb("a", d, k, nv, 64)
+
+    def climbed(d, k):
+        return [key for key in wrote if isinstance(key, tuple) and key[:3] == ("cand", d, k)]
+
+    def pick(d, k):
+        c, bank = cand(d, k), bank4(d) if k == 4 else d
+        calls = []
+        for b in range(8):
+            src, dst = (b, 256 + 8 * cross(b)) if k == 3 else (cross(b), 64 * (k - 1) + 8 * b)
+            calls.append((ps[bank][:, dst:dst + 8], T.cand[:, c + 128 * src:c + 128 * src + 128],
+                          T.sb[:, 48 + 8 * d:56 + 8 * d], True, True))
+        mms(climbed(d, k) + ["sn"], [bank], calls)
 
     def offsets(d, k):
-        need("v", t_sel[d, k])
-        c = offc(d, k)
-        t_off[d, k] = ts(T.off[:, c:c + 64], ps[d][:, 64 * (k - 1):64 * k], -0.25, None, A.add)
+        c, o = (64 if k == 2 else 256), 192 * (k - 1) + 64 * d
+        ts([d], [("off", d, k)], T.off[:, o:o + 64], ps[d][:, c:c + 64], -0.25, None, A.add)
 
-    def climb(q, d, k, a=0, b=64):
-        need(q, t_off[d, k - 1], *t_tab)
-        c = offc(d, k - 1)
-        return cp(q, T.cand[:, d * M + 16 * a:d * M + 16 * b], T.tab[:, 0:P + 1].indirect(T.off[:, c + a:c + b]))
+    def keep3(d):
+        c = cand(d, 3)
+        mms(climbed(d, 3) + [("zs", d)], [d],
+            [(ps[d][:, 128:192], T.zs[:, d * 144 + 16 - i:d * 144 + 144 - i], T.cand[:, c + i:c + M:16], i == 0, i == 15)
+             for i in range(16)])
 
-    def pick(d, k, *toks):
-        need("p", *toks)
-        for i in range(16):
-            mm = PE.matmul(ps[d][:, 64 * (k - 1):64 * k], T.zs[:, d * 144 + 16 - i:d * 144 + 144 - i],
-                           T.cand[:, d * M + i:(d + 1) * M:16], i == 0, i == 15)
-        t_sel[d, k] = done("p", mm)
-
-    def step(d, k):
-        offsets(d, k - 1)
-        pick(d, k, climb("v", d, k, 0, 32), climb("a", d, k, 32, 64))
-
-    for k in (2, 3, 4):
-        step(0, k)
-        if not LATE:
-            offsets(1, k - 1)
-            offsets(2, k - 1)
-            pick(1, k, climb("a", 1, k))
-            pick(2, k, climb("a" if k == 4 else "v", 2, k))
-        elif k < 4:
-            step(1, k)
-        else:
-            offsets(1, 3)
-            offsets(2, 1)
-            pick(1, 4, climb("a", 1, 4))
-            pick(2, 2, climb("a", 2, 2))
-
-    need("v", i_pr, i_sl)
-    ts(T.zr[:, :], T.pr[:, :], 0.0, None, A.is_equal)
-    ts(cf[:, 7:8], cf[:, 1:2], float(M - 16), None, A.mult)
-    ts(cf[:, 4:5], cf[:, 1:2], float(-M), float(2 * P), A.mult, A.add)
-    for w in W:
-        done("v", V.memset(w[:, P:WW], 0.0))
-    done("v", V.memset(T.ne[:, 0::3], 0.0))
-    chain()
-    ts(T.offs[:, :], T.sl[:, :], cf[:, 7:8], None, A.add)
-
-    def lists(d):
-        offsets(d, 4)
-        pp, ff, ee, ne, tq, so = T.pp, T.ff, T.ee, T.ne, T.tt, T.so
-        c = offc(d, 1)
-        chain()
-        ts(pp[:, :], T.off[:, c:c + 256], float(-P), None, A.add)
-        chain()
-        tt(ff[:, :], ps[d][:, 0:256], pp[:, :], A.subtract)
-        chain()
-        for k in range(3):
-            tt(ee[:, 64 * k:64 * k + 64], ff[:, 64 * k + 64:64 * k + 128], ff[:, 0:64], A.not_equal)
-        chain()
-        for k in range(3):
-            tt(tq[:, 2 - k::3], pp[:, 64 * k + 64:64 * k + 128], ee[:, 64 * k:64 * k + 64], A.mult)
-        for k in range(2):
-            ts(ne[:, 2 - k::3], ee[:, 64 * k:64 * k + 64], -1.0, 1.0, A.mult, A.add)
-        chain()
-        done("v", V.tensor_tensor_scan(so[:, :], ne[:, :], tq[:, :], 0.0, A.mult, A.add))
-        o = T.offm[:, 128 * d:128 * d + 128]
+    def address(d, a, src, key):
+        o = T.offm[:, 128 * d + a:128 * d + a + 64]
         if d == 0:
-            ts(T.offm[:, 64:128], pp[:, 0:64], float(P), None, A.add)
-            chain()
-            return ts(T.offm[:, 0:64], so[:, 2::3], float(P), None, A.add)
-        ts(T.ri[:, 64:128], pp[:, 0:64], cf[:, 4:5], None, A.add)
-        ts(T.zi[:, 64:128], pp[:, 0:64], 0.0, float(P), A.is_ge, A.mult)
-        chain()
-        ts(T.ri[:, 0:64], so[:, 2::3], cf[:, 4:5], None, A.add)
-        ts(T.zi[:, 0:64], so[:, 2::3], 0.0, float(P), A.is_ge, A.mult)
-        chain()
-        ts(T.ri[:, :], T.ri[:, :], P - 1, None, A.bitwise_and)
-        chain()
-        tt(T.ri[:, :], T.ri[:, :], T.zi[:, :], A.max)
-        chain()
-        return cp("v", o, T.ri[:, :])
+            ts([key], [("offm", d, a)], o, src, float(P), None, A.add)
+            return
+        ri, zi = T.ri[:, a:a + 64], T.zi[:, a:a + 64]
+        ts([key, "c8"], [("ri", a)], ri, src, cf[:, 8:9], None, A.add)
+        ts([key], [("zi", a)], zi, src, 0.0, float(P), A.is_ge, A.mult)
+        yield True
+        ts([("ri", a)], [("ri", a)], ri, ri, P - 1, None, A.bitwise_and)
+        yield True
+        tt([("ri", a), ("zi", a)], [("ri", a)], ri, ri, zi, A.max)
+        yield True
+        cp("v", [("ri", a)], [("offm", d, a)], o, ri)
 
-    ready = [lists(0), ("w0in", 2 * sum(len(topo.engines(_helper_of(T, topo, rank, q), core)) for q in _others(rank))),
+    def head(d):
+        c = slice(192 * d, 192 * d + 64)
+        ts([d], [("pi", d, 1)], T.pi[:, c], ps[d][:, 0:64], -0.25 - P, None, A.add)
+        yield True
+        tt([d, ("pi", d, 1)], [("ff", d, 1)], T.ff[:, c], ps[d][:, 0:64], T.pi[:, c], A.subtract)
+        yield True
+        ts([("ff", d, 1)], [("tg", d)], T.tg[:, 64 * d:64 * d + 64], T.ff[:, c], -1.0, 2 * P + 0.5, A.mult, A.add)
+
+    def parent(d):
+        yield from address(d, 64, T.pi[:, 192 * d:192 * d + 64], ("pi", d, 1))
+
+    def side(d, k):
+        c, e = slice(192 * d + 64 * k - 64, 192 * d + 64 * k), slice(256 * d + 5 - k, 256 * d + 256, 4)
+        tg, src = T.tg[:, 64 * d:64 * d + 64], ps[d][:, 64 * k - 64:64 * k]
+        tt([d, ("tg", d)], [("ff", d, k)], T.ff[:, c], src, tg, A.subtract)
+        tt([d, ("tg", d)], [("pi", d, k)], T.pi[:, c], src, tg, A.subtract)
+        yield True
+        tt([("pi", d, k), ("ff", d, k)], [("ee", d, k)], T.ee[:, c], T.ff[:, c], T.pi[:, c], A.is_equal)
+        tt([("pi", d, k), ("ff", d, k)], [("d0", d, k)], T.d0[:, e], T.ff[:, c], T.pi[:, c], A.not_equal)
+        yield True
+        tt([("ee", d, k), ("ff", d, k)], [("d1", d, k)], T.d1[:, e], T.ff[:, c], T.ee[:, c], A.mult)
+
+    def tail(d):
+        tg, z, b = T.tg[:, 64 * d:64 * d + 64], 256 * d, bank4(d)
+        tt([b, ("tg", d)], [("d1", d, 0)], T.d1[:, z:z + 256:4], ps[b][:, 192:256], tg, A.subtract)
+        tt([b, ("tg", d)], ["z4"], T.z4[:, :], ps[b][:, 192:256], tg, A.subtract)
+        yield True
+        tt(["z4", ("d1", d, 0)], [("d0", d, 0)], T.d0[:, z + 1:z + 256:4], T.d1[:, z:z + 256:4], T.z4[:, :], A.is_equal)
+        yield True
+        call("v", [(n, d, k) for n in ("d0", "d1") for k in (0, 2, 3)], ["so"],
+             lambda: V.tensor_tensor_scan(T.so[:, :], T.d0[:, z:z + 256], T.d1[:, z:z + 256], 0.0, A.mult, A.add))
+        yield True
+        yield from address(d, 0, T.so[:, 3::4], "so")
+
+    def on(*chains):
+        for c in chains:
+            next(c, False)
+
+    def constants():
+        ts([], ["c8"], cf[:, 8:9], cf[:, 0:1], -M / 16.0, float(2 * P), A.mult, A.add)
+        ts([], ["c9"], cf[:, 9:10], cf[:, 0:1], M / 16.0 - 1, None, A.mult)
+
+    def turner():
+        ts(["pr"], ["zr"], T.zr[:, :], T.pr[:, :], 0.0, None, A.is_equal)
+
+    H, PA, S2, S3, TL = ([f(d) for d in range(3)] for f in (head, parent, lambda d: side(d, 2), lambda d: side(d, 3), tail))
+    own_codes(0, 0); own_codes(0, 1)
+    both(0, 2, 32); pick(0, 2); own_codes(1, 0)
+    both(1, 2, 24); offsets(0, 2); on(H[0]); pick(1, 2); turner(); on(H[0]); shifted(0)
+    both(0, 3, 30); pick(0, 3); offsets(1, 2); own_codes(1, 1); on(H[0], PA[0]); constants(); shifted(1)
+    climb("v", 1, 3, 0, 16); offsets(0, 3); on(S2[0]); keep3(0); climb("v", 1, 3, 16, 26); climb("a", 1, 3, 26, 64); pick(1, 3)
+    both(0, 4, 32); pick(0, 4)
+    on(S3[0]); offsets(1, 3); on(S2[0]); keep3(1); shifted(2); climb("a", 1, 4, 0, 64)
+    on(S3[0], S2[0], TL[0], S3[0], H[1])
+    ts(["sl", "c9"], ["offs"], T.offs[:, :], T.sl[:, :], cf[:, 9:10], None, A.add)
+    on(TL[0], H[1], PA[1], TL[0], H[1], PA[1], TL[0], PA[1], S2[1], S3[1], PA[1], S2[1], S3[1])
+    pick(1, 4); own_codes(2, 0); own_codes(2, 1)
+
+    ready = [("w0in", NIN * sum(len(topo.engines(_helper_of(T, topo, rank, q), core)) for q in _others(rank))),
              ("w0own", 16 * NG)]
     far = _far_senders(T, topo, rank)
 
@@ -340,94 +386,91 @@ def rank_program(g, core, T, topo):
         win = w[:, 0:P + 1]
         need("v", *ready)
         need("a", *ready)
-        tg, tsum, th, tn, t_rot, t_e = {}, {}, {}, {}, {}, {}
-        free0 = [5, 6, 7, 0][:NPE]
-        free1 = [3, 4] + [b for b in (5, 6, 7, 0) if b not in free0]
-        banks = (free0, (free1 + free0)[:NPE])
+        WIN = [("zero", d)] + ([("w", d, c) for c in range(4)] + [("slot", d, h, n) for h in range(2) for n in range(NPE)]
+                               if d else [])
+        banks = ((3, 4, 5), (6, 7, 0)) if d == 0 else ((5, 6, 7), (0, 1, 3))
 
         def ck(buf, c):
             return buf[:, 256 * c:256 * c + 256]
 
         def ga(c):
-            tg[c] = cp("a", ck(T.gb, c), win.indirect(T.offm[:, 128 * d + 16 * c:128 * d + 16 * c + 16]))
+            o = 128 * d + 16 * c
+            cp("a", WIN + [("offm", d, 0)], [("gb", c)], ck(T.gb, c), win.indirect(T.offm[:, o:o + 16]))
 
         def su(c):
-            need("v", tg[c])
             o = 128 * d + 64 + 16 * c
-            tsum[c] = tt(ck(T.ss, c), win.indirect(T.offm[:, o:o + 16]), ck(T.gb, c), A.add)
+            tt(WIN + [("offm", d, 64), ("gb", c)], [("ss", c)], ck(T.ss, c), win.indirect(T.offm[:, o:o + 16]), ck(T.gb, c), A.add)
 
         def hv(c):
-            return ck(T.hh, c) if d == 0 else ps[3 + c % 2][:, 0:256]
+            return (("hh", c), ck(T.hh, c)) if d == 0 else (4 + c, ps[4 + c][:, 0:256])
 
         def ha(c):
-            need("a", tsum[c])
-            if c >= 2:
-                need("a", tn[c - 2])
-            th[c] = cp("a", hv(c), ck(T.ss, c), -0.5)
+            cp("a", [("ss", c)], [hv(c)[0]], hv(c)[1], ck(T.ss, c), (-0.5, None, 0.25)[d])
 
-        def turn(h):
-            cols = slice(512 * h, 512 * h + 512)
-            need("s", tn[2 * h + 1])
+        def turn(a, b):
+            cols = slice(256 * a, 256 * b)
+            after("s", [("w", d + 1, b - 1)], [])
             for t in DMA_SLOTS:
-                oc = slice(t * M + 512 * h, t * M + 512 * h + 512)
+                oc = slice(t * M + 256 * a, t * M + 256 * b)
                 g.sync.dma_start(out[0:128 - 16 * t, oc], out[16 * t:128, cols]).then_inc(T.sem["rot%d" % d], 16)
                 g.sync.dma_start(out[128 - 16 * t:128, oc], out[0:16 * t, cols]).then_inc(T.sem["rot%d" % d], 16)
 
-        def pe_turn(h, n):
-            need("p", tn[2 * h + 1])
-            if h == 1 and n >= len(free1):
-                need("p", t_e[0, n - len(free1)])
-            t = PE_SLOTS[n]
-            t_rot[h, n] = done("p", PE.matmul(ps[banks[h][n]][:, :], T.zr[:, 16 * t:16 * t + 128],
-                                              out[:, 512 * h:512 * h + 512], True, True))
+        def pe_turn(c):
+            for n, t in enumerate(PE_SLOTS):
+                b = banks[c // 2][n]
+                mms([("w", d + 1, c), "zr"], [b], [(ck(ps[b], c % 2), T.zr[:, 16 * t:16 * t + 128], ck(out, c), True, True)])
 
         def evac(q, h, n):
-            need(q, t_rot[h, n])
-            t = PE_SLOTS[n]
-            t_e[h, n] = cp(q, out[:, t * M + 512 * h:t * M + 512 * h + 512], ps[banks[h][n]][:, :])
+            if n < NPE:
+                t, b = PE_SLOTS[n], banks[h][n]
+                cp(q, [b], [("slot", d + 1, h, n)], out[:, t * M + 512 * h:t * M + 512 * h + 512], ps[b][:, :])
+
+        def own_next(h):
+            src, keys = out[:, 512 * h:512 * h + 512], [("w", d + 1, 2 * h), ("w", d + 1, 2 * h + 1)]
+            if d == 0:
+                cp("a", keys, [3 + h], ps[3 + h][:, :], src, -2.0)
+            else:
+                cp("a", keys, [("hh", 2 * h), ("hh", 2 * h + 1)], T.hh[:, 512 * h:512 * h + 512], src, -0.5)
 
         def nw(c):
-            need("v", th[c])
-            own = win.indirect(T.offs[:, 16 * c:16 * c + 16]) if d == 0 else ck(w, c)
-            tn[c] = tt(ck(out, c), own, hv(c), A.add)
-            if d < 2 and c % 2 == 1:
-                turn(c // 2)
-            if d < 2 and c == 1:
-                for n in range(NPE):
-                    pe_turn(0, n)
-            if LATE and d == 1 and c == 0:
-                offsets(2, 3)
+            if d == 0:
+                tt([("hh", c), "offs"], [("w", 1, c)], ck(out, c), win.indirect(T.offs[:, 16 * c:16 * c + 16]), ck(T.hh, c), A.add)
+            elif d == 1:
+                tt([("ss", c), 3 + c // 2], [("w", 2, c)], ck(out, c), ck(T.ss, c), ck(ps[3 + c // 2], c % 2), A.add)
+            else:
+                tt([("hh", c), 4 + c], [("w", 3, c)], ck(out, c), ck(T.hh, c), hv(c)[1], A.add)
+            if d < 2:
+                for a, b in TURN_PIECES:
+                    if b == c + 1:
+                        turn(a, b)
+                if c < 2:
+                    pe_turn(c)
             if d == 2 and c < 2:
-                need("g", tn[c])
+                after("g", [("w", 3, c)], [])
                 rid, pid, _ = topo.addr(far[c])
                 g.remote_dma(T.fh[:, :], ck(T.res, c), T.sem.fq, T.sem.ls, pid, rid, _bits(_half_engines(topo, core, far[c])))
             if d == 2 and c >= 2:
-                need("s", tn[c])
+                after("s", [("w", 3, c)], [])
                 b = (c - 2) * NG
                 g.sync.dma_start(T.fs[b:b + NG], ck(T.res, c)).then_inc(T.sem["fst%d" % (c - 2)], 16)
 
-        ga(0); su(0); ga(1); ha(0); su(1); ga(2); nw(0); ha(1); su(2); ga(3); nw(1); ha(2); su(3); nw(2); ha(3); nw(3)
+        if d != 1:
+            ga(0); ga(1); su(0); su(1); ga(2); ha(0); su(2); ga(3); nw(0); ha(1); su(3); ha(2); nw(1); ha(3); nw(2); nw(3)
+        if d == 0:
+            climb("a", 2, 2, 0, 52); on(S2[1], S3[1]); climb("v", 2, 2, 52, 64); pick(2, 2); pe_turn(2)
+            on(TL[1]); evac("a", 0, 0); evac("v", 0, 1); on(TL[1]); offsets(2, 2); on(H[2]); evac("a", 0, 2)
+            on(TL[1], H[2]); climb("v", 2, 3, 0, 12); on(TL[1], H[2]); climb("v", 2, 3, 12, 24); climb("a", 2, 3, 24, 64)
+            on(TL[1], S2[2]); pick(2, 3); pe_turn(3); own_next(0); own_next(1)
+            on(TL[1], S2[2], TL[1], PA[2]); offsets(2, 3); keep3(2); on(S2[2], PA[2])
+            evac("v", 1, 0); evac("a", 1, 1); evac("v", 1, 2); on(PA[2], S3[2], PA[2], S3[2])
+        if d == 1:
+            ga(0); ga(1); su(0); ga(2); su(1); ga(3); nw(0); su(2); nw(1); su(3); nw(2); nw(3)
+            climb("a", 2, 4, 0, 64); pick(2, 4); pe_turn(2); pe_turn(3)
+            on(S3[2]); evac("v", 0, 0); evac("a", 0, 1); own_next(0); own_next(1)
+            weave(TL[2], links((evac, "v", 0, 2)))
+            evac("a", 1, 0); evac("v", 1, 1); evac("a", 1, 2)
         if d < 2:
-            up = None
-            if LATE and d == 0:
-                offsets(2, 2)
-            if LATE and d == 1:
-                up = climb("a", 2, 4)
-            first = "v" if up else "a"
-            for n in range(NPE):
-                evac(first if n % 2 == 0 else "va".replace(first, ""), 0, n)
-            if LATE and d == 0:
-                up = climb("a", 2, 3)
-            for n in range(NPE):
-                pe_turn(1, n)
-                if LATE and d == 1 and n == 0:
-                    pick(2, 4, up)
-            if LATE and d == 0:
-                pick(2, 3, up)
-            lists(d + 1)
-            for n in range(NPE):
-                evac("a", 1, n)
-            ready = [last("v"), last("a"), ("rot%d" % d, 16 * 4 * len(DMA_SLOTS))]
+            ready = [("rot%d" % d, 16 * 2 * len(TURN_PIECES) * len(DMA_SLOTS))]
 
     sent += sum(len(_half_engines(topo, core, f)) for f in far)
     for c in (2, 3):

@@ -3,39 +3,36 @@ from concourse.mybir import AluOpType as A, ActivationFunctionType as F
 
 P, M, NG = 8192, 1024, 8
 WW = P + 8
-NPE = 3
-NIN = 2
+NPE = 2
+IN = ((0, 320, None), (704, 864, 0), (864, 1024, 1), (320, 704, None))
+IN_WRITES = ((0,), (3,), (1, 2))
+NIN = len(IN)
 PE_SLOTS = tuple(range(1, NPE + 1))
-DMA_SLOTS = tuple(range(NPE + 1, NG))
+DMA_SLOTS = ((3, 4, 5, 6, 7), (3, 5, 6, 7))
 TURN_PIECES = ((0, 1), (1, 4))
-CIN = M // NIN
+FAR = (0, 1)
+Y_ORDER = (2, 0, 3, 1)
 
 SCRATCH = {}
 for _dt, _bufs in (
-        ("float32", dict(w0=WW, w1=WW, w2=WW, gb=M, ss=M, hh=M, res=M, cf=16, iy=160, ib=72, ck=32, pr=256, zr=256,
+        ("float32", dict(w0=WW, w1=WW, w2=WW, gb=M, ss=M, hh=M, res=M, cf=16, iy=160, ib=72, ck=32, one=256, zr=256,
                          sl=64, z0=144, z1=144, ff=576, ee=576, tg=192, d0=768, d1=768, so=256, rep=M, fh=256)),
         ("bfloat16", dict(tab=P + 16, xb=512, l16=128, l0=128, lt=2048, cand=9 * M, sb=72, zs=3 * 144, zc=6 * 144)),
         ("int32", dict(xi=512, xt=512, pcol=4, ci=8, pi=576, z4=64, ri=128, zi=128)),
         ("uint16", dict(off=576, offm=384, offs=64))):
     for _n, _w in _bufs.items():
         SCRATCH[_n] = ("sbuf", [128, _w], _dt)
-SCRATCH["stg"] = ("dram", [NIN * NG, 128, CIN // 8], "float32")
-SCRATCH["piece"] = ("dram", [NIN, 128, CIN // 8], "float32")
-SCRATCH["fs"] = ("dram", [16, 128, 32], "float32")
+for _h, (_a, _b, _via) in enumerate(IN):
+    SCRATCH["stg%d" % _h] = ("dram", [NG, 128, (_b - _a) // 8], "float32")
+    SCRATCH["piece%d" % _h] = ("dram", [128, (_b - _a) // 8], "float32")
+SCRATCH["fs"] = ("dram", [32, 128, 32], "float32")
 SCRATCH["land"] = ("dram", [32, 128, 32], "float32")
 for _b in range(8):
     SCRATCH["ps%d" % _b] = ("psum", [128, 512], "float32")
 
-SEMAPHORES = (["sv", "sa", "sp", "sg", "ls", "hi_in", "lo_in", "w0in", "w0own", "rot0", "rot1", "fq", "fst0", "fst1",
-               "yo", "ya"] + ["fa%d" % i for i in range(4)]
+SEMAPHORES = (["sv", "sa", "sp", "sg", "ls", "hi_in", "lo_in", "w0in", "w0own", "rot0", "rot1", "fq", "vq", "yo", "ya"]
+              + [n + str(i) for n in ("fa", "fst") for i in range(4)]
               + [n + str(i) for n in ("st", "pa", "pb") for i in range(NIN)])
-
-
-def _bits(es):
-    m = 0
-    for e in es:
-        m |= 1 << e
-    return m
 
 
 def _dst(topo, c):
@@ -54,21 +51,31 @@ def _helper_of(T, topo, grp, q):
 
 def _far_senders(T, topo, grp):
     rc = T.cores[grp]
-    far = [c for c in topo.cores_of(rc) if topo.die(c) != topo.die(rc) and all(topo.may_write(c, r) for r in T.cores)]
-    return far[0], far[1]
+    return [c for c in topo.cores_of(rc) if topo.die(c) != topo.die(rc) and all(topo.may_write(c, r) for r in T.cores)]
 
 
-def _half_engines(topo, src, dst):
+def _half_mask(topo, src, dst):
     es = topo.engines(src, dst)
-    return es[:len(es) // 2]
+    return sum(1 << e for e in es[:len(es) // 2]), len(es) // 2
 
 
-def _send_back(g, T, topo, src, grp, quarter, base):
+def _send_in(g, T, topo, src, owner, h):
+    tr = []
+    for n, grp in enumerate(_others(owner)):
+        hc = _helper_of(T, topo, grp, owner)
+        tr.append(RemoteDMATransfer(dst_ids=[_dst(topo, hc)], dma_engine_mask=1 << topo.engines(src, hc)[n],
+                                    remote_sem=T.sem["pa%d" % h], src=T["stg%d" % h][grp], dst=T["piece%d" % h][:]))
+    g.remote_dma_fused(tr, local_sem=T.sem.ls)
+    return len(tr)
+
+
+def _send_back(g, T, topo, src, grp, quarter):
     tr = []
     for n, q in enumerate(_others(grp)):
         c = T.cores[q]
         tr.append(RemoteDMATransfer(dst_ids=[_dst(topo, c)], dma_engine_mask=1 << topo.engines(src, c)[n],
-                                    remote_sem=T.sem["fa%d" % quarter], src=T.fs[base + q], dst=T.land[quarter * NG + grp]))
+                                    remote_sem=T.sem["fa%d" % quarter], src=T.fs[quarter * NG + q],
+                                    dst=T.land[quarter * NG + grp]))
     g.remote_dma_fused(tr, local_sem=T.sem.ls)
     return len(tr)
 
@@ -82,23 +89,31 @@ def helper_program(g, core, T, topo):
     rid, pid, _ = topo.addr(rc)
     q = [r for r in _others(grp) if _helper_of(T, topo, grp, r) == core][0]
     sent = 0
-    for h in range(NIN):
+    far = _far_senders(T, topo, grp)
+    for h, (a, b, via) in enumerate(IN):
+        if via is not None and far[via] == core:
+            g.wait_ge(T.sem.vq, NG - 1)
+            sent += _send_in(g, T, topo, core, grp, h)
+    for h in sum(IN_WRITES, ()):
+        a, b, via = IN[h]
         for qu in (g.sync, g.scalar):
             qu.wait_ge(T.sem["pa%d" % h], 1)
         for j in range(NG):
             qu = g.sync if j % 2 == 0 else g.scalar
-            qu.dma_start(T.rep[16 * j:16 * j + 16, h * CIN:(h + 1) * CIN], T.piece[h]).then_inc(T.sem["pb%d" % h], 16)
-    for h in range(NIN):
-        g.wait_ge(T.sem["pb%d" % h], 16 * NG)
-        g.remote_dma(T.w0[:, q * M + h * CIN:q * M + (h + 1) * CIN], T.rep[:, h * CIN:(h + 1) * CIN],
-                     T.sem.w0in, T.sem.ls, pid, rid, topo.mask(core, rc))
+            qu.dma_start(T.rep[16 * j:16 * j + 16, a:b], T["piece%d" % h][:]).then_inc(T.sem["pb%d" % h], 16)
+    for hs in IN_WRITES:
+        a, b = IN[hs[0]][0], IN[hs[-1]][1]
+        for h in hs:
+            g.wait_ge(T.sem["pb%d" % h], 16 * NG)
+        g.remote_dma(T.w0[:, q * M + a:q * M + b], T.rep[:, a:b], T.sem.w0in, T.sem.ls, pid, rid, topo.mask(core, rc))
         sent += len(topo.engines(core, rc))
-    far = _far_senders(T, topo, grp)
+    far = far[:len(FAR)]
     if core in far:
-        g.sync.wait_ge(T.sem.fq, len(_half_engines(topo, rc, core)))
-        g.sync.dma_start(T.fs[0:NG], T.fh[:, :]).then_inc(T.sem.fst0, 16)
+        c = FAR[far.index(core)]
+        g.sync.wait_ge(T.sem.fq, _half_mask(topo, rc, core)[1])
+        g.sync.dma_start(T.fs[c * NG:(c + 1) * NG], T.fh[:, :]).then_inc(T.sem.fst0, 16)
         g.wait_ge(T.sem.fst0, 16)
-        sent += _send_back(g, T, topo, core, grp, far.index(core), 0)
+        sent += _send_back(g, T, topo, core, grp, c)
     g.wait_ge(T.sem.ls, sent)
 
 
@@ -184,8 +199,8 @@ def rank_program(g, core, T, topo):
     S.dma_start(T.xi[0:48, :], T.tree[rank]).then_inc(T.sem.hi_in, 16)
     S.dma_start(T.xi[48:64, :], T.tree[rank, 0:P]).then_inc(T.sem.hi_in, 16)
     g.sync.dma_start(T.xi[64:112, :], T.tree[rank]).then_inc(T.sem.lo_in, 16)
-    for h in range(NIN):
-        g.sync.dma_start(T.stg[h * NG:(h + 1) * NG], T.v[:, h * CIN:(h + 1) * CIN]).then_inc(T.sem["st%d" % h], 16)
+    for h, (a, b, via) in enumerate(IN):
+        g.sync.dma_start(T["stg%d" % h][:], T.v[:, a:b]).then_inc(T.sem["st%d" % h], 16)
     for j in range(NG):
         g.sync.dma_start(T.w0[16 * j:16 * j + 16, rank * M:(rank + 1) * M],
                          T.v[16 * rank:16 * rank + 16, :]).then_inc(T.sem.w0own, 16)
@@ -196,17 +211,20 @@ def rank_program(g, core, T, topo):
     iota(["ib"], T.ib[:, 0:48], [[16, 3], [1, 2], [2, 8]], 0)
     iota(["ic"], T.ib[:, 48:72], [[1, 3], [16, 8]], 0)
     sent = 0
-    for h in range(NIN):
-        tr = []
-        for n, grp in enumerate(_others(rank)):
-            hc = _helper_of(T, topo, grp, rank)
-            tr.append(RemoteDMATransfer(dst_ids=[_dst(topo, hc)], dma_engine_mask=1 << topo.engines(core, hc)[n],
-                                        remote_sem=T.sem["pa%d" % h], src=T.stg[h * NG + grp], dst=T.piece[h]))
-        sent += len(tr)
+    for h, (a, b, via) in enumerate(IN):
         need("g", ("st%d" % h, 16))
-        g.remote_dma_fused(tr, local_sem=T.sem.ls)
-    iota(["pr"], T.pr[:, :], [[0, 2], [1, 128]], -1)
+        if via is None:
+            sent += _send_in(g, T, topo, core, rank, h)
+        else:
+            f = _far_senders(T, topo, rank)[via]
+            g.remote_dma_fused([RemoteDMATransfer(dst_ids=[_dst(topo, f)], dma_engine_mask=1 << topo.engines(core, f)[-1 - n],
+                                                  remote_sem=T.sem.vq, src=T["stg%d" % h][grp], dst=T["stg%d" % h][grp])
+                                for n, grp in enumerate(_others(rank))], local_sem=T.sem.ls)
+            sent += NG - 1
+    iota(["one"], T.one[:, :], [[0, 256]], 0, 1)
     iota(["sl"], T.sl[:, :], [[16, 64]], 1)
+    call("g", ["one"], ["zr"],
+         lambda: g.affine_select(T.zr[:, :], T.one[:, :], [[0, 2], [1, 128]], A.is_equal, 0.0, 0, -1))
 
     MASKS = (112, 15, 14, 49, 3, 63, 115)
     call("v", [], ["wt"], lambda: V.memset(cf[0:64, 7:8], 64.0))
@@ -360,25 +378,21 @@ def rank_program(g, core, T, topo):
         ts([], ["c8"], cf[:, 8:9], cf[:, 0:1], -M / 16.0, float(2 * P), A.mult, A.add)
         ts([], ["c9"], cf[:, 9:10], cf[:, 0:1], M / 16.0 - 1, None, A.mult)
 
-    def turner():
-        ts(["pr"], ["zr"], T.zr[:, :], T.pr[:, :], 0.0, None, A.is_equal)
-
     H, PA, S2, S3, TL = ([f(d) for d in range(3)] for f in (head, parent, lambda d: side(d, 2), lambda d: side(d, 3), tail))
     own_codes(0, 0); own_codes(0, 1)
     both(0, 2, 32); pick(0, 2); own_codes(1, 0)
-    both(1, 2, 24); offsets(0, 2); on(H[0]); pick(1, 2); turner(); on(H[0]); shifted(0)
-    both(0, 3, 30); pick(0, 3); offsets(1, 2); own_codes(1, 1); on(H[0], PA[0]); constants(); shifted(1)
-    climb("v", 1, 3, 0, 16); offsets(0, 3); on(S2[0]); keep3(0); climb("v", 1, 3, 16, 26); climb("a", 1, 3, 26, 64); pick(1, 3)
-    both(0, 4, 32); pick(0, 4)
-    on(S3[0]); offsets(1, 3); on(S2[0]); keep3(1); shifted(2); climb("a", 1, 4, 0, 64)
+    both(1, 2, 28); offsets(0, 2); on(H[0]); pick(1, 2); constants(); on(H[0]); shifted(0)
+    both(0, 3, 32); pick(0, 3); offsets(1, 2); own_codes(1, 1); on(H[0], PA[0]); shifted(1)
+    climb("v", 1, 3, 0, 20); offsets(0, 3); on(S2[0]); keep3(0); climb("v", 1, 3, 20, 26); climb("a", 1, 3, 26, 64); pick(1, 3)
+    both(0, 4, 30); pick(0, 4)
+    offsets(1, 3); on(S3[0], S2[0]); keep3(1); shifted(2); climb("a", 1, 4, 0, 64)
     on(S3[0], S2[0], TL[0], S3[0], H[1])
     ts(["sl", "c9"], ["offs"], T.offs[:, :], T.sl[:, :], cf[:, 9:10], None, A.add)
-    on(TL[0], H[1], PA[1], TL[0], H[1], PA[1], TL[0], PA[1], S2[1], S3[1], PA[1], S2[1], S3[1])
+    on(TL[0], H[1], PA[1], TL[0], H[1], PA[1], TL[0], S2[1], S3[1])
     pick(1, 4); own_codes(2, 0); own_codes(2, 1)
 
-    ready = [("w0in", NIN * sum(len(topo.engines(_helper_of(T, topo, rank, q), core)) for q in _others(rank))),
+    ready = [("w0in", len(IN_WRITES) * sum(len(topo.engines(_helper_of(T, topo, rank, q), core)) for q in _others(rank))),
              ("w0own", 16 * NG)]
-    far = _far_senders(T, topo, rank)
 
     for d in range(3):
         w = W[d]
@@ -386,20 +400,20 @@ def rank_program(g, core, T, topo):
         win = w[:, 0:P + 1]
         need("v", *ready)
         need("a", *ready)
-        WIN = [("zero", d)] + ([("w", d, c) for c in range(4)] + [("slot", d, h, n) for h in range(2) for n in range(NPE)]
+        WIN = [("zero", d)] + ([("w", d, c) for c in range(4)] + [("slot", d, h, n) for h in range(2) for n in range(NPE + 2)]
                                if d else [])
-        banks = ((3, 4, 5), (6, 7, 0)) if d == 0 else ((5, 6, 7), (0, 1, 3))
+        banks = ((5, 6), (7, 0))
 
         def ck(buf, c):
             return buf[:, 256 * c:256 * c + 256]
 
         def ga(c):
-            o = 128 * d + 16 * c
-            cp("a", WIN + [("offm", d, 0)], [("gb", c)], ck(T.gb, c), win.indirect(T.offm[:, o:o + 16]))
+            o = 128 * d + 64 + 16 * c
+            cp("a", WIN + [("offm", d, 64)], [("gb", c)], ck(T.gb, c), win.indirect(T.offm[:, o:o + 16]))
 
         def su(c):
-            o = 128 * d + 64 + 16 * c
-            tt(WIN + [("offm", d, 64), ("gb", c)], [("ss", c)], ck(T.ss, c), win.indirect(T.offm[:, o:o + 16]), ck(T.gb, c), A.add)
+            o = 128 * d + 16 * c
+            tt(WIN + [("offm", d, 0), ("gb", c)], [("ss", c)], ck(T.ss, c), win.indirect(T.offm[:, o:o + 16]), ck(T.gb, c), A.add)
 
         def hv(c):
             return (("hh", c), ck(T.hh, c)) if d == 0 else (4 + c, ps[4 + c][:, 0:256])
@@ -410,7 +424,7 @@ def rank_program(g, core, T, topo):
         def turn(a, b):
             cols = slice(256 * a, 256 * b)
             after("s", [("w", d + 1, b - 1)], [])
-            for t in DMA_SLOTS:
+            for t in DMA_SLOTS[d]:
                 oc = slice(t * M + 256 * a, t * M + 256 * b)
                 g.sync.dma_start(out[0:128 - 16 * t, oc], out[16 * t:128, cols]).then_inc(T.sem["rot%d" % d], 16)
                 g.sync.dma_start(out[128 - 16 * t:128, oc], out[0:16 * t, cols]).then_inc(T.sem["rot%d" % d], 16)
@@ -424,6 +438,11 @@ def rank_program(g, core, T, topo):
             if n < NPE:
                 t, b = PE_SLOTS[n], banks[h][n]
                 cp(q, [b], [("slot", d + 1, h, n)], out[:, t * M + 512 * h:t * M + 512 * h + 512], ps[b][:, :])
+
+        def across(h):
+            for a in (0, 64):
+                cp("a", [("w", d + 1, 2 * h), ("w", d + 1, 2 * h + 1)], [("slot", d + 1, h, NPE + a // 64)],
+                   out[a:a + 64, 4 * M + 512 * h:4 * M + 512 * h + 512], out[64 - a:128 - a, 512 * h:512 * h + 512])
 
         def own_next(h):
             src, keys = out[:, 512 * h:512 * h + 512], [("w", d + 1, 2 * h), ("w", d + 1, 2 * h + 1)]
@@ -445,45 +464,45 @@ def rank_program(g, core, T, topo):
                         turn(a, b)
                 if c < 2:
                     pe_turn(c)
-            if d == 2 and c < 2:
+            if d == 2 and c in FAR:
+                f = _far_senders(T, topo, rank)[FAR.index(c)]
                 after("g", [("w", 3, c)], [])
-                rid, pid, _ = topo.addr(far[c])
-                g.remote_dma(T.fh[:, :], ck(T.res, c), T.sem.fq, T.sem.ls, pid, rid, _bits(_half_engines(topo, core, far[c])))
-            if d == 2 and c >= 2:
+                rid, pid, _ = topo.addr(f)
+                g.remote_dma(T.fh[:, :], ck(T.res, c), T.sem.fq, T.sem.ls, pid, rid, _half_mask(topo, core, f)[0])
+            elif d == 2:
                 after("s", [("w", 3, c)], [])
-                b = (c - 2) * NG
-                g.sync.dma_start(T.fs[b:b + NG], ck(T.res, c)).then_inc(T.sem["fst%d" % (c - 2)], 16)
+                g.sync.dma_start(T.fs[c * NG:(c + 1) * NG], ck(T.res, c)).then_inc(T.sem["fst%d" % c], 16)
 
         if d != 1:
             ga(0); ga(1); su(0); su(1); ga(2); ha(0); su(2); ga(3); nw(0); ha(1); su(3); ha(2); nw(1); ha(3); nw(2); nw(3)
         if d == 0:
-            climb("a", 2, 2, 0, 52); on(S2[1], S3[1]); climb("v", 2, 2, 52, 64); pick(2, 2); pe_turn(2)
-            on(TL[1]); evac("a", 0, 0); evac("v", 0, 1); on(TL[1]); offsets(2, 2); on(H[2]); evac("a", 0, 2)
-            on(TL[1], H[2]); climb("v", 2, 3, 0, 12); on(TL[1], H[2]); climb("v", 2, 3, 12, 24); climb("a", 2, 3, 24, 64)
-            on(TL[1], S2[2]); pick(2, 3); pe_turn(3); own_next(0); own_next(1)
-            on(TL[1], S2[2], TL[1], PA[2]); offsets(2, 3); keep3(2); on(S2[2], PA[2])
-            evac("v", 1, 0); evac("a", 1, 1); evac("v", 1, 2); on(PA[2], S3[2], PA[2], S3[2])
+            climb("a", 2, 2, 0, 64); on(TL[1], S2[1], S3[1], PA[1], TL[1], S2[1], S3[1], PA[1])
+            pick(2, 2); pe_turn(2); pe_turn(3)
+            evac("v", 0, 0); evac("a", 0, 1); own_next(0); offsets(2, 2); on(H[2], TL[1], H[2])
+            climb("v", 2, 3, 0, 14); on(TL[1], H[2]); climb("v", 2, 3, 14, 28); climb("a", 2, 3, 28, 64); pick(2, 3)
+            on(TL[1]); own_next(1); evac("a", 1, 0); on(TL[1]); offsets(2, 3); keep3(2); on(TL[1]); evac("v", 1, 1)
+            both(2, 4, 24); pick(2, 4)
         if d == 1:
-            ga(0); ga(1); su(0); ga(2); su(1); ga(3); nw(0); su(2); nw(1); su(3); nw(2); nw(3)
-            climb("a", 2, 4, 0, 64); pick(2, 4); pe_turn(2); pe_turn(3)
-            on(S3[2]); evac("v", 0, 0); evac("a", 0, 1); own_next(0); own_next(1)
-            weave(TL[2], links((evac, "v", 0, 2)))
-            evac("a", 1, 0); evac("v", 1, 1); evac("a", 1, 2)
+            ga(0); ga(1); on(S2[2], S3[2], TL[2]); su(0); ga(2); su(1); ga(3); nw(0); su(2); nw(1); su(3); nw(2); nw(3)
+            across(0); pe_turn(2); pe_turn(3); evac("a", 0, 0)
+            on(S2[2], S3[2], TL[2], S2[2], S3[2], PA[2]); evac("v", 0, 1); across(1); own_next(0); own_next(1)
+            on(TL[2], PA[2], TL[2], PA[2]); evac("v", 1, 0); on(TL[2], PA[2]); evac("a", 1, 1); weave(TL[2])
         if d < 2:
-            ready = [("rot%d" % d, 16 * 2 * len(TURN_PIECES) * len(DMA_SLOTS))]
+            ready = [("rot%d" % d, 16 * 2 * len(TURN_PIECES) * len(DMA_SLOTS[d]))]
 
-    sent += sum(len(_half_engines(topo, core, f)) for f in far)
-    for c in (2, 3):
-        need("g", ("fst%d" % (c - 2), 16))
-        sent += _send_back(g, T, topo, core, rank, c, (c - 2) * NG)
+    for c in range(4):
+        if c in FAR:
+            sent += _half_mask(topo, core, _far_senders(T, topo, rank)[0])[1]
+        else:
+            need("g", ("fst%d" % c, 16))
+            sent += _send_back(g, T, topo, core, rank, c)
     g.sync.dma_start(T.y[16 * rank:16 * rank + 16, :], T.res[16 * rank:16 * rank + 16, :]).then_inc(T.sem.yo, 16)
     n_y = {"yo": 16, "ya": 0}
-    for c in range(4):
-        q, sem = ("a", "ya") if c < 2 else ("s", "yo")
-        need(q, ("fa%d" % c, NG - 1))
+    for c in Y_ORDER:
         cols = slice(256 * c, 256 * c + 256)
-        for a, b in ((0, rank), (rank + 1, NG)):
+        for q, sem, a, b in (("a", "ya", 0, rank), ("s", "yo", rank + 1, NG)):
             if b > a:
+                need(q, ("fa%d" % c, NG - 1))
                 Q[q].dma_start(T.y[16 * a:16 * b, cols], T.land[c * NG + a:c * NG + b]).then_inc(T.sem[sem], 16)
                 n_y[sem] += 16
     need("g", ("ls", sent), last("v"), last("a"), last("p"), last("g"), ("yo", n_y["yo"]), ("ya", n_y["ya"]))

@@ -3,36 +3,51 @@ from concourse.mybir import AluOpType as A, ActivationFunctionType as F
 
 P, M, NG = 8192, 1024, 8
 WW = P + 8
-NPE = 2
-IN = ((0, 320, None), (704, 864, 0), (864, 1024, 1), (320, 704, None))
+IN = ((0, 256, None), (704, 864, 0), (864, 1024, 1), (256, 704, None))
 IN_WRITES = ((0,), (3,), (1, 2))
-NIN = len(IN)
-PE_SLOTS = tuple(range(1, NPE + 1))
-DMA_SLOTS = ((3, 4, 5, 6, 7), (3, 5, 6, 7))
+PE_SLOTS = (1,)
+DMA_SLOTS = ((2, 3, 5, 6, 7), (2, 3, 6, 7))
+LATE = ((), (2,))
 TURN_PIECES = ((0, 1), (1, 4))
+CHUNKS = ((0, 256, 512, 704, M), (0, 256, 512, 768, M), (0, 256, 512, 768, M))
 FAR = (0, 1)
 Y_ORDER = (2, 0, 3, 1)
+CUTS = ((0, 32, 64), (0, 22, 44, 64), (0, 22, 44, 64))
+HALVES = (((0, 8),), ((0, 8),), ((0, 8),))
+STEPS = (("s0 s1 n0 s2 n1 s3 n2 n3", "g0 g1 g2 g3"), ("s0 s1 n0 s2 n1 s3 n2 n3", "g0 g1 g2 g3"),
+         ("s0 s1 s2 n0 s3 n1 n2 n3", "g0 g1 g2 h0 g3 h1 h2 h3"))
+
+CYC, PE_CYC, GATHER = 0.83e-3, 0.42e-3, 1.56
+WAKE = 0.22
+DMA_ISSUE, DMA_START, DMA_ROW, DMA_RATE = 0.06, 1.06, 0.012, 45e3
+ARRIVES = {"pcol": 0.13, "l16": 0.47, "iy": 0.87, "ib": 1.08, "ic": 1.25, "lo": 1.9, "hi": 1.5, "zr": 5.6,
+           "w0in2": 13.9, "ob0": 12.0, "ob1": 14.6, "ob2": 15.4}
+BACK_TAIL = (5.8, 5.3, 4.3, 4.0)
+ROUNDS, BIAS, FIRST, AHEAD, POLISH = 8, 0.05, 2.0, 0.5, 400
 
 SCRATCH = {}
 for _dt, _bufs in (
-        ("float32", dict(w0=WW, w1=WW, w2=WW, gb=M, ss=M, hh=M, res=M, cf=16, iy=160, ib=72, ck=32, one=256, zr=256,
-                         sl=64, z0=144, z1=144, ff=576, ee=576, tg=192, d0=768, d1=768, so=256, rep=M, fh=256)),
+        ("float32", dict(w0=WW, w1=WW, w2=WW, gb=M, ss=M, hh=M, res=M, ob=M, cf=16, iy=160, ib=72, ck=32, one=256, zr=256,
+                         zd=256, z0=144, z1=144, ff=576, ee=576, tg=192, d0=768, d1=768, so=768, rep=M, fh=256)),
         ("bfloat16", dict(tab=P + 16, xb=512, l16=128, l0=128, lt=2048, cand=9 * M, sb=72, zs=3 * 144, zc=6 * 144)),
-        ("int32", dict(xi=512, xt=512, pcol=4, ci=8, pi=576, z4=64, ri=128, zi=128)),
-        ("uint16", dict(off=576, offm=384, offs=64))):
+        ("int32", dict(xi=512, xt=512, pcol=4, ci=8, pi=576, z4=192, ri=256, zi=256)),
+        ("uint16", dict(off=576, offm=384))):
     for _n, _w in _bufs.items():
         SCRATCH[_n] = ("sbuf", [128, _w], _dt)
 for _h, (_a, _b, _via) in enumerate(IN):
     SCRATCH["stg%d" % _h] = ("dram", [NG, 128, (_b - _a) // 8], "float32")
     SCRATCH["piece%d" % _h] = ("dram", [128, (_b - _a) // 8], "float32")
+SCRATCH["od"] = SCRATCH["stg0"]
 SCRATCH["fs"] = ("dram", [32, 128, 32], "float32")
 SCRATCH["land"] = ("dram", [32, 128, 32], "float32")
 for _b in range(8):
     SCRATCH["ps%d" % _b] = ("psum", [128, 512], "float32")
 
-SEMAPHORES = (["sv", "sa", "sp", "sg", "ls", "hi_in", "lo_in", "w0in", "w0own", "rot0", "rot1", "fq", "vq", "yo", "ya"]
+SEMAPHORES = (["sv", "sa", "sp", "sg", "ls", "hi_in", "lo_in", "od", "w0own", "rot0", "rot1", "fq", "vq", "yo", "ya"]
               + [n + str(i) for n in ("fa", "fst") for i in range(4)]
-              + [n + str(i) for n in ("st", "pa", "pb") for i in range(NIN)])
+              + [n + str(i) for n in ("st", "pa", "pb") for i in range(len(IN))]
+              + [n + str(i) for n in ("w0in", "ob") for i in range(len(IN_WRITES))])
+_ORDER = []
 
 
 def _dst(topo, c):
@@ -52,11 +67,6 @@ def _helper_of(T, topo, grp, q):
 def _far_senders(T, topo, grp):
     rc = T.cores[grp]
     return [c for c in topo.cores_of(rc) if topo.die(c) != topo.die(rc) and all(topo.may_write(c, r) for r in T.cores)]
-
-
-def _half_mask(topo, src, dst):
-    es = topo.engines(src, dst)
-    return sum(1 << e for e in es[:len(es) // 2]), len(es) // 2
 
 
 def _send_in(g, T, topo, src, owner, h):
@@ -88,7 +98,7 @@ def helper_program(g, core, T, topo):
     rc = T.cores[grp]
     rid, pid, _ = topo.addr(rc)
     q = [r for r in _others(grp) if _helper_of(T, topo, grp, r) == core][0]
-    sent = 0
+    sent, every = 0, len(topo.engines(core, rc))
     far = _far_senders(T, topo, grp)
     for h, (a, b, via) in enumerate(IN):
         if via is not None and far[via] == core:
@@ -101,20 +111,121 @@ def helper_program(g, core, T, topo):
         for j in range(NG):
             qu = g.sync if j % 2 == 0 else g.scalar
             qu.dma_start(T.rep[16 * j:16 * j + 16, a:b], T["piece%d" % h][:]).then_inc(T.sem["pb%d" % h], 16)
-    for hs in IN_WRITES:
+    g.wait_ge(T.sem.pa0, 1)
+    g.remote_dma(T.od[q], T.piece0[:], T.sem.od, T.sem.ls, pid, rid, topo.mask(core, rc))
+    for n, hs in enumerate(IN_WRITES):
         a, b = IN[hs[0]][0], IN[hs[-1]][1]
         for h in hs:
             g.wait_ge(T.sem["pb%d" % h], 16 * NG)
-        g.remote_dma(T.w0[:, q * M + a:q * M + b], T.rep[:, a:b], T.sem.w0in, T.sem.ls, pid, rid, topo.mask(core, rc))
-        sent += len(topo.engines(core, rc))
-    far = far[:len(FAR)]
-    if core in far:
+        g.remote_dma(T.w0[:, q * M + a:q * M + b], T.rep[:, a:b], T.sem["w0in%d" % n], T.sem.ls, pid, rid, topo.mask(core, rc))
+    sent += every * (1 + len(IN_WRITES))
+    if core in far[:len(FAR)]:
         c = FAR[far.index(core)]
-        g.sync.wait_ge(T.sem.fq, _half_mask(topo, rc, core)[1])
+        g.sync.wait_ge(T.sem.fq, len(topo.engines(rc, core)))
         g.sync.dma_start(T.fs[c * NG:(c + 1) * NG], T.fh[:, :]).then_inc(T.sem.fst0, 16)
         g.wait_ge(T.sem.fst0, 16)
         sent += _send_back(g, T, topo, core, grp, c)
     g.wait_ge(T.sem.ls, sent)
+
+
+def issue_order(tasks, runs):
+    n = len(tasks)
+    pred, succ, wrote, read = [{} for _ in range(n)], [{} for _ in range(n)], {}, {}
+    for i, t in enumerate(tasks):
+        for a in [wrote[k] for k in t[1] + t[2] if k in wrote] + [a for k in t[2] for a in read.get(k, [])]:
+            if a != i:
+                pred[i][a] = 0.0 if tasks[a][0] == t[0] == "p" else DMA_START - tasks[a][4]["s"] if tasks[a][0] == "s" else WAKE
+        for k in t[1]:
+            read.setdefault(k, []).append(i)
+        for k in t[2]:
+            wrote[k], read[k] = i, []
+    for run in runs:
+        for a, b in zip(run, run[1:]):
+            pred[b].setdefault(a, 0.0)
+    for i in range(n):
+        for a, x in pred[i].items():
+            succ[a][i] = x
+    first = [max([ARRIVES.get(k, -WAKE) + WAKE for k in t[1]] + [0.0]) for t in tasks]
+    tail = [t[5] for t in tasks]
+    stage = [min([k[1] for k in t[2] if k[:1] == ("w",)] + [3]) for t in tasks]
+    value = [FIRST * (t[2][0][0] in ("own", "gv", "gb", "ss", "hh", "w", "rot")) for t in tasks]
+    for i in reversed(range(n)):
+        for a in pred[i]:
+            stage[a] = min(stage[a], stage[i])
+
+    def place(urgency, pred, first):
+        end, where, busy = {}, {}, {}
+        todo = sorted(range(n), key=lambda i: -urgency[i])
+        while todo:
+            i = next(i for i in todo if all(a in end for a in pred[i]))
+            todo.remove(i)
+            best = None
+            for q in tasks[i][0]:
+                s, d = max([first[i]] + [end[a] + x for a, x in pred[i].items()]), tasks[i][4][q]
+                for a, b in sorted(busy.get(q, []) + [(a - WAKE, b + WAKE) for k in tasks[i][3]
+                                                      for a, b, x in busy.get(k, []) if x != q]):
+                    if a < s + d - 1e-9 and b > s + 1e-9:
+                        s = b
+                if best is None or s + d < best[0] + BIAS:
+                    best = (s + d, s, q)
+            end[i], s, q = best
+            where[i] = (s, q)
+            busy.setdefault(q, []).append((s, end[i]))
+            for k in tasks[i][3]:
+                busy.setdefault(k, []).append((s, end[i], q))
+        return end, where
+
+    end, best = list(range(n)), None
+    for _ in range(ROUNDS):
+        back = place(end, succ, tail)[0]
+        end, where = place([back[i] - AHEAD * stage[i] + value[i] for i in range(n)], pred, first)
+        total = max(end[i] + tail[i] for i in range(n))
+        if best is None or total < best[0]:
+            best = (total, where)
+
+    def play(order, queue):
+        end, why, free, bank = [0.0] * n, [None] * n, {}, {}
+        for i in order:
+            q, s = queue[i], first[i]
+            for a, x in list(pred[i].items()) + ([(free[q], 0.0)] if q in free else []) + [
+                    (a, WAKE) for b in tasks[i][3] for y, a in bank.get(b, {}).items() if y != q]:
+                if end[a] + x > s:
+                    s, why[i] = end[a] + x, a
+            end[i], free[q] = s + tasks[i][4][q], i
+            for b in tasks[i][3]:
+                bank.setdefault(b, {})[q] = i
+        i, chain = max(range(n), key=lambda i: end[i] + tail[i]), []
+        total = end[i] + tail[i] + 0.05 * sum(end) / n
+        while why[i] is not None:
+            chain.append((why[i], i))
+            i = why[i]
+        return total, chain
+
+    order, queue = sorted(range(n), key=lambda i: best[1][i][0]), [best[1][i][1] for i in range(n)]
+    total, chain = play(order, queue)
+    kept, tried = (total, order, queue), []
+    for _ in range(POLISH):
+        moves = []
+        for a, i in chain:
+            if a not in pred[i] and (a, i) not in tried[-40:]:
+                pa, pi = order.index(a), order.index(i)
+                ahead, mid = {i}, order[pa:pi + 1]
+                for x in reversed(mid):
+                    if x in ahead:
+                        ahead.update(pred[x])
+                if a not in ahead:
+                    mid = [x for x in mid if x in ahead] + [x for x in mid if x not in ahead]
+                    moves.append(((a, i), order[:pa] + mid + order[pi + 1:], queue))
+                for x in (a, i):
+                    if len(tasks[x][0]) > 1:
+                        moves.append(((a, i), order, queue[:x] + [tasks[x][0].replace(queue[x], "")] + queue[x + 1:]))
+        if not moves:
+            break
+        (total, chain), key, order, queue = min(((play(o, q), k, o, q) for k, o, q in moves), key=lambda m: m[0][0])
+        tried += [key, key[::-1]]
+        if total < kept[0]:
+            kept = (total, order, queue)
+    return [(i, kept[2][i]) for i in kept[1] if tasks[i][0] != "d"]
 
 
 def rank_program(g, core, T, topo):
@@ -125,7 +236,8 @@ def rank_program(g, core, T, topo):
     SEM = {"v": "sv", "a": "sa", "p": "sp", "g": "sg"}
     cnt = {"v": 0, "a": 0, "p": 0, "g": 0}
     seen = {k: {} for k in Q}
-    wrote, read = {}, {}
+    wrote, read, held = {}, {}, {}
+    tasks, makes, runs = [], [], []
     V, S, PE = g.vector, g.scalar, g.tensor
     ps = [T["ps%d" % b] for b in range(8)]
     W = [T.w0, T.w1, T.w2]
@@ -140,363 +252,315 @@ def rank_program(g, core, T, topo):
     def last(q):
         return (SEM[q], cnt[q])
 
-    def after(q, r, w):
+    def call(q, r, w, banks, make):
+        old = [wrote[k] for k in r + w if k in wrote] + [t for k in w for t in read.get(k, {}).values()]
+        need(q, *[t for t in old if q != "p" or t[0] != SEM[q]])
+        need(q, *[t for b in banks for x, t in held.get(b, {}).items() if x != q])
+        done = make(q)
+        if not isinstance(done, tuple):
+            done.then_inc(T.sem[SEM[q]], 1)
+            cnt[q] += 1
+            done = last(q)
         for k in r:
-            if k in wrote:
-                need(q, wrote[k])
-            if isinstance(k, int):
-                need(q, *[t for t in read.get(k, {}).values() if t[0] != SEM.get(q)])
+            read.setdefault(k, {})[q] = done
         for k in w:
-            old = list(read.get(k, {}).values()) + ([wrote[k]] if k in wrote else [])
-            need(q, *[t for t in old if t[0] != SEM.get(q) or q != "p"])
+            wrote[k], read[k] = done, {}
+        for b in banks:
+            held.setdefault(b, {})[q] = done
 
-    def call(q, r, w, make):
-        after(q, r, w)
-        make().then_inc(T.sem[SEM[q]], 1)
-        cnt[q] += 1
-        for k in r:
-            read.setdefault(k, {})[q] = last(q)
-        for k in w:
-            wrote[k] = last(q)
-            read[k] = {}
-        return last(q)
+    def task(qs, r, w, banks, cycles, make, fixed=(0.01, 0.03)):
+        cost = {"v": max(64, cycles) * CYC + fixed[0], "a": max(64, cycles) * CYC + fixed[1], "p": cycles * PE_CYC}
+        tasks.append((qs, r, w, banks, {q: cost[q] for q in qs}, 0.0))
+        makes.append(make)
 
-    def ts(r, w, out, in0, s1, s2, op0, op1=None):
-        if op1 is None:
-            return call("v", r, w, lambda: V.tensor_scalar(out, in0, s1, None, op0))
-        return call("v", r, w, lambda: V.tensor_scalar(out, in0, s1, s2, op0, op1))
+    def dma(r, w, n, rows, row, make, tail=0.0):
+        tasks.append(("s", r, w, (), {"s": DMA_ISSUE * n}, 0.0))
+        tasks.append(("d", w, [("landed",) + w[0]], (), {"d": rows / 16 * (DMA_ROW + row / DMA_RATE)}, tail))
+        makes.extend([make, None])
 
-    def tt(r, w, out, in0, in1, op):
-        return call("v", r, w, lambda: V.tensor_tensor(out, in0, in1, op))
+    def size(ap):
+        return ap.shape[1]
 
-    def cp(q, r, w, out, in_, scale=None):
-        if q == "a":
-            return call(q, r, w, lambda: S.activation(out, in_, F.Copy, scale=1.0 if scale is None else scale))
-        if scale is None:
-            return call(q, r, w, lambda: V.tensor_copy(out, in_))
-        return ts(r, w, out, in_, scale, None, A.mult)
+    def ts(r, w, out, in0, s1, s2, op0, op1=None, banks=()):
+        args = (out, in0, s1, None, op0) if op1 is None else (out, in0, s1, s2, op0, op1)
+        task("v", r, w, banks, size(out), lambda q: V.tensor_scalar(*args))
+
+    def tt(r, w, out, in0, in1, op, banks=()):
+        task("v", r, w, banks, size(out) * (1 if banks else 2), lambda q: V.tensor_tensor(out, in0, in1, op))
+
+    def cp(qs, r, w, out, in_, scale=None, banks=(), gather=False):
+        def make(q):
+            if q == "a":
+                return S.activation(out, in_, F.Copy, scale=1.0 if scale is None else scale)
+            return V.tensor_copy(out, in_) if scale is None else V.tensor_scalar(out, in_, scale, None, A.mult)
+        task(qs, r, w, banks, size(out) * (GATHER if gather else 1), make, (0.05, 0.065) if gather else (0.01, 0.03))
+
+    def fill(w, out, x):
+        task("v", [], w, (), size(out), lambda q: V.memset(out, x))
 
     def iota(w, out, pat, cm, base=0):
-        return call("g", [], w, lambda: g.iota(out, pat, base, cm, allow_small_or_imprecise_dtypes=True))
+        call("g", [], w, (), lambda q: g.iota(out, pat, base, cm, allow_small_or_imprecise_dtypes=True))
 
-    def mms(r, w, calls):
-        def make():
+    def mms(r, w, bank, calls, passes=1):
+        def make(q):
             for c in calls[:-1]:
                 PE.matmul(*c)
             return PE.matmul(*calls[-1])
-        return call("p", r, w, make)
+        task("p", r, w, (bank,), passes * sum(max(64, size(c[0])) for c in calls), make)
 
-    def weave(*chains):
-        chains = list(chains)
-        while chains:
-            chains = [c for c in chains if next(c, False)]
-
-    def links(*calls):
-        for c in calls:
-            c[0](*c[1:])
-            yield True
-
+    mine = slice(16 * rank, 16 * rank + 16)
     S.dma_start(T.xi[0:48, :], T.tree[rank]).then_inc(T.sem.hi_in, 16)
     S.dma_start(T.xi[48:64, :], T.tree[rank, 0:P]).then_inc(T.sem.hi_in, 16)
-    g.sync.dma_start(T.xi[64:112, :], T.tree[rank]).then_inc(T.sem.lo_in, 16)
+    S.dma_start(T.xi[64:112, :], T.tree[rank]).then_inc(T.sem.lo_in, 16)
     for h, (a, b, via) in enumerate(IN):
         g.sync.dma_start(T["stg%d" % h][:], T.v[:, a:b]).then_inc(T.sem["st%d" % h], 16)
     for j in range(NG):
-        g.sync.dma_start(T.w0[16 * j:16 * j + 16, rank * M:(rank + 1) * M],
-                         T.v[16 * rank:16 * rank + 16, :]).then_inc(T.sem.w0own, 16)
+        g.sync.dma_start(T.w0[16 * j:16 * j + 16, rank * M:(rank + 1) * M], T.v[mine, :]).then_inc(T.sem.w0own, 16)
+    g.sync.dma_start(T.ob[mine, :], T.v[mine, :]).then_inc(T.sem.ob0, 16)
+    engines = sum(len(topo.engines(_helper_of(T, topo, rank, q), core)) for q in _others(rank))
+    wrote.update(hi=("hi_in", 32), lo=("lo_in", 16), w0own=("w0own", 16 * NG))
+    for n, hs in enumerate(IN_WRITES):
+        a, b = IN[hs[0]][0], IN[hs[-1]][1]
+        wrote["w0in%d" % n] = ("w0in%d" % n, engines)
+        if n == 0:
+            need("s", ("od", engines))
+            parts = [(T.ob[16 * x:16 * y, a:b], T.od[x:y]) for x, y in ((0, rank), (rank + 1, NG)) if y > x]
+        else:
+            need("s", wrote["w0in%d" % n])
+            parts = [(T.ob[16 * j:16 * j + 16, a:b], T.w0[16 * j:16 * j + 16, j * M + a:j * M + b]) for j in _others(rank)]
+        for out, src in parts:
+            g.sync.dma_start(out, src).then_inc(T.sem["ob%d" % n], 16)
+        wrote["ob%d" % n] = ("ob%d" % n, 16 * (len(parts) + (n == 0)))
 
-    call("g", [], ["pcol"], lambda: g.iota(T.pcol[:, 0:1], [[0, 1]], 0, 1))
+    call("g", [], ["pcol"], (), lambda q: g.iota(T.pcol[:, 0:1], [[0, 1]], 0, 1))
     iota(["l16"], T.l16[:, :], [[0, 8], [16, 16]], 0)
     iota(["iy"], T.iy[:, :], [[1, 160]], 0, -16)
     iota(["ib"], T.ib[:, 0:48], [[16, 3], [1, 2], [2, 8]], 0)
     iota(["ic"], T.ib[:, 48:72], [[1, 3], [16, 8]], 0)
-    sent = 0
+    sent = [0]
     for h, (a, b, via) in enumerate(IN):
         need("g", ("st%d" % h, 16))
         if via is None:
-            sent += _send_in(g, T, topo, core, rank, h)
+            sent[0] += _send_in(g, T, topo, core, rank, h)
         else:
             f = _far_senders(T, topo, rank)[via]
             g.remote_dma_fused([RemoteDMATransfer(dst_ids=[_dst(topo, f)], dma_engine_mask=1 << topo.engines(core, f)[-1 - n],
                                                   remote_sem=T.sem.vq, src=T["stg%d" % h][grp], dst=T["stg%d" % h][grp])
                                 for n, grp in enumerate(_others(rank))], local_sem=T.sem.ls)
-            sent += NG - 1
+            sent[0] += NG - 1
     iota(["one"], T.one[:, :], [[0, 256]], 0, 1)
-    iota(["sl"], T.sl[:, :], [[16, 64]], 1)
-    call("g", ["one"], ["zr"],
-         lambda: g.affine_select(T.zr[:, :], T.one[:, :], [[0, 2], [1, 128]], A.is_equal, 0.0, 0, -1))
+    call("g", ["one"], ["zr"], (),
+         lambda q: g.affine_select(T.zr[:, :], T.one[:, :], [[0, 2], [1, 128]], A.is_equal, 0.0, 0, -1))
 
     MASKS = (112, 15, 14, 49, 3, 63, 115)
-    call("v", [], ["wt"], lambda: V.memset(cf[0:64, 7:8], 64.0))
-    call("v", [], ["wt2"], lambda: V.memset(cf[64:128, 7:8], 0.5))
-    call("v", [], [("d0", d, 0) for d in range(3)], lambda: V.memset(T.d0[:, 0::4], 0.0))
+    fill(["wt"], cf[0:64, 7:8], 64.0)
+    fill(["wt2"], cf[64:128, 7:8], 0.5)
+    fill([("d0", d, 0) for d in range(3)], T.d0[:, 0::4], 0.0)
+    fill([("d1", d, 0) for d in range(3)], T.d1[:, 1::4], 0.0)
+    for d in range(3):
+        fill([("zero", d)], W[d][:, P:WW], 0.0)
     for n, x in enumerate(MASKS):
         ts(["pcol"], [("ci", n)], T.ci[:, n:n + 1], T.pcol[:, 0:1], x, None, A.bitwise_and)
-    call("v", [], [("d1", d, 0) for d in range(3)], lambda: V.memset(T.d1[:, 1::4], 0.0))
-    cp("v", [("ci", 6)], ["cf"], cf[:, 0:7], T.ci[:, 0:7])
-    for d in range(3):
-        call("v", [], [("zero", d)], lambda: V.memset(W[d][:, P:WW], 0.0))
+    cp("v", [("ci", n) for n in range(7)], ["cf"], cf[:, 0:7], T.ci[:, 0:7])
     ts(["cf", "l16"], ["l0"], T.l0[:, :], T.l16[:, :], cf[:, 0:1], None, A.is_equal)
-    ts(["iy"], ["ck"], T.ck[:, 0:16], T.iy[:, 16:32], cf[:, 1:2], None, A.is_equal)
-
-    def spreading(q, k):
-        cp(q, ["l0", "ck"], [("lt", k)], T.lt[:, k * 128:k * 128 + 128], T.l0[:, :], T.ck[:, k:k + 1])
-
-    for k in range(8):
-        spreading("a", k)
-    ts(["ib"], ["cz"], T.ck[:, 16:22], T.ib[:, 0:48:8], cf[:, 3:4], None, A.is_equal)
-    ts([], ["z0"], T.z0[:, :], T.iy[:, 0:144], 0.125, cf[:, 2:3], A.mult, A.is_equal)
-
-    need("v", ("lo_in", 16))
-    ts([], ["xl"], T.xt[64:112, :], T.xi[64:112, :], 127, None, A.bitwise_and)
-    need("v", ("hi_in", 32))
-    ts([], ["xt"], T.xt[0:64, :], T.xi[0:64, :], 7, None, A.arith_shift_right)
-    ts([], ["cs"], T.ck[:, 22:25], T.iy[:, 16:19], cf[:, 4:5], None, A.is_equal)
-    ts([], ["z1"], T.z1[:, :], T.iy[:, 0:144], cf[:, 0:1], None, A.is_equal)
-    cp("v", ["xt", "xl"], ["xb"], T.xb[0:112, :], T.xt[0:112, :], cf[0:112, 7:8])
-    ts([], ["sb"], T.sb[:, 0:48], T.ib[:, 0:48], cf[:, 5:6], None, A.is_equal)
-    for k in range(8, 16):
-        spreading("v", k)
-    ts(["ic"], ["sn"], T.sb[:, 48:72], T.ib[:, 48:72], cf[:, 6:7], None, A.is_equal)
-    ts([], [("tab", 16)], T.tab[:, P:P + 1], cf[:, 1:2], 3.0, float(P), A.is_lt, A.mult)
-    for n in range(6):
-        cp("a", ["z0", "cz"], [("zc", n)], T.zc[:, n * 144:n * 144 + 144], T.z0[:, :], T.ck[:, 16 + n:17 + n])
-
-    def shifted(d):
-        cp("a", ["z1", "cs"], [("zs", d)], T.zs[:, d * 144:d * 144 + 144], T.z1[:, :], T.ck[:, 22 + d:23 + d])
-
-    def cross(b):
-        return 2 * (b % 4) + b // 4
-
+    ts(["cf", "iy"], ["ck"], T.ck[:, 0:16], T.iy[:, 16:32], cf[:, 1:2], None, A.is_equal)
+    ts(["cf", "ib"], ["cz"], T.ck[:, 16:22], T.ib[:, 0:48:8], cf[:, 3:4], None, A.is_equal)
+    ts(["cf", "iy"], ["cs"], T.ck[:, 22:25], T.iy[:, 16:19], cf[:, 4:5], None, A.is_equal)
+    ts(["cf", "iy"], ["z0"], T.z0[:, :], T.iy[:, 0:144], 0.125, cf[:, 2:3], A.mult, A.is_equal)
+    ts(["cf", "iy"], ["z1"], T.z1[:, :], T.iy[:, 0:144], cf[:, 0:1], None, A.is_equal)
+    ts(["cf", "ib"], ["sb"], T.sb[:, 0:48], T.ib[:, 0:48], cf[:, 5:6], None, A.is_equal)
+    ts(["cf", "ic"], ["sn"], T.sb[:, 48:72], T.ib[:, 48:72], cf[:, 6:7], None, A.is_equal)
+    ts(["cf"], ["none"], T.tab[:, P:P + 1], cf[:, 1:2], 3.0, float(P), A.is_lt, A.mult)
+    ts(["cf"], ["c8"], cf[:, 8:9], cf[:, 0:1], -M / 16.0, float(2 * P), A.mult, A.add)
     for k in range(16):
-        b = (4, 5, 0, 1, 2, 6, 7)[k % 7]
-        mms(["xb", ("lt", k)], [b], [(ps[b][:, :], T.lt[0:112, k * 128:k * 128 + 128], T.xb[0:112, :], True, True)])
-        cp("va"[k % 2], [b], [("tab", k)], T.tab[:, k * 512:k * 512 + 512], ps[b][:, :])
-        if k == 6:
-            mms(["xb", "sb"], [3], [(ps[3][:, 64 * d + 16 * b:64 * d + 16 * b + 16], T.xb[0:112, 128 * b:128 * b + 128],
-                                     T.sb[0:112, 16 * d:16 * d + 16], True, True) for d in range(3) for b in range(4)])
-        if k == 10:
-            ts([3], [("off", d, 1) for d in range(3)], T.off[:, 0:192], ps[3][:, 0:192], -0.25, None, A.add)
-    TAB = [("tab", k) for k in range(17)]
+        task("va", ["l0", "ck"], [("lt", k)], (), 64, lambda q, k=k: (
+            S.activation(T.lt[:, k * 128:k * 128 + 128], T.l0[:, :], F.Copy, scale=T.ck[:, k:k + 1]) if q == "a" else
+            V.tensor_scalar(T.lt[:, k * 128:k * 128 + 128], T.l0[:, :], T.ck[:, k:k + 1], None, A.mult)), (0.01, 0.085))
+    for n in range(6):
+        cp("va", ["z0", "cz"], [("zc", n)], T.zc[:, n * 144:n * 144 + 144], T.z0[:, :], T.ck[:, 16 + n:17 + n])
+    for d in range(3):
+        cp("va", ["z1", "cs"], [("zs", d)], T.zs[:, d * 144:d * 144 + 144], T.z1[:, :], T.ck[:, 22 + d:23 + d])
+    for n, x in enumerate((-2.0, 0.25)):
+        cp("va", ["zr"], [("zd", n)], T.zd[:, 128 * n:128 * n + 128], T.zr[:, 0:128], x)
 
-    def own_codes(d, h):
-        z = (2 * d + h) * 144
-        mms(["xb", ("zc", 2 * d + h)], [d], [(ps[d][:, 32 * h:32 * h + 32], T.zc[0:112, z + 16 - i:z + 144 - i],
-                                              T.xb[0:112, i::16], i == 0, i == 15) for i in range(16)])
+    ts(["lo"], ["xl"], T.xt[64:112, :], T.xi[64:112, :], 127, None, A.bitwise_and)
+    ts(["hi"], ["xt"], T.xt[0:64, :], T.xi[0:64, :], 7, None, A.arith_shift_right)
+    cp("v", ["xt", "xl", "wt", "wt2"], ["xb"], T.xb[0:112, :], T.xt[0:112, :], cf[0:112, 7:8])
 
-    def bank4(d):
-        return d or 3
-
-    def cand(d, k):
-        return (3 * d + k - 2) * M
-
-    def climb(q, d, k, a, b):
-        c, o = cand(d, k), 192 * (k - 2) + 64 * d
-        cp(q, [("off", d, k - 1)] + TAB, [("cand", d, k, q, a)], T.cand[:, c + 16 * a:c + 16 * b],
-           T.tab[:, 0:P + 1].indirect(T.off[:, o + a:o + b]))
-
-    def both(d, k, nv):
-        climb("v", d, k, 0, nv)
-        climb("a", d, k, nv, 64)
-
-    def climbed(d, k):
-        return [key for key in wrote if isinstance(key, tuple) and key[:3] == ("cand", d, k)]
-
-    def pick(d, k):
-        c, bank = cand(d, k), bank4(d) if k == 4 else d
-        calls = []
-        for b in range(8):
-            src, dst = (b, 256 + 8 * cross(b)) if k == 3 else (cross(b), 64 * (k - 1) + 8 * b)
-            calls.append((ps[bank][:, dst:dst + 8], T.cand[:, c + 128 * src:c + 128 * src + 128],
-                          T.sb[:, 48 + 8 * d:56 + 8 * d], True, True))
-        mms(climbed(d, k) + ["sn"], [bank], calls)
-
-    def offsets(d, k):
-        c, o = (64 if k == 2 else 256), 192 * (k - 1) + 64 * d
-        ts([d], [("off", d, k)], T.off[:, o:o + 64], ps[d][:, c:c + 64], -0.25, None, A.add)
-
-    def keep3(d):
-        c = cand(d, 3)
-        mms(climbed(d, 3) + [("zs", d)], [d],
-            [(ps[d][:, 128:192], T.zs[:, d * 144 + 16 - i:d * 144 + 144 - i], T.cand[:, c + i:c + M:16], i == 0, i == 15)
-             for i in range(16)])
+    TABLE_BANKS = (4, 5, 0, 1, 2, 6, 7)
+    for k in range(16):
+        b = TABLE_BANKS[k % 7]
+        mms(["xb", ("lt", k)], [("sp", b)], b,
+            [(ps[b][:, :], T.lt[0:112, k * 128:k * 128 + 128], T.xb[0:112, :], True, True)])
+        cp("va", [("sp", b)], [("tab", k)], T.tab[:, k * 512:k * 512 + 512], ps[b][:, :], banks=(b,))
+    TAB = [("tab", k) for k in range(16)] + ["none"]
 
     def address(d, a, src, key):
         o = T.offm[:, 128 * d + a:128 * d + a + 64]
         if d == 0:
-            ts([key], [("offm", d, a)], o, src, float(P), None, A.add)
-            return
-        ri, zi = T.ri[:, a:a + 64], T.zi[:, a:a + 64]
-        ts([key, "c8"], [("ri", a)], ri, src, cf[:, 8:9], None, A.add)
-        ts([key], [("zi", a)], zi, src, 0.0, float(P), A.is_ge, A.mult)
-        yield True
-        ts([("ri", a)], [("ri", a)], ri, ri, P - 1, None, A.bitwise_and)
-        yield True
-        tt([("ri", a), ("zi", a)], [("ri", a)], ri, ri, zi, A.max)
-        yield True
-        cp("v", [("ri", a)], [("offm", d, a)], o, ri)
-
-    def head(d):
-        c = slice(192 * d, 192 * d + 64)
-        ts([d], [("pi", d, 1)], T.pi[:, c], ps[d][:, 0:64], -0.25 - P, None, A.add)
-        yield True
-        tt([d, ("pi", d, 1)], [("ff", d, 1)], T.ff[:, c], ps[d][:, 0:64], T.pi[:, c], A.subtract)
-        yield True
-        ts([("ff", d, 1)], [("tg", d)], T.tg[:, 64 * d:64 * d + 64], T.ff[:, c], -1.0, 2 * P + 0.5, A.mult, A.add)
-
-    def parent(d):
-        yield from address(d, 64, T.pi[:, 192 * d:192 * d + 64], ("pi", d, 1))
-
-    def side(d, k):
-        c, e = slice(192 * d + 64 * k - 64, 192 * d + 64 * k), slice(256 * d + 5 - k, 256 * d + 256, 4)
-        tg, src = T.tg[:, 64 * d:64 * d + 64], ps[d][:, 64 * k - 64:64 * k]
-        tt([d, ("tg", d)], [("ff", d, k)], T.ff[:, c], src, tg, A.subtract)
-        tt([d, ("tg", d)], [("pi", d, k)], T.pi[:, c], src, tg, A.subtract)
-        yield True
-        tt([("pi", d, k), ("ff", d, k)], [("ee", d, k)], T.ee[:, c], T.ff[:, c], T.pi[:, c], A.is_equal)
-        tt([("pi", d, k), ("ff", d, k)], [("d0", d, k)], T.d0[:, e], T.ff[:, c], T.pi[:, c], A.not_equal)
-        yield True
-        tt([("ee", d, k), ("ff", d, k)], [("d1", d, k)], T.d1[:, e], T.ff[:, c], T.ee[:, c], A.mult)
-
-    def tail(d):
-        tg, z, b = T.tg[:, 64 * d:64 * d + 64], 256 * d, bank4(d)
-        tt([b, ("tg", d)], [("d1", d, 0)], T.d1[:, z:z + 256:4], ps[b][:, 192:256], tg, A.subtract)
-        tt([b, ("tg", d)], ["z4"], T.z4[:, :], ps[b][:, 192:256], tg, A.subtract)
-        yield True
-        tt(["z4", ("d1", d, 0)], [("d0", d, 0)], T.d0[:, z + 1:z + 256:4], T.d1[:, z:z + 256:4], T.z4[:, :], A.is_equal)
-        yield True
-        call("v", [(n, d, k) for n in ("d0", "d1") for k in (0, 2, 3)], ["so"],
-             lambda: V.tensor_tensor_scan(T.so[:, :], T.d0[:, z:z + 256], T.d1[:, z:z + 256], 0.0, A.mult, A.add))
-        yield True
-        yield from address(d, 0, T.so[:, 3::4], "so")
-
-    def on(*chains):
-        for c in chains:
-            next(c, False)
-
-    def constants():
-        ts([], ["c8"], cf[:, 8:9], cf[:, 0:1], -M / 16.0, float(2 * P), A.mult, A.add)
-        ts([], ["c9"], cf[:, 9:10], cf[:, 0:1], M / 16.0 - 1, None, A.mult)
-
-    H, PA, S2, S3, TL = ([f(d) for d in range(3)] for f in (head, parent, lambda d: side(d, 2), lambda d: side(d, 3), tail))
-    own_codes(0, 0); own_codes(0, 1)
-    both(0, 2, 32); pick(0, 2); own_codes(1, 0)
-    both(1, 2, 28); offsets(0, 2); on(H[0]); pick(1, 2); constants(); on(H[0]); shifted(0)
-    both(0, 3, 32); pick(0, 3); offsets(1, 2); own_codes(1, 1); on(H[0], PA[0]); shifted(1)
-    climb("v", 1, 3, 0, 20); offsets(0, 3); on(S2[0]); keep3(0); climb("v", 1, 3, 20, 26); climb("a", 1, 3, 26, 64); pick(1, 3)
-    both(0, 4, 30); pick(0, 4)
-    offsets(1, 3); on(S3[0], S2[0]); keep3(1); shifted(2); climb("a", 1, 4, 0, 64)
-    on(S3[0], S2[0], TL[0], S3[0], H[1])
-    ts(["sl", "c9"], ["offs"], T.offs[:, :], T.sl[:, :], cf[:, 9:10], None, A.add)
-    on(TL[0], H[1], PA[1], TL[0], H[1], PA[1], TL[0], S2[1], S3[1])
-    pick(1, 4); own_codes(2, 0); own_codes(2, 1)
-
-    ready = [("w0in", len(IN_WRITES) * sum(len(topo.engines(_helper_of(T, topo, rank, q), core)) for q in _others(rank))),
-             ("w0own", 16 * NG)]
+            return ts([key], [("offm", d, a)], o, src, float(P), None, A.add)
+        c = slice(128 * d + a - 128, 128 * d + a - 64)
+        ri, zi, k = T.ri[:, c], T.zi[:, c], ("ri", d, a)
+        ts([key, "c8"], [k], ri, src, cf[:, 8:9], None, A.add)
+        ts([key], [("zi", d, a)], zi, src, 0.0, float(P), A.is_ge, A.mult)
+        ts([k], [k], ri, ri, P - 1, None, A.bitwise_and)
+        tt([k, ("zi", d, a)], [k], ri, ri, zi, A.max)
+        cp("v", [k], [("offm", d, a)], o, ri)
 
     for d in range(3):
-        w = W[d]
+        parts = HALVES[d]
+        mms(["xb", "sb"], [("x", d, 1)], 3,
+            [(ps[3][:, 64 * d + 32 * h + 8 * b:64 * d + 32 * h + 8 * b + 8], T.xb[0:112, 128 * b:128 * b + 128],
+              T.sb[0:112, 16 * d + 8 * h:16 * d + 8 * h + 8], True, True) for h in range(2) for b in range(4)])
+        ts([("x", d, 1)], [("off", d, 1, a) for a, b in parts], T.off[:, 64 * d:64 * d + 64], ps[3][:, 64 * d:64 * d + 64],
+           -0.25, None, A.add, banks=(3,))
+        for h in range(2):
+            z = (2 * d + h) * 144
+            mms(["xb", ("zc", 2 * d + h), ("tab", 13)], [("c", d, 1, h)], 7,
+                [(ps[7][:, 64 * d + 32 * h:64 * d + 32 * h + 32], T.zc[0:112, z + 16 - i:z + 144 - i], T.xb[0:112, i::16],
+                  i == 0, i == 15) for i in range(16)])
+        for k in (2, 3, 4):
+            c, o = (3 * d + k - 2) * M, 192 * (k - 2) + 64 * d
+            bank, at = (d or (0, 6, 3)[k - 2]), (256 if k == 3 else 192 if k == 4 else 64)
+            for a, b in parts:
+                cuts = [x for x in CUTS[d] if 8 * a <= x <= 8 * b]
+                for x, y in zip(cuts, cuts[1:]):
+                    cp("va", [("off", d, k - 1, a)] + TAB, [("cand", d, k, x)], T.cand[:, c + 16 * x:c + 16 * y],
+                       T.tab[:, 0:P + 1].indirect(T.off[:, o + x:o + y]), gather=True)
+                mms([("cand", d, k, x) for x in cuts[:-1]] + ["sn"], [("x" if k == 3 else "c", d, k, a)], bank,
+                    [(ps[bank][:, at + 8 * n:at + 8 * n + 8], T.cand[:, c + 128 * n:c + 128 * n + 128],
+                      T.sb[:, 48 + 8 * d:56 + 8 * d], True, True) for n in range(a, b)])
+                if k < 4:
+                    ts([("x" if k == 3 else "c", d, k, a)], [("off", d, k, a)], T.off[:, o + 192 + 8 * a:o + 192 + 8 * b],
+                       ps[bank][:, at + 8 * a:at + 8 * b], -0.25, None, A.add, banks=(bank,))
+            if k == 3:
+                mms([("cand", d, 3, x) for x in CUTS[d][:-1]] + [("zs", d)], [("c", d, 3, a) for a, b in parts], d,
+                    [(ps[d][:, 128:192], T.zs[:, d * 144 + 16 - i:d * 144 + 144 - i], T.cand[:, c + i:c + M:16], i == 0,
+                      i == 15) for i in range(16)])
+        c, tg, z = slice(192 * d, 192 * d + 64), T.tg[:, 64 * d:64 * d + 64], 256 * d
+        own = [("c", d, 1, 0), ("c", d, 1, 1)]
+        ts(own, [("pi", d, 1)], T.pi[:, c], ps[7][:, 64 * d:64 * d + 64], -0.25 - P, None, A.add, banks=(7,))
+        tt(own + [("pi", d, 1)], [("ff", d, 1)], T.ff[:, c], ps[7][:, 64 * d:64 * d + 64], T.pi[:, c], A.subtract, banks=(7,))
+        ts([("ff", d, 1)], [("tg", d)], tg, T.ff[:, c], -1.0, 2 * P + 0.5, A.mult, A.add)
+        address(d, 64, T.pi[:, c], ("pi", d, 1))
+        for k in (2, 3):
+            c, e = slice(192 * d + 64 * k - 64, 192 * d + 64 * k), slice(z + 5 - k, z + 256, 4)
+            r = [("c", d, k, a) for a, b in parts] + [("tg", d)]
+            tt(r, [("ff", d, k)], T.ff[:, c], ps[d][:, 64 * k - 64:64 * k], tg, A.subtract, banks=(d,))
+            tt(r, [("pi", d, k)], T.pi[:, c], ps[d][:, 64 * k - 64:64 * k], tg, A.subtract, banks=(d,))
+            tt([("pi", d, k), ("ff", d, k)], [("ee", d, k)], T.ee[:, c], T.ff[:, c], T.pi[:, c], A.is_equal)
+            ts([("ee", d, k)], [("d0", d, k)], T.d0[:, e], T.ee[:, c], -1.0, 1.0, A.mult, A.add)
+            tt([("ee", d, k), ("ff", d, k)], [("d1", d, k)], T.d1[:, e], T.ff[:, c], T.ee[:, c], A.mult)
+        r, z4 = [("c", d, 4, a) for a, b in parts] + [("tg", d)], T.z4[:, 64 * d:64 * d + 64]
+        tt(r, [("d1", d, 4)], T.d1[:, z:z + 256:4], ps[d or 3][:, 192:256], tg, A.subtract, banks=(d or 3,))
+        tt(r, [("z4", d)], z4, ps[d or 3][:, 192:256], tg, A.subtract, banks=(d or 3,))
+        tt([("z4", d), ("d1", d, 4)], [("d0", d, 4)], T.d0[:, z + 1:z + 256:4], T.d1[:, z:z + 256:4], z4, A.is_equal)
+        task("v", [(n, d, k) for n in ("d0", "d1") for k in (0, 2, 3, 4)], [("so", d)], (), 256, lambda q, z=z:
+             V.tensor_tensor_scan(T.so[:, z:z + 256], T.d0[:, z:z + 256], T.d1[:, z:z + 256], 0.0, A.mult, A.add))
+        address(d, 0, T.so[:, z + 3:z + 256:4], ("so", d))
+
+    WIN = ["w0own"] + ["w0in%d" % n for n in range(len(IN_WRITES))]
+    for d in range(3):
         out = W[d + 1] if d < 2 else T.res
-        win = w[:, 0:P + 1]
-        need("v", *ready)
-        need("a", *ready)
-        WIN = [("zero", d)] + ([("w", d, c) for c in range(4)] + [("slot", d, h, n) for h in range(2) for n in range(NPE + 2)]
-                               if d else [])
-        banks = ((5, 6), (7, 0))
+        win = W[d][:, 0:P + 1]
+        WIN = WIN + [("zero", d)]
+        cut = CHUNKS[d]
 
-        def ck(buf, c):
-            return buf[:, 256 * c:256 * c + 256]
+        def ck(buf, c, cut=cut):
+            return buf[:, cut[c]:cut[c + 1]]
 
-        def ga(c):
-            o = 128 * d + 64 + 16 * c
-            cp("a", WIN + [("offm", d, 64)], [("gb", c)], ck(T.gb, c), win.indirect(T.offm[:, o:o + 16]))
+        def half(b, c, cut=cut):
+            return ps[b][:, cut[c] - 512 * (c // 2):cut[c + 1] - 512 * (c // 2)]
 
-        def su(c):
-            o = 128 * d + 16 * c
-            tt(WIN + [("offm", d, 0), ("gb", c)], [("ss", c)], ck(T.ss, c), win.indirect(T.offm[:, o:o + 16]), ck(T.gb, c), A.add)
+        for c in range(4):
+            b = 4 - c // 2
+            had = [(("w", d, n), CHUNKS[d - 1][n:n + 2]) for n in range(4)] if d else [
+                ("ob%d" % n, (IN[hs[0]][0], IN[hs[-1]][1])) for n, hs in enumerate(IN_WRITES)]
+            src = [k for k, (x, y) in had if x < cut[c + 1] and y > cut[c]] + ([] if d else ["ob0"])
+            old = ([("c", 0, 4, a) for a, _ in HALVES[0]] + [("x", x, 1) for x in range(3)] if b == 3 else [("sp", b)])
+            mms(src + [("zd", d // 2)], [("own", c)] + (old if d == 0 else []), b,
+                [(half(b, c), T.zd[:, 128 * (d // 2):128 * (d // 2) + 128], ck(W[d] if d else T.ob, c), True, True)], 4)
+        runs += [[i, len(tasks) - 4] for i, t in enumerate(tasks) if t[2][0][0] == "turn"]
+        runs.append(list(range(len(tasks) - 4, len(tasks))))
+        cp("v", WIN + [("offm", d, 64)], [("gv", 0)], T.gb[:, 0:128], win.indirect(T.offm[:, 128 * d + 64:128 * d + 72]),
+           gather=True)
+        name = {x + str(c): len(tasks) + (3 + d // 2) * c + n for c in range(4) for n, x in enumerate("gshn" if d == 2 else "gsn")}
+        runs += [[name[x] for x in r.split()] for r in STEPS[d]]
+        for c in range(4):
+            x, y, b, e = 128 * d + cut[c] // 16, 128 * d + cut[c + 1] // 16, 4 - c // 2, 0 if c else 8
+            cp("a", WIN + [("offm", d, 64)], [("gb", c)], T.gb[:, cut[c] + 16 * e:cut[c + 1]],
+               win.indirect(T.offm[:, x + 64 + e:y + 64]), gather=True)
+            args = (ck(T.ss, c), win.indirect(T.offm[:, x:y]), ck(T.gb, c), A.add)
+            task("v", WIN + [("offm", d, 0), ("gb", c), ("gv", c)], [("ss", c)], (), 16 * (y - x) * GATHER,
+                 lambda q, args=args: V.tensor_tensor(*args), (0.05, 0))
+            if d == 2:
+                cp("a", [("ss", c)], [("hh", c)], ck(T.hh, c), ck(T.ss, c), -0.125)
+            tt([("hh" if d == 2 else "ss", c), ("own", c)], [("w", d + 1, c)], ck(out, c), ck(T.hh if d == 2 else T.ss, c),
+               half(b, c), A.add, banks=(b,))
+        if d == 2:
+            break
+        new = [("w", d + 1, c) for c in range(4)]
+        WIN = list(new)
+        n_rot = [0]
+        for a, b in TURN_PIECES:
+            slots = [t for t in DMA_SLOTS[d] if a == 0 or t not in LATE[d]]
 
-        def hv(c):
-            return (("hh", c), ck(T.hh, c)) if d == 0 else (4 + c, ps[4 + c][:, 0:256])
-
-        def ha(c):
-            cp("a", [("ss", c)], [hv(c)[0]], hv(c)[1], ck(T.ss, c), (-0.5, None, 0.25)[d])
-
-        def turn(a, b):
-            cols = slice(256 * a, 256 * b)
-            after("s", [("w", d + 1, b - 1)], [])
-            for t in DMA_SLOTS[d]:
-                oc = slice(t * M + 256 * a, t * M + 256 * b)
-                g.sync.dma_start(out[0:128 - 16 * t, oc], out[16 * t:128, cols]).then_inc(T.sem["rot%d" % d], 16)
-                g.sync.dma_start(out[128 - 16 * t:128, oc], out[0:16 * t, cols]).then_inc(T.sem["rot%d" % d], 16)
-
-        def pe_turn(c):
-            for n, t in enumerate(PE_SLOTS):
-                b = banks[c // 2][n]
-                mms([("w", d + 1, c), "zr"], [b], [(ck(ps[b], c % 2), T.zr[:, 16 * t:16 * t + 128], ck(out, c), True, True)])
-
-        def evac(q, h, n):
-            if n < NPE:
-                t, b = PE_SLOTS[n], banks[h][n]
-                cp(q, [b], [("slot", d + 1, h, n)], out[:, t * M + 512 * h:t * M + 512 * h + 512], ps[b][:, :])
-
-        def across(h):
-            for a in (0, 64):
-                cp("a", [("w", d + 1, 2 * h), ("w", d + 1, 2 * h + 1)], [("slot", d + 1, h, NPE + a // 64)],
-                   out[a:a + 64, 4 * M + 512 * h:4 * M + 512 * h + 512], out[64 - a:128 - a, 512 * h:512 * h + 512])
-
-        def own_next(h):
-            src, keys = out[:, 512 * h:512 * h + 512], [("w", d + 1, 2 * h), ("w", d + 1, 2 * h + 1)]
-            if d == 0:
-                cp("a", keys, [3 + h], ps[3 + h][:, :], src, -2.0)
-            else:
-                cp("a", keys, [("hh", 2 * h), ("hh", 2 * h + 1)], T.hh[:, 512 * h:512 * h + 512], src, -0.5)
-
-        def nw(c):
-            if d == 0:
-                tt([("hh", c), "offs"], [("w", 1, c)], ck(out, c), win.indirect(T.offs[:, 16 * c:16 * c + 16]), ck(T.hh, c), A.add)
-            elif d == 1:
-                tt([("ss", c), 3 + c // 2], [("w", 2, c)], ck(out, c), ck(T.ss, c), ck(ps[3 + c // 2], c % 2), A.add)
-            else:
-                tt([("hh", c), 4 + c], [("w", 3, c)], ck(out, c), ck(T.hh, c), hv(c)[1], A.add)
-            if d < 2:
-                for a, b in TURN_PIECES:
-                    if b == c + 1:
-                        turn(a, b)
-                if c < 2:
-                    pe_turn(c)
-            if d == 2 and c in FAR:
-                f = _far_senders(T, topo, rank)[FAR.index(c)]
-                after("g", [("w", 3, c)], [])
-                rid, pid, _ = topo.addr(f)
-                g.remote_dma(T.fh[:, :], ck(T.res, c), T.sem.fq, T.sem.ls, pid, rid, _half_mask(topo, core, f)[0])
-            elif d == 2:
-                after("s", [("w", 3, c)], [])
-                g.sync.dma_start(T.fs[c * NG:(c + 1) * NG], ck(T.res, c)).then_inc(T.sem["fst%d" % c], 16)
-
-        if d != 1:
-            ga(0); ga(1); su(0); su(1); ga(2); ha(0); su(2); ga(3); nw(0); ha(1); su(3); ha(2); nw(1); ha(3); nw(2); nw(3)
-        if d == 0:
-            climb("a", 2, 2, 0, 64); on(TL[1], S2[1], S3[1], PA[1], TL[1], S2[1], S3[1], PA[1])
-            pick(2, 2); pe_turn(2); pe_turn(3)
-            evac("v", 0, 0); evac("a", 0, 1); own_next(0); offsets(2, 2); on(H[2], TL[1], H[2])
-            climb("v", 2, 3, 0, 14); on(TL[1], H[2]); climb("v", 2, 3, 14, 28); climb("a", 2, 3, 28, 64); pick(2, 3)
-            on(TL[1]); own_next(1); evac("a", 1, 0); on(TL[1]); offsets(2, 3); keep3(2); on(TL[1]); evac("v", 1, 1)
-            both(2, 4, 24); pick(2, 4)
-        if d == 1:
-            ga(0); ga(1); on(S2[2], S3[2], TL[2]); su(0); ga(2); su(1); ga(3); nw(0); su(2); nw(1); su(3); nw(2); nw(3)
-            across(0); pe_turn(2); pe_turn(3); evac("a", 0, 0)
-            on(S2[2], S3[2], TL[2], S2[2], S3[2], PA[2]); evac("v", 0, 1); across(1); own_next(0); own_next(1)
-            on(TL[2], PA[2], TL[2], PA[2]); evac("v", 1, 0); on(TL[2], PA[2]); evac("a", 1, 1); weave(TL[2])
-        if d < 2:
-            ready = [("rot%d" % d, 16 * 2 * len(TURN_PIECES) * len(DMA_SLOTS[d]))]
+            def turn(q, a=cut[a], b=cut[b], d=d, out=out, n_rot=n_rot, slots=slots):
+                for t in slots:
+                    oc, cols = slice(t * M + a, t * M + b), slice(a, b)
+                    g.sync.dma_start(out[0:128 - 16 * t, oc], out[16 * t:128, cols]).then_inc(T.sem["rot%d" % d], 16)
+                    g.sync.dma_start(out[128 - 16 * t:128, oc], out[0:16 * t, cols]).then_inc(T.sem["rot%d" % d], 16)
+                    n_rot[0] += 32
+                return ("rot%d" % d, n_rot[0])
+            dma(new[a:b], [("rot", d, b)], 2 * len(slots), 128 * len(slots), 4 * (cut[b] - cut[a]), turn)
+        runs.append(list(range(len(tasks) - 2 * len(TURN_PIECES), len(tasks), 2)))
+        WIN += [("rot", d, 4)] + [("landed", "rot", d, b) for a, b in TURN_PIECES]
+        old = {0: [("c", 0, k, a) for k in (2, 3) for a, b in HALVES[0]], 6: [("x", 0, 3, a) for a, b in HALVES[0]],
+               7: [("c", x, 1, h) for x in range(3) for h in range(2)]}
+        for h in range(2):
+            cols = slice(512 * h, 512 * h + 512)
+            for n, t in enumerate(PE_SLOTS + LATE[d]):
+                b, e = ((5, 6), (7, 0))[h][n], cut[1] if t in LATE[d] and h == 0 else 0
+                for c in (2 * h, 2 * h + 1)[e > 0:]:
+                    mms([new[c], "zr"], [("turn", b, c % 2)] + old.get(b, []), b,
+                        [(half(b, c), T.zr[:, 16 * t:16 * t + 128], ck(out, c), True, True)], 4)
+                cp("va", [("turn", b, 0), ("turn", b, 1)], [("slot", d, t, h)],
+                   out[:, t * M + 512 * h + e:t * M + 512 * h + 512], ps[b][:, e:512], banks=(b,))
+                WIN.append(("slot", d, t, h))
+                for a in (0, 64) if t + 4 not in DMA_SLOTS[d] else ():
+                    cp("va", [("turn", b, 0), ("turn", b, 1)], [("slot", d, t + 4, h, a)],
+                       out[a:a + 64, (t + 4) * M + 512 * h:(t + 4) * M + 512 * h + 512], ps[b][64 - a:128 - a, :], banks=(b,))
+                    WIN.append(("slot", d, t + 4, h, a))
+            if 4 not in DMA_SLOTS[d]:
+                for a in (0, 64):
+                    cp("va", new[2 * h:2 * h + 2], [("slot", d, a, h)], out[a:a + 64, 4 * M + 512 * h:4 * M + 512 * h + 512],
+                       out[64 - a:128 - a, cols])
+                    WIN.append(("slot", d, a, h))
 
     for c in range(4):
-        if c in FAR:
-            sent += _half_mask(topo, core, _far_senders(T, topo, rank)[0])[1]
-        else:
+        def back(q, c=c):
+            if c not in FAR:
+                g.sync.dma_start(T.fs[c * NG:(c + 1) * NG], ck(T.res, c)).then_inc(T.sem["fst%d" % c], 16)
+                return ("fst%d" % c, 16)
+            f = _far_senders(T, topo, rank)[FAR.index(c)]
+            rid, pid, _ = topo.addr(f)
+            need("g", wrote["w", 3, c])
+            g.remote_dma(T.fh[:, :], ck(T.res, c), T.sem.fq, T.sem.ls, pid, rid, topo.mask(core, f))
+            sent[0] += len(topo.engines(core, f))
+            return wrote["w", 3, c]
+        dma([("w", 3, c)], [("back", c)], 1, 128, 1024, back, BACK_TAIL[c])
+
+    if not _ORDER:
+        _ORDER.extend(issue_order(tasks, runs))
+    for i, q in _ORDER:
+        call(q, tasks[i][1], tasks[i][2], tasks[i][3], makes[i])
+
+    for c in range(4):
+        if c not in FAR:
             need("g", ("fst%d" % c, 16))
-            sent += _send_back(g, T, topo, core, rank, c)
-    g.sync.dma_start(T.y[16 * rank:16 * rank + 16, :], T.res[16 * rank:16 * rank + 16, :]).then_inc(T.sem.yo, 16)
+            sent[0] += _send_back(g, T, topo, core, rank, c)
+    need("s", last("v"))
+    g.sync.dma_start(T.y[mine, :], T.res[mine, :]).then_inc(T.sem.yo, 16)
     n_y = {"yo": 16, "ya": 0}
     for c in Y_ORDER:
         cols = slice(256 * c, 256 * c + 256)
@@ -505,4 +569,4 @@ def rank_program(g, core, T, topo):
                 need(q, ("fa%d" % c, NG - 1))
                 Q[q].dma_start(T.y[16 * a:16 * b, cols], T.land[c * NG + a:c * NG + b]).then_inc(T.sem[sem], 16)
                 n_y[sem] += 16
-    need("g", ("ls", sent), last("v"), last("a"), last("p"), last("g"), ("yo", n_y["yo"]), ("ya", n_y["ya"]))
+    need("g", ("ls", sent[0]), last("v"), last("a"), last("p"), last("g"), ("yo", n_y["yo"]), ("ya", n_y["ya"]))

from concourse.bass import DstId, RemoteDMATransfer
from concourse.mybir import AluOpType as A, ActivationFunctionType as F

P, M, NG = 8192, 1024, 8
WW = P + 8
IN = ((0, 256, None), (704, 864, 0), (864, 1024, 1), (256, 704, None))
IN_WRITES = ((0,), (3,), (1, 2))
PE_SLOTS = (1,)
DMA_SLOTS = ((2, 3, 5, 6, 7), (2, 3, 6, 7))
LATE = ((), (2,))
TURN_PIECES = ((0, 1), (1, 4))
CHUNKS = ((0, 256, 512, 704, M), (0, 256, 512, 768, M), (0, 256, 512, 768, M))
FAR = (0, 1)
Y_ORDER = (2, 0, 3, 1)
CUTS = ((0, 32, 64), (0, 22, 44, 64), (0, 22, 44, 64))
HALVES = (((0, 8),), ((0, 8),), ((0, 8),))
STEPS = (("s0 s1 n0 s2 n1 s3 n2 n3", "g0 g1 g2 g3"), ("s0 s1 n0 s2 n1 s3 n2 n3", "g0 g1 g2 g3"),
         ("s0 s1 s2 n0 s3 n1 n2 n3", "g0 g1 g2 h0 g3 h1 h2 h3"))

CYC, PE_CYC, GATHER = 0.83e-3, 0.42e-3, 1.56
WAKE = 0.22
DMA_ISSUE, DMA_START, DMA_ROW, DMA_RATE = 0.06, 1.06, 0.012, 45e3
ARRIVES = {"pcol": 0.13, "l16": 0.47, "iy": 0.87, "ib": 1.08, "ic": 1.25, "lo": 1.9, "hi": 1.5, "zr": 5.6,
           "w0in2": 13.9, "ob0": 12.0, "ob1": 14.6, "ob2": 15.4}
BACK_TAIL = (5.8, 5.3, 4.3, 4.0)
ROUNDS, BIAS, FIRST, AHEAD, POLISH = 8, 0.05, 2.0, 0.5, 400

SCRATCH = {}
for _dt, _bufs in (
        ("float32", dict(w0=WW, w1=WW, w2=WW, gb=M, ss=M, hh=M, res=M, ob=M, cf=16, iy=160, ib=72, ck=32, one=256, zr=256,
                         zd=256, z0=144, z1=144, ff=576, ee=576, tg=192, d0=768, d1=768, so=768, rep=M, fh=256)),
        ("bfloat16", dict(tab=P + 16, xb=512, l16=128, l0=128, lt=2048, cand=9 * M, sb=72, zs=3 * 144, zc=6 * 144)),
        ("int32", dict(xi=512, xt=512, pcol=4, ci=8, pi=576, z4=192, ri=256, zi=256)),
        ("uint16", dict(off=576, offm=384))):
    for _n, _w in _bufs.items():
        SCRATCH[_n] = ("sbuf", [128, _w], _dt)
for _h, (_a, _b, _via) in enumerate(IN):
    SCRATCH["stg%d" % _h] = ("dram", [NG, 128, (_b - _a) // 8], "float32")
    SCRATCH["piece%d" % _h] = ("dram", [128, (_b - _a) // 8], "float32")
SCRATCH["od"] = SCRATCH["stg0"]
SCRATCH["fs"] = ("dram", [32, 128, 32], "float32")
SCRATCH["land"] = ("dram", [32, 128, 32], "float32")
for _b in range(8):
    SCRATCH["ps%d" % _b] = ("psum", [128, 512], "float32")

SEMAPHORES = (["sv", "sa", "sp", "sg", "ls", "hi_in", "lo_in", "od", "w0own", "rot0", "rot1", "fq", "vq", "yo", "ya"]
              + [n + str(i) for n in ("fa", "fst") for i in range(4)]
              + [n + str(i) for n in ("st", "pa", "pb") for i in range(len(IN))]
              + [n + str(i) for n in ("w0in", "ob") for i in range(len(IN_WRITES))])
_ORDER = []


def _dst(topo, c):
    rid, pid, _ = topo.addr(c)
    return DstId(rid=rid, pnc=pid)


def _others(r):
    return [q for q in range(NG) if q != r]


def _helper_of(T, topo, grp, q):
    rc = T.cores[grp]
    return [c for c in topo.cores_of(rc) if c != rc][_others(grp).index(q)]


def _far_senders(T, topo, grp):
    rc = T.cores[grp]
    return [c for c in topo.cores_of(rc) if topo.die(c) != topo.die(rc) and all(topo.may_write(c, r) for r in T.cores)]


def _send_in(g, T, topo, src, owner, h):
    tr = []
    for n, grp in enumerate(_others(owner)):
        hc = _helper_of(T, topo, grp, owner)
        tr.append(RemoteDMATransfer(dst_ids=[_dst(topo, hc)], dma_engine_mask=1 << topo.engines(src, hc)[n],
                                    remote_sem=T.sem["pa%d" % h], src=T["stg%d" % h][grp], dst=T["piece%d" % h][:]))
    g.remote_dma_fused(tr, local_sem=T.sem.ls)
    return len(tr)


def _send_back(g, T, topo, src, grp, quarter):
    tr = []
    for n, q in enumerate(_others(grp)):
        c = T.cores[q]
        tr.append(RemoteDMATransfer(dst_ids=[_dst(topo, c)], dma_engine_mask=1 << topo.engines(src, c)[n],
                                    remote_sem=T.sem["fa%d" % quarter], src=T.fs[quarter * NG + q],
                                    dst=T.land[quarter * NG + grp]))
    g.remote_dma_fused(tr, local_sem=T.sem.ls)
    return len(tr)


def helper_program(g, core, T, topo):
    grp = [r for r in range(NG) if topo.chip(T.cores[r]) == topo.chip(core)]
    if not grp:
        return
    grp = grp[0]
    rc = T.cores[grp]
    rid, pid, _ = topo.addr(rc)
    q = [r for r in _others(grp) if _helper_of(T, topo, grp, r) == core][0]
    sent, every = 0, len(topo.engines(core, rc))
    far = _far_senders(T, topo, grp)
    for h, (a, b, via) in enumerate(IN):
        if via is not None and far[via] == core:
            g.wait_ge(T.sem.vq, NG - 1)
            sent += _send_in(g, T, topo, core, grp, h)
    for h in sum(IN_WRITES, ()):
        a, b, via = IN[h]
        for qu in (g.sync, g.scalar):
            qu.wait_ge(T.sem["pa%d" % h], 1)
        for j in range(NG):
            qu = g.sync if j % 2 == 0 else g.scalar
            qu.dma_start(T.rep[16 * j:16 * j + 16, a:b], T["piece%d" % h][:]).then_inc(T.sem["pb%d" % h], 16)
    g.wait_ge(T.sem.pa0, 1)
    g.remote_dma(T.od[q], T.piece0[:], T.sem.od, T.sem.ls, pid, rid, topo.mask(core, rc))
    for n, hs in enumerate(IN_WRITES):
        a, b = IN[hs[0]][0], IN[hs[-1]][1]
        for h in hs:
            g.wait_ge(T.sem["pb%d" % h], 16 * NG)
        g.remote_dma(T.w0[:, q * M + a:q * M + b], T.rep[:, a:b], T.sem["w0in%d" % n], T.sem.ls, pid, rid, topo.mask(core, rc))
    sent += every * (1 + len(IN_WRITES))
    if core in far[:len(FAR)]:
        c = FAR[far.index(core)]
        g.sync.wait_ge(T.sem.fq, len(topo.engines(rc, core)))
        g.sync.dma_start(T.fs[c * NG:(c + 1) * NG], T.fh[:, :]).then_inc(T.sem.fst0, 16)
        g.wait_ge(T.sem.fst0, 16)
        sent += _send_back(g, T, topo, core, grp, c)
    g.wait_ge(T.sem.ls, sent)


def issue_order(tasks, runs):
    n = len(tasks)
    pred, succ, wrote, read = [{} for _ in range(n)], [{} for _ in range(n)], {}, {}
    for i, t in enumerate(tasks):
        for a in [wrote[k] for k in t[1] + t[2] if k in wrote] + [a for k in t[2] for a in read.get(k, [])]:
            if a != i:
                pred[i][a] = 0.0 if tasks[a][0] == t[0] == "p" else DMA_START - tasks[a][4]["s"] if tasks[a][0] == "s" else WAKE
        for k in t[1]:
            read.setdefault(k, []).append(i)
        for k in t[2]:
            wrote[k], read[k] = i, []
    for run in runs:
        for a, b in zip(run, run[1:]):
            pred[b].setdefault(a, 0.0)
    for i in range(n):
        for a, x in pred[i].items():
            succ[a][i] = x
    first = [max([ARRIVES.get(k, -WAKE) + WAKE for k in t[1]] + [0.0]) for t in tasks]
    tail = [t[5] for t in tasks]
    stage = [min([k[1] for k in t[2] if k[:1] == ("w",)] + [3]) for t in tasks]
    value = [FIRST * (t[2][0][0] in ("own", "gv", "gb", "ss", "hh", "w", "rot")) for t in tasks]
    for i in reversed(range(n)):
        for a in pred[i]:
            stage[a] = min(stage[a], stage[i])

    def place(urgency, pred, first):
        end, where, busy = {}, {}, {}
        todo = sorted(range(n), key=lambda i: -urgency[i])
        while todo:
            i = next(i for i in todo if all(a in end for a in pred[i]))
            todo.remove(i)
            best = None
            for q in tasks[i][0]:
                s, d = max([first[i]] + [end[a] + x for a, x in pred[i].items()]), tasks[i][4][q]
                for a, b in sorted(busy.get(q, []) + [(a - WAKE, b + WAKE) for k in tasks[i][3]
                                                      for a, b, x in busy.get(k, []) if x != q]):
                    if a < s + d - 1e-9 and b > s + 1e-9:
                        s = b
                if best is None or s + d < best[0] + BIAS:
                    best = (s + d, s, q)
            end[i], s, q = best
            where[i] = (s, q)
            busy.setdefault(q, []).append((s, end[i]))
            for k in tasks[i][3]:
                busy.setdefault(k, []).append((s, end[i], q))
        return end, where

    end, best = list(range(n)), None
    for _ in range(ROUNDS):
        back = place(end, succ, tail)[0]
        end, where = place([back[i] - AHEAD * stage[i] + value[i] for i in range(n)], pred, first)
        total = max(end[i] + tail[i] for i in range(n))
        if best is None or total < best[0]:
            best = (total, where)

    def play(order, queue):
        end, why, free, bank = [0.0] * n, [None] * n, {}, {}
        for i in order:
            q, s = queue[i], first[i]
            for a, x in list(pred[i].items()) + ([(free[q], 0.0)] if q in free else []) + [
                    (a, WAKE) for b in tasks[i][3] for y, a in bank.get(b, {}).items() if y != q]:
                if end[a] + x > s:
                    s, why[i] = end[a] + x, a
            end[i], free[q] = s + tasks[i][4][q], i
            for b in tasks[i][3]:
                bank.setdefault(b, {})[q] = i
        i, chain = max(range(n), key=lambda i: end[i] + tail[i]), []
        total = end[i] + tail[i] + 0.05 * sum(end) / n
        while why[i] is not None:
            chain.append((why[i], i))
            i = why[i]
        return total, chain

    order, queue = sorted(range(n), key=lambda i: best[1][i][0]), [best[1][i][1] for i in range(n)]
    total, chain = play(order, queue)
    kept, tried = (total, order, queue), []
    for _ in range(POLISH):
        moves = []
        for a, i in chain:
            if a not in pred[i] and (a, i) not in tried[-40:]:
                pa, pi = order.index(a), order.index(i)
                ahead, mid = {i}, order[pa:pi + 1]
                for x in reversed(mid):
                    if x in ahead:
                        ahead.update(pred[x])
                if a not in ahead:
                    mid = [x for x in mid if x in ahead] + [x for x in mid if x not in ahead]
                    moves.append(((a, i), order[:pa] + mid + order[pi + 1:], queue))
                for x in (a, i):
                    if len(tasks[x][0]) > 1:
                        moves.append(((a, i), order, queue[:x] + [tasks[x][0].replace(queue[x], "")] + queue[x + 1:]))
        if not moves:
            break
        (total, chain), key, order, queue = min(((play(o, q), k, o, q) for k, o, q in moves), key=lambda m: m[0][0])
        tried += [key, key[::-1]]
        if total < kept[0]:
            kept = (total, order, queue)
    return [(i, kept[2][i]) for i in kept[1] if tasks[i][0] != "d"]


def rank_program(g, core, T, topo):
    rank = T.rank_of(core)
    if rank is None:
        return helper_program(g, core, T, topo)
    Q = {"v": g.vector, "a": g.scalar, "p": g.tensor, "g": g, "s": g.sync}
    SEM = {"v": "sv", "a": "sa", "p": "sp", "g": "sg"}
    cnt = {"v": 0, "a": 0, "p": 0, "g": 0}
    seen = {k: {} for k in Q}
    wrote, read, held = {}, {}, {}
    tasks, makes, runs = [], [], []
    V, S, PE = g.vector, g.scalar, g.tensor
    ps = [T["ps%d" % b] for b in range(8)]
    W = [T.w0, T.w1, T.w2]
    cf = T.cf

    def need(q, *toks):
        for sem, n in toks:
            if seen[q].get(sem, 0) < n:
                Q[q].wait_ge(T.sem[sem], n)
                seen[q][sem] = n

    def last(q):
        return (SEM[q], cnt[q])

    def call(q, r, w, banks, make):
        old = [wrote[k] for k in r + w if k in wrote] + [t for k in w for t in read.get(k, {}).values()]
        need(q, *[t for t in old if q != "p" or t[0] != SEM[q]])
        need(q, *[t for b in banks for x, t in held.get(b, {}).items() if x != q])
        done = make(q)
        if not isinstance(done, tuple):
            done.then_inc(T.sem[SEM[q]], 1)
            cnt[q] += 1
            done = last(q)
        for k in r:
            read.setdefault(k, {})[q] = done
        for k in w:
            wrote[k], read[k] = done, {}
        for b in banks:
            held.setdefault(b, {})[q] = done

    def task(qs, r, w, banks, cycles, make, fixed=(0.01, 0.03)):
        cost = {"v": max(64, cycles) * CYC + fixed[0], "a": max(64, cycles) * CYC + fixed[1], "p": cycles * PE_CYC}
        tasks.append((qs, r, w, banks, {q: cost[q] for q in qs}, 0.0))
        makes.append(make)

    def dma(r, w, n, rows, row, make, tail=0.0):
        tasks.append(("s", r, w, (), {"s": DMA_ISSUE * n}, 0.0))
        tasks.append(("d", w, [("landed",) + w[0]], (), {"d": rows / 16 * (DMA_ROW + row / DMA_RATE)}, tail))
        makes.extend([make, None])

    def size(ap):
        return ap.shape[1]

    def ts(r, w, out, in0, s1, s2, op0, op1=None, banks=()):
        args = (out, in0, s1, None, op0) if op1 is None else (out, in0, s1, s2, op0, op1)
        task("v", r, w, banks, size(out), lambda q: V.tensor_scalar(*args))

    def tt(r, w, out, in0, in1, op, banks=()):
        task("v", r, w, banks, size(out) * (1 if banks else 2), lambda q: V.tensor_tensor(out, in0, in1, op))

    def cp(qs, r, w, out, in_, scale=None, banks=(), gather=False):
        def make(q):
            if q == "a":
                return S.activation(out, in_, F.Copy, scale=1.0 if scale is None else scale)
            return V.tensor_copy(out, in_) if scale is None else V.tensor_scalar(out, in_, scale, None, A.mult)
        task(qs, r, w, banks, size(out) * (GATHER if gather else 1), make, (0.05, 0.065) if gather else (0.01, 0.03))

    def fill(w, out, x):
        task("v", [], w, (), size(out), lambda q: V.memset(out, x))

    def iota(w, out, pat, cm, base=0):
        call("g", [], w, (), lambda q: g.iota(out, pat, base, cm, allow_small_or_imprecise_dtypes=True))

    def mms(r, w, bank, calls, passes=1):
        def make(q):
            for c in calls[:-1]:
                PE.matmul(*c)
            return PE.matmul(*calls[-1])
        task("p", r, w, (bank,), passes * sum(max(64, size(c[0])) for c in calls), make)

    mine = slice(16 * rank, 16 * rank + 16)
    S.dma_start(T.xi[0:48, :], T.tree[rank]).then_inc(T.sem.hi_in, 16)
    S.dma_start(T.xi[48:64, :], T.tree[rank, 0:P]).then_inc(T.sem.hi_in, 16)
    S.dma_start(T.xi[64:112, :], T.tree[rank]).then_inc(T.sem.lo_in, 16)
    for h, (a, b, via) in enumerate(IN):
        g.sync.dma_start(T["stg%d" % h][:], T.v[:, a:b]).then_inc(T.sem["st%d" % h], 16)
    for j in range(NG):
        g.sync.dma_start(T.w0[16 * j:16 * j + 16, rank * M:(rank + 1) * M], T.v[mine, :]).then_inc(T.sem.w0own, 16)
    g.sync.dma_start(T.ob[mine, :], T.v[mine, :]).then_inc(T.sem.ob0, 16)
    engines = sum(len(topo.engines(_helper_of(T, topo, rank, q), core)) for q in _others(rank))
    wrote.update(hi=("hi_in", 32), lo=("lo_in", 16), w0own=("w0own", 16 * NG))
    for n, hs in enumerate(IN_WRITES):
        a, b = IN[hs[0]][0], IN[hs[-1]][1]
        wrote["w0in%d" % n] = ("w0in%d" % n, engines)
        if n == 0:
            need("s", ("od", engines))
            parts = [(T.ob[16 * x:16 * y, a:b], T.od[x:y]) for x, y in ((0, rank), (rank + 1, NG)) if y > x]
        else:
            need("s", wrote["w0in%d" % n])
            parts = [(T.ob[16 * j:16 * j + 16, a:b], T.w0[16 * j:16 * j + 16, j * M + a:j * M + b]) for j in _others(rank)]
        for out, src in parts:
            g.sync.dma_start(out, src).then_inc(T.sem["ob%d" % n], 16)
        wrote["ob%d" % n] = ("ob%d" % n, 16 * (len(parts) + (n == 0)))

    call("g", [], ["pcol"], (), lambda q: g.iota(T.pcol[:, 0:1], [[0, 1]], 0, 1))
    iota(["l16"], T.l16[:, :], [[0, 8], [16, 16]], 0)
    iota(["iy"], T.iy[:, :], [[1, 160]], 0, -16)
    iota(["ib"], T.ib[:, 0:48], [[16, 3], [1, 2], [2, 8]], 0)
    iota(["ic"], T.ib[:, 48:72], [[1, 3], [16, 8]], 0)
    sent = [0]
    for h, (a, b, via) in enumerate(IN):
        need("g", ("st%d" % h, 16))
        if via is None:
            sent[0] += _send_in(g, T, topo, core, rank, h)
        else:
            f = _far_senders(T, topo, rank)[via]
            g.remote_dma_fused([RemoteDMATransfer(dst_ids=[_dst(topo, f)], dma_engine_mask=1 << topo.engines(core, f)[-1 - n],
                                                  remote_sem=T.sem.vq, src=T["stg%d" % h][grp], dst=T["stg%d" % h][grp])
                                for n, grp in enumerate(_others(rank))], local_sem=T.sem.ls)
            sent[0] += NG - 1
    iota(["one"], T.one[:, :], [[0, 256]], 0, 1)
    call("g", ["one"], ["zr"], (),
         lambda q: g.affine_select(T.zr[:, :], T.one[:, :], [[0, 2], [1, 128]], A.is_equal, 0.0, 0, -1))

    MASKS = (112, 15, 14, 49, 3, 63, 115)
    fill(["wt"], cf[0:64, 7:8], 64.0)
    fill(["wt2"], cf[64:128, 7:8], 0.5)
    fill([("d0", d, 0) for d in range(3)], T.d0[:, 0::4], 0.0)
    fill([("d1", d, 0) for d in range(3)], T.d1[:, 1::4], 0.0)
    for d in range(3):
        fill([("zero", d)], W[d][:, P:WW], 0.0)
    for n, x in enumerate(MASKS):
        ts(["pcol"], [("ci", n)], T.ci[:, n:n + 1], T.pcol[:, 0:1], x, None, A.bitwise_and)
    cp("v", [("ci", n) for n in range(7)], ["cf"], cf[:, 0:7], T.ci[:, 0:7])
    ts(["cf", "l16"], ["l0"], T.l0[:, :], T.l16[:, :], cf[:, 0:1], None, A.is_equal)
    ts(["cf", "iy"], ["ck"], T.ck[:, 0:16], T.iy[:, 16:32], cf[:, 1:2], None, A.is_equal)
    ts(["cf", "ib"], ["cz"], T.ck[:, 16:22], T.ib[:, 0:48:8], cf[:, 3:4], None, A.is_equal)
    ts(["cf", "iy"], ["cs"], T.ck[:, 22:25], T.iy[:, 16:19], cf[:, 4:5], None, A.is_equal)
    ts(["cf", "iy"], ["z0"], T.z0[:, :], T.iy[:, 0:144], 0.125, cf[:, 2:3], A.mult, A.is_equal)
    ts(["cf", "iy"], ["z1"], T.z1[:, :], T.iy[:, 0:144], cf[:, 0:1], None, A.is_equal)
    ts(["cf", "ib"], ["sb"], T.sb[:, 0:48], T.ib[:, 0:48], cf[:, 5:6], None, A.is_equal)
    ts(["cf", "ic"], ["sn"], T.sb[:, 48:72], T.ib[:, 48:72], cf[:, 6:7], None, A.is_equal)
    ts(["cf"], ["none"], T.tab[:, P:P + 1], cf[:, 1:2], 3.0, float(P), A.is_lt, A.mult)
    ts(["cf"], ["c8"], cf[:, 8:9], cf[:, 0:1], -M / 16.0, float(2 * P), A.mult, A.add)
    for k in range(16):
        task("va", ["l0", "ck"], [("lt", k)], (), 64, lambda q, k=k: (
            S.activation(T.lt[:, k * 128:k * 128 + 128], T.l0[:, :], F.Copy, scale=T.ck[:, k:k + 1]) if q == "a" else
            V.tensor_scalar(T.lt[:, k * 128:k * 128 + 128], T.l0[:, :], T.ck[:, k:k + 1], None, A.mult)), (0.01, 0.085))
    for n in range(6):
        cp("va", ["z0", "cz"], [("zc", n)], T.zc[:, n * 144:n * 144 + 144], T.z0[:, :], T.ck[:, 16 + n:17 + n])
    for d in range(3):
        cp("va", ["z1", "cs"], [("zs", d)], T.zs[:, d * 144:d * 144 + 144], T.z1[:, :], T.ck[:, 22 + d:23 + d])
    for n, x in enumerate((-2.0, 0.25)):
        cp("va", ["zr"], [("zd", n)], T.zd[:, 128 * n:128 * n + 128], T.zr[:, 0:128], x)

    ts(["lo"], ["xl"], T.xt[64:112, :], T.xi[64:112, :], 127, None, A.bitwise_and)
    ts(["hi"], ["xt"], T.xt[0:64, :], T.xi[0:64, :], 7, None, A.arith_shift_right)
    cp("v", ["xt", "xl", "wt", "wt2"], ["xb"], T.xb[0:112, :], T.xt[0:112, :], cf[0:112, 7:8])

    TABLE_BANKS = (4, 5, 0, 1, 2, 6, 7)
    for k in range(16):
        b = TABLE_BANKS[k % 7]
        mms(["xb", ("lt", k)], [("sp", b)], b,
            [(ps[b][:, :], T.lt[0:112, k * 128:k * 128 + 128], T.xb[0:112, :], True, True)])
        cp("va", [("sp", b)], [("tab", k)], T.tab[:, k * 512:k * 512 + 512], ps[b][:, :], banks=(b,))
    TAB = [("tab", k) for k in range(16)] + ["none"]

    def address(d, a, src, key):
        o = T.offm[:, 128 * d + a:128 * d + a + 64]
        if d == 0:
            return ts([key], [("offm", d, a)], o, src, float(P), None, A.add)
        c = slice(128 * d + a - 128, 128 * d + a - 64)
        ri, zi, k = T.ri[:, c], T.zi[:, c], ("ri", d, a)
        ts([key, "c8"], [k], ri, src, cf[:, 8:9], None, A.add)
        ts([key], [("zi", d, a)], zi, src, 0.0, float(P), A.is_ge, A.mult)
        ts([k], [k], ri, ri, P - 1, None, A.bitwise_and)
        tt([k, ("zi", d, a)], [k], ri, ri, zi, A.max)
        cp("v", [k], [("offm", d, a)], o, ri)

    for d in range(3):
        parts = HALVES[d]
        mms(["xb", "sb"], [("x", d, 1)], 3,
            [(ps[3][:, 64 * d + 32 * h + 8 * b:64 * d + 32 * h + 8 * b + 8], T.xb[0:112, 128 * b:128 * b + 128],
              T.sb[0:112, 16 * d + 8 * h:16 * d + 8 * h + 8], True, True) for h in range(2) for b in range(4)])
        ts([("x", d, 1)], [("off", d, 1, a) for a, b in parts], T.off[:, 64 * d:64 * d + 64], ps[3][:, 64 * d:64 * d + 64],
           -0.25, None, A.add, banks=(3,))
        for h in range(2):
            z = (2 * d + h) * 144
            mms(["xb", ("zc", 2 * d + h), ("tab", 13)], [("c", d, 1, h)], 7,
                [(ps[7][:, 64 * d + 32 * h:64 * d + 32 * h + 32], T.zc[0:112, z + 16 - i:z + 144 - i], T.xb[0:112, i::16],
                  i == 0, i == 15) for i in range(16)])
        for k in (2, 3, 4):
            c, o = (3 * d + k - 2) * M, 192 * (k - 2) + 64 * d
            bank, at = (d or (0, 6, 3)[k - 2]), (256 if k == 3 else 192 if k == 4 else 64)
            for a, b in parts:
                cuts = [x for x in CUTS[d] if 8 * a <= x <= 8 * b]
                for x, y in zip(cuts, cuts[1:]):
                    cp("va", [("off", d, k - 1, a)] + TAB, [("cand", d, k, x)], T.cand[:, c + 16 * x:c + 16 * y],
                       T.tab[:, 0:P + 1].indirect(T.off[:, o + x:o + y]), gather=True)
                mms([("cand", d, k, x) for x in cuts[:-1]] + ["sn"], [("x" if k == 3 else "c", d, k, a)], bank,
                    [(ps[bank][:, at + 8 * n:at + 8 * n + 8], T.cand[:, c + 128 * n:c + 128 * n + 128],
                      T.sb[:, 48 + 8 * d:56 + 8 * d], True, True) for n in range(a, b)])
                if k < 4:
                    ts([("x" if k == 3 else "c", d, k, a)], [("off", d, k, a)], T.off[:, o + 192 + 8 * a:o + 192 + 8 * b],
                       ps[bank][:, at + 8 * a:at + 8 * b], -0.25, None, A.add, banks=(bank,))
            if k == 3:
                mms([("cand", d, 3, x) for x in CUTS[d][:-1]] + [("zs", d)], [("c", d, 3, a) for a, b in parts], d,
                    [(ps[d][:, 128:192], T.zs[:, d * 144 + 16 - i:d * 144 + 144 - i], T.cand[:, c + i:c + M:16], i == 0,
                      i == 15) for i in range(16)])
        c, tg, z = slice(192 * d, 192 * d + 64), T.tg[:, 64 * d:64 * d + 64], 256 * d
        own = [("c", d, 1, 0), ("c", d, 1, 1)]
        ts(own, [("pi", d, 1)], T.pi[:, c], ps[7][:, 64 * d:64 * d + 64], -0.25 - P, None, A.add, banks=(7,))
        tt(own + [("pi", d, 1)], [("ff", d, 1)], T.ff[:, c], ps[7][:, 64 * d:64 * d + 64], T.pi[:, c], A.subtract, banks=(7,))
        ts([("ff", d, 1)], [("tg", d)], tg, T.ff[:, c], -1.0, 2 * P + 0.5, A.mult, A.add)
        address(d, 64, T.pi[:, c], ("pi", d, 1))
        for k in (2, 3):
            c, e = slice(192 * d + 64 * k - 64, 192 * d + 64 * k), slice(z + 5 - k, z + 256, 4)
            r = [("c", d, k, a) for a, b in parts] + [("tg", d)]
            tt(r, [("ff", d, k)], T.ff[:, c], ps[d][:, 64 * k - 64:64 * k], tg, A.subtract, banks=(d,))
            tt(r, [("pi", d, k)], T.pi[:, c], ps[d][:, 64 * k - 64:64 * k], tg, A.subtract, banks=(d,))
            tt([("pi", d, k), ("ff", d, k)], [("ee", d, k)], T.ee[:, c], T.ff[:, c], T.pi[:, c], A.is_equal)
            ts([("ee", d, k)], [("d0", d, k)], T.d0[:, e], T.ee[:, c], -1.0, 1.0, A.mult, A.add)
            tt([("ee", d, k), ("ff", d, k)], [("d1", d, k)], T.d1[:, e], T.ff[:, c], T.ee[:, c], A.mult)
        r, z4 = [("c", d, 4, a) for a, b in parts] + [("tg", d)], T.z4[:, 64 * d:64 * d + 64]
        tt(r, [("d1", d, 4)], T.d1[:, z:z + 256:4], ps[d or 3][:, 192:256], tg, A.subtract, banks=(d or 3,))
        tt(r, [("z4", d)], z4, ps[d or 3][:, 192:256], tg, A.subtract, banks=(d or 3,))
        tt([("z4", d), ("d1", d, 4)], [("d0", d, 4)], T.d0[:, z + 1:z + 256:4], T.d1[:, z:z + 256:4], z4, A.is_equal)
        task("v", [(n, d, k) for n in ("d0", "d1") for k in (0, 2, 3, 4)], [("so", d)], (), 256, lambda q, z=z:
             V.tensor_tensor_scan(T.so[:, z:z + 256], T.d0[:, z:z + 256], T.d1[:, z:z + 256], 0.0, A.mult, A.add))
        address(d, 0, T.so[:, z + 3:z + 256:4], ("so", d))

    WIN = ["w0own"] + ["w0in%d" % n for n in range(len(IN_WRITES))]
    for d in range(3):
        out = W[d + 1] if d < 2 else T.res
        win = W[d][:, 0:P + 1]
        WIN = WIN + [("zero", d)]
        cut = CHUNKS[d]

        def ck(buf, c, cut=cut):
            return buf[:, cut[c]:cut[c + 1]]

        def half(b, c, cut=cut):
            return ps[b][:, cut[c] - 512 * (c // 2):cut[c + 1] - 512 * (c // 2)]

        for c in range(4):
            b = 4 - c // 2
            had = [(("w", d, n), CHUNKS[d - 1][n:n + 2]) for n in range(4)] if d else [
                ("ob%d" % n, (IN[hs[0]][0], IN[hs[-1]][1])) for n, hs in enumerate(IN_WRITES)]
            src = [k for k, (x, y) in had if x < cut[c + 1] and y > cut[c]] + ([] if d else ["ob0"])
            old = ([("c", 0, 4, a) for a, _ in HALVES[0]] + [("x", x, 1) for x in range(3)] if b == 3 else [("sp", b)])
            mms(src + [("zd", d // 2)], [("own", c)] + (old if d == 0 else []), b,
                [(half(b, c), T.zd[:, 128 * (d // 2):128 * (d // 2) + 128], ck(W[d] if d else T.ob, c), True, True)], 4)
        runs += [[i, len(tasks) - 4] for i, t in enumerate(tasks) if t[2][0][0] == "turn"]
        runs.append(list(range(len(tasks) - 4, len(tasks))))
        cp("v", WIN + [("offm", d, 64)], [("gv", 0)], T.gb[:, 0:128], win.indirect(T.offm[:, 128 * d + 64:128 * d + 72]),
           gather=True)
        name = {x + str(c): len(tasks) + (3 + d // 2) * c + n for c in range(4) for n, x in enumerate("gshn" if d == 2 else "gsn")}
        runs += [[name[x] for x in r.split()] for r in STEPS[d]]
        for c in range(4):
            x, y, b, e = 128 * d + cut[c] // 16, 128 * d + cut[c + 1] // 16, 4 - c // 2, 0 if c else 8
            cp("a", WIN + [("offm", d, 64)], [("gb", c)], T.gb[:, cut[c] + 16 * e:cut[c + 1]],
               win.indirect(T.offm[:, x + 64 + e:y + 64]), gather=True)
            args = (ck(T.ss, c), win.indirect(T.offm[:, x:y]), ck(T.gb, c), A.add)
            task("v", WIN + [("offm", d, 0), ("gb", c), ("gv", c)], [("ss", c)], (), 16 * (y - x) * GATHER,
                 lambda q, args=args: V.tensor_tensor(*args), (0.05, 0))
            if d == 2:
                cp("a", [("ss", c)], [("hh", c)], ck(T.hh, c), ck(T.ss, c), -0.125)
            tt([("hh" if d == 2 else "ss", c), ("own", c)], [("w", d + 1, c)], ck(out, c), ck(T.hh if d == 2 else T.ss, c),
               half(b, c), A.add, banks=(b,))
        if d == 2:
            break
        new = [("w", d + 1, c) for c in range(4)]
        WIN = list(new)
        n_rot = [0]
        for a, b in TURN_PIECES:
            slots = [t for t in DMA_SLOTS[d] if a == 0 or t not in LATE[d]]

            def turn(q, a=cut[a], b=cut[b], d=d, out=out, n_rot=n_rot, slots=slots):
                for t in slots:
                    oc, cols = slice(t * M + a, t * M + b), slice(a, b)
                    g.sync.dma_start(out[0:128 - 16 * t, oc], out[16 * t:128, cols]).then_inc(T.sem["rot%d" % d], 16)
                    g.sync.dma_start(out[128 - 16 * t:128, oc], out[0:16 * t, cols]).then_inc(T.sem["rot%d" % d], 16)
                    n_rot[0] += 32
                return ("rot%d" % d, n_rot[0])
            dma(new[a:b], [("rot", d, b)], 2 * len(slots), 128 * len(slots), 4 * (cut[b] - cut[a]), turn)
        runs.append(list(range(len(tasks) - 2 * len(TURN_PIECES), len(tasks), 2)))
        WIN += [("rot", d, 4)] + [("landed", "rot", d, b) for a, b in TURN_PIECES]
        old = {0: [("c", 0, k, a) for k in (2, 3) for a, b in HALVES[0]], 6: [("x", 0, 3, a) for a, b in HALVES[0]],
               7: [("c", x, 1, h) for x in range(3) for h in range(2)]}
        for h in range(2):
            cols = slice(512 * h, 512 * h + 512)
            for n, t in enumerate(PE_SLOTS + LATE[d]):
                b, e = ((5, 6), (7, 0))[h][n], cut[1] if t in LATE[d] and h == 0 else 0
                for c in (2 * h, 2 * h + 1)[e > 0:]:
                    mms([new[c], "zr"], [("turn", b, c % 2)] + old.get(b, []), b,
                        [(half(b, c), T.zr[:, 16 * t:16 * t + 128], ck(out, c), True, True)], 4)
                cp("va", [("turn", b, 0), ("turn", b, 1)], [("slot", d, t, h)],
                   out[:, t * M + 512 * h + e:t * M + 512 * h + 512], ps[b][:, e:512], banks=(b,))
                WIN.append(("slot", d, t, h))
                for a in (0, 64) if t + 4 not in DMA_SLOTS[d] else ():
                    cp("va", [("turn", b, 0), ("turn", b, 1)], [("slot", d, t + 4, h, a)],
                       out[a:a + 64, (t + 4) * M + 512 * h:(t + 4) * M + 512 * h + 512], ps[b][64 - a:128 - a, :], banks=(b,))
                    WIN.append(("slot", d, t + 4, h, a))
            if 4 not in DMA_SLOTS[d]:
                for a in (0, 64):
                    cp("va", new[2 * h:2 * h + 2], [("slot", d, a, h)], out[a:a + 64, 4 * M + 512 * h:4 * M + 512 * h + 512],
                       out[64 - a:128 - a, cols])
                    WIN.append(("slot", d, a, h))

    for c in range(4):
        def back(q, c=c):
            if c not in FAR:
                g.sync.dma_start(T.fs[c * NG:(c + 1) * NG], ck(T.res, c)).then_inc(T.sem["fst%d" % c], 16)
                return ("fst%d" % c, 16)
            f = _far_senders(T, topo, rank)[FAR.index(c)]
            rid, pid, _ = topo.addr(f)
            need("g", wrote["w", 3, c])
            g.remote_dma(T.fh[:, :], ck(T.res, c), T.sem.fq, T.sem.ls, pid, rid, topo.mask(core, f))
            sent[0] += len(topo.engines(core, f))
            return wrote["w", 3, c]
        dma([("w", 3, c)], [("back", c)], 1, 128, 1024, back, BACK_TAIL[c])

    if not _ORDER:
        _ORDER.extend(issue_order(tasks, runs))
    for i, q in _ORDER:
        call(q, tasks[i][1], tasks[i][2], tasks[i][3], makes[i])

    for c in range(4):
        if c not in FAR:
            need("g", ("fst%d" % c, 16))
            sent[0] += _send_back(g, T, topo, core, rank, c)
    need("s", last("v"))
    g.sync.dma_start(T.y[mine, :], T.res[mine, :]).then_inc(T.sem.yo, 16)
    n_y = {"yo": 16, "ya": 0}
    for c in Y_ORDER:
        cols = slice(256 * c, 256 * c + 256)
        for q, sem, a, b in (("a", "ya", 0, rank), ("s", "yo", rank + 1, NG)):
            if b > a:
                need(q, ("fa%d" % c, NG - 1))
                Q[q].dma_start(T.y[16 * a:16 * b, cols], T.land[c * NG + a:c * NG + b]).then_inc(T.sem[sem], 16)
                n_y[sem] += 16
    need("g", ("ls", sent[0]), last("v"), last("a"), last("p"), last("g"), ("yo", n_y["yo"]), ("ya", n_y["ya"]))
